import numpy as np, ml_dtypes
CORES = [25,29,65,69,153,157,193,197]
N = 8
import mx_ref
BF = ml_dtypes.bfloat16
def gcols(t, e):
    v = np.concatenate([t.reshape(8, 16, -1, 4), np.zeros((8, 16, 1, 4), BF)], axis=2)
    return np.ascontiguousarray(np.stack([v[g][:, e[g]] for g in range(8)])).reshape(128, -1)
def tile(rs):
    return np.stack(rs, axis=2).reshape(128, -1).astype(BF)
def pick(q, e):
    c = np.concatenate([q[0].reshape(128, -1, 4), np.zeros((128, 1, 4), np.uint8)], axis=1); s = np.concatenate([q[1], np.ones((16, 1), np.uint8)], axis=1)
    return (np.ascontiguousarray(c[:, e].reshape(128, -1)), np.ascontiguousarray(s[:, e]))
def join(*qs):
    return (np.concatenate([q[0] for q in qs], axis=1), np.concatenate([q[1] for q in qs], axis=1))
def put(q, e, v):
    c, s = q[0].reshape(128, -1, 4).copy(), q[1].copy(); c[:, e] = v[0].reshape(128, -1, 4); s[:, e] = v[1]
    return (c.reshape(128, -1), s)
def pk(c, s):
    return (np.ascontiguousarray(c), mx_ref.live(s))
def emit(q):
    return q[0], q[1]
def packed(v, rng):
    q = [mx_ref.quantize(np.ascontiguousarray(v[r])) for r in range(N)]
    return np.stack([a for a, b in q]), np.stack([mx_ref.plane(b, rng) for a, b in q])
def values_of_codes():
    e, c = np.zeros((128, 128, 4), np.float32), np.zeros((128, 2, 4), np.uint8)
    e[np.arange(128), np.arange(128), 0] = 1
    c[:127, :, 0] = np.arange(256).reshape(2, 128).T[:127]
    return mx_ref.matmul(mx_ref.quantize(e.reshape(128, 512).astype(BF)), (c.reshape(128, 8), np.full((16, 2), 127, np.uint8))).T.reshape(-1).astype(np.float64)
CODE_VALUE, SCALE_VALUE = values_of_codes(), 2.0 ** (np.arange(256) - 127.0)
def decode(q):
    return (CODE_VALUE[q[0]].reshape(16, 8, -1, 4) * SCALE_VALUE[q[1]][:, None, :, None] + 0.0).reshape(128, -1).astype(np.float32)
def f(rng, *shape):
    return mx_ref.flush((rng.standard_normal(shape, dtype=np.float32) * np.exp2(rng.integers(-2, 3, shape[:-1] + (1,)))).astype(BF))
def wide(rng, *shape, cols=0):
    v = rng.standard_normal(shape, dtype=np.float32) * np.exp2(rng.integers(-12, 13, shape)).astype(np.float32)
    if cols: v *= np.repeat(np.exp2(rng.integers(-cols, cols + 1, shape[:-2] + (1, shape[-1] // 4))) * (rng.random(shape[:-2] + (1, shape[-1] // 4)) > 0.0625), 4, axis=-1).astype(np.float32)
    return mx_ref.flush(v.astype(BF))
C, R, SWEEPS = 256, 2, 12
def order(p):
    return np.argsort(-(p[::16] + np.float32(0.0)), axis=1, kind="stable")
def matched(a, b):
    gap = np.abs(a.reshape(8, C // 16, 16, 1) - b.reshape(8, C // 16, 1, 16))
    l = np.arange(16)
    k = np.zeros((8, C // 16, 16), np.int64)
    for s in range(SWEEPS):
        at = (l // 2) ^ k
        here = at[:, :, :, None] == l
        best = np.argmin(np.where(here, gap, np.float32(np.inf)), axis=2)
        stays = np.take_along_axis(best, at, axis=2) == l
        k = k + ~stays
    left = np.argsort(here.any(axis=2), axis=2, kind="stable")
    turn = np.argsort(np.argsort(stays, axis=2, kind="stable"), axis=2)
    m = np.where(stays, at, np.take_along_axis(left, turn, axis=2))
    return (m + 16 * np.arange(C // 16)[:, None]).reshape(8, C)
def same(u):
    return np.stack([u] * N)
def numbers_of(rng):
    return {"x": np.array(f(rng, N, 128, 4 * C)), "u": same(np.array(f(rng, 128, 512))), "v": np.array(f(rng, N, 128, 512))}
def packed_layer(w):
    return w.reshape(N, 128, 2048)
def weights(rng, w):
    c, p = packed(packed_layer(w), rng)
    return {"wc": c, "ws": p}
def apart(rng, free):
    w = np.array(f(rng, N, 128, 2048)).reshape(N, 8, 16, 4, 8, 16, 4)
    w[:, :, ~free] = 0
    w[:, :, :, :, :, ~free] = 0
    return weights(rng, w)
def digits(n, k):
    return n[..., None] & (1 << np.arange(k))
def deciding(rng, a, b, k):
    u = np.array(f(rng, 128, 512)).reshape(128, 128, 4)
    for h, m in ((0, a), (1, b)):
        u[:, h::16] = 0
        for g in range(8): u[16 * g:16 * g + 16, 16 * g + h] = (m * k[g]).astype(np.float32).astype(BF)
    return same(u.reshape(128, 512))
def setup_inputs(rng):
    return {**numbers_of(rng), **weights(rng, f(rng, N, 128, 2048))}
def setup_inputs_ties(rng):
    d = numbers_of(rng)
    e = rng.permutation(N)
    x = d["x"].reshape(N, 8, 16, C, 4)
    for r in range(N):
        k = np.zeros(C, int) if r == e[0] else rng.permutation(C) % 3
        a = x[r][:, :8, :3].copy()
        a[:, :, 2] = 0
        x[r][:, :8] = a[:, :, k]
    x[e[1]] = 0
    u = d["u"][0].reshape(8, 16, 128, 4)
    u[:, 8:, ::16] = 0
    u[:, 8:, 1::16] = 0
    w = np.array(f(rng, N, 128, 2048)).reshape(N, 8, 16, 4, 8, 16, 4)
    w[:, :, 8:, :, :, :8] = 0
    return {"x": x.reshape(N, 128, 4 * C), "u": same(u.reshape(128, 512)), "v": d["v"], **weights(rng, w)}
def setup_inputs_near(rng):
    d = numbers_of(rng)
    x = d["x"].astype(np.float32).reshape(N, 8, 16, C, 4)
    s = digits(np.arange(C) // 2, 8) * 2.0 ** -23
    e = digits(rng.integers(0, 24, (N, 8, C)), 8) * 2.0 ** -23
    m = ((np.arange(N) + rng.integers(2)) % 2 * 2.0 - 1.0)[:, None, None]
    x[:, :, :2] = 0
    x[:, :, 0, :, 0] = rng.choice([-1.0, 1.0], (N, 8, 1))
    x[:, :, 0, :, 1] = m * 2.0 ** -9
    x[:, :, 1, :, 0] = m
    x[:, :, 2:8] = rng.integers(4, 8, (N, 8, 6, C, 4)) * rng.choice([-1.0, 1.0], (N, 8, 6, C, 4)) * 0.25
    x[:, :, 8] = s[:, :4]
    x[:, :, 9] = s[:, 4:]
    x[:, :, 10] = e[..., :4]
    x[:, :, 11] = e[..., 4:]
    x[:, :, 12:] = rng.integers(4, 8, (N, 8, 4, C, 4)) * rng.choice([-1.0, 1.0], (N, 8, 4, C, 4)) * 2.0 ** -20
    x *= np.float32(2.0 ** -7)
    a, b = np.zeros((16, 4)), np.zeros((16, 4))
    a[0, 0] = 1
    a[8:10] = 1
    b[0, 1] = 1
    b[1, 0] = 1
    b[10:12] = 1
    i = np.arange(16)
    return {"x": x.reshape(N, 128, 4 * C).astype(BF), "u": deciding(rng, a, b, np.where(rng.permutation(8) < 4, 2.0 ** -30, 1.0)), "v": d["v"], **apart(rng, (i >= 2) & (i < 8))}
def setup_inputs_jilts(rng):
    d = numbers_of(rng)
    i = np.argsort(rng.random((N, 8, C)), axis=2)
    q = 1 + np.argsort(rng.random((N, 8, C // 16, 2, 8)), axis=4)
    q[:, :, :, 0] += 8
    q = q.reshape(N, 8, C // 16, 16)
    q[:, :, 1::3] = 1 + np.argsort(rng.random((N, 8, C // 16, 16)), axis=3)[:, :, 1::3]
    q[:, :, 2::3] = 8
    m = np.take_along_axis(q.reshape(N, 8, C), i, axis=2) * ((np.arange(N) + rng.integers(2)) % 2)[:, None, None]
    x = d["x"].astype(np.float32).reshape(N, 8, 16, C, 4)
    n = rng.integers(1, 64, (N, 8, C, 32)) * rng.choice([-0.0625, 0.0625], (N, 8, C, 32))
    np.put_along_axis(n, rng.integers(0, 32, (N, 8, C, 1)), -32640.0, axis=3)
    x[:, :, :8] = n.reshape(N, 8, C, 8, 4).transpose(0, 1, 3, 2, 4)
    x[:, :, 8:] = 0
    s = digits(C - 1 - i, 12)
    for k in range(3): x[:, :, 8 + k] = s[..., 4 * k:4 * k + 4]
    s = digits(m, 8) * rng.choice([-1.0, 1.0], (N, 8, C, 1))
    for k in range(2): x[:, :, 12 + k] = s[..., 4 * k:4 * k + 4]
    a, b = np.zeros((16, 4)), np.zeros((16, 4))
    a[8:11] = 1
    b[12:14] = 1
    return {"x": x.reshape(N, 128, 4 * C).astype(BF), "u": deciding(rng, a, b, np.ones(8)), "v": d["v"], **apart(rng, np.arange(16) < 8)}
def setup_inputs_huge(rng):
    d = numbers_of(rng)
    x = 2.0 ** 30 * (0.9 + 0.1 * rng.random((N, 8, 16, C, 4)))
    c = np.stack([rng.permutation(C) % 2 * 2.0 - 1.0 for r in range(N)])
    c[rng.permutation(N) < N // 2] = 1
    x[:, :, :6] *= c[:, None, None, :, None]
    x[:, :, 6:] *= ((np.arange(N) + rng.integers(2)) % 2 * 2.0 - 1.0)[:, None, None, None, None]
    u = d["u"][0].reshape(8, 16, 128, 4)
    for h, i, j in ((0, 0, 6), (1, 6, 16)):
        a = 2.0 ** 30 * (1 - 0.05 * rng.random((8, j - i, 8, 4))) * (rng.permutation(8) % 2 * 2.0 - 1.0)[:, None]
        u[:, :, h::16] = 0
        u[:, i:j, h::16] = a.astype(np.float32).astype(BF)
    w = np.zeros((N, 128, 4, 128, 4), np.float32)
    i = np.flatnonzero(np.arange(128) % 16 >= 14)
    for b in range(4): w[:, i, b, i, b] = 8
    return {"x": x.astype(np.float32).reshape(N, 128, 4 * C).astype(BF), "u": same(u.reshape(128, 512)), "v": d["v"], **weights(rng, w.astype(BF))}
def setup_inputs_spread(rng):
    d = setup_inputs(rng)
    d["x"] = wide(rng, N, 128, 4 * C, cols=6)
    return d
def check_inputs(d):
    b = []
    for k in ("x", "u", "v"):
        a = np.abs(d[k].astype(np.float32))
        if not (np.isfinite(a).all() and ((a == 0) | (a >= 2.0 ** -30) & (a <= 2.0 ** 30)).all()): b.append("a value of " + k)
    if (d["u"].astype(np.float32) != d["u"][:1].astype(np.float32)).any(): b.append("u differs between ranks")
    if ((d["wc"] & 127) == 127).any(): b.append("a code of wc")
    return b
def reference(x, u, v, wc, ws):
    qu = mx_ref.quantize(u[0])
    lay = [pk(wc[r], ws[r]) for r in range(N)]
    now = [mx_ref.quantize(x[r]) for r in range(N)]
    for t in range(R):
        o, mark, num, wed = [], [], [], []
        for r in range(N):
            p = mx_ref.matmul(qu, now[r])
            o.append(order(p))
            mark.append(np.take_along_axis(p[1::16], o[r], axis=1))
            num.append(decode(now[r]).astype(BF))
        for r in range(N):
            e = (r + 1) % N
            w = np.zeros((8, C), np.int64)
            np.put_along_axis(w, o[r], np.take_along_axis(o[e], matched(mark[r], mark[e]), axis=1), axis=1)
            wed.append(w)
        came = [decode(mx_ref.quantize(gcols(num[r], np.argsort(wed[r], axis=1)))) for r in range(N)]
        for r in range(N):
            wives = gcols(num[(r + 1) % N], wed[r]).astype(np.float32)
            q = mx_ref.quantize(np.maximum(wives, came[(r - 1) % N]).astype(BF))
            a = num[r].astype(np.float32).reshape(128, C, 4)
            now[r] = mx_ref.quantize(tile([a[:, :, b] + mx_ref.matmul(pick(lay[r], np.arange(128 * b, 128 * b + 128)), q) * np.float32(0.03125) for b in range(4)]))
    y, ol = np.zeros((N, 128, C), np.float32), np.zeros((N, 8, C), np.float32)
    oc, osc = np.zeros((N, 128, 4 * C), np.uint8), np.zeros((N, 16, C), np.uint8)
    for r in range(N):
        y[r] = mx_ref.matmul(mx_ref.quantize(v[r]), now[r])
        ol[r] = wed[r]
        oc[r], osc[r] = emit(now[r])
    return {"y": y, "ol": ol, "oc": oc, "osc": osc}

@@ -1,0 +1,625 @@
+from concourse.bass import DstId, RemoteDMATransfer
+from concourse.mybir import dt, AluOpType as A, ActivationFunctionType as F
+
+R, C = 2, 256
+X4, U8, BF, F32, I32, U16 = "float8_e4m3fn_x4", "uint8", "bfloat16", "float32", "int32", "uint16"
+UP, EQ, SEL, LO, HI, BT, QL, AT, BL, END, PV, PE, CU, HS, XL, Q7, NL = 0, 8, 24, 26, 58, 90, 122, 130, 142, 154, 166, 178, 190, 198, 214, 230, 238
+SCRATCH = {}
+for _n, _w, _d in [
+    ("xt", 1024, BF), ("ut", 512, BF), ("vt", 512, BF), ("uq", 128, X4), ("us", 128, U8), ("ub", 128, X4), ("ubs", 128, U8),
+    ("vq", 128, X4), ("vs", 128, U8), ("wq", 512, X4), ("wsc", 512, U8), ("eq", 512, X4), ("es", 512, U8),
+    ("ones", 576, BF), ("one", 256, BF), ("fe", 528, BF), ("et", 2048, BF),
+    ("xq0", 256, X4), ("xs0", 256, U8), ("xq1", 256, X4), ("xs1", 256, U8), ("xq2", 256, X4), ("xs2", 256, U8),
+    ("lq0", 512, X4), ("ls0", 512, U8), ("lq1", 512, X4), ("ls1", 512, U8),
+    ("rq0", 256, X4), ("rs0", 256, U8), ("rq1", 256, X4), ("rs1", 256, U8),
+    ("gt", 1024, BF), ("gq", 256, X4), ("gs", 256, U8), ("zt", 1024, BF), ("zq", 256, X4), ("zs", 256, U8), ("xn", 1024, BF),
+    ("dn", 1024, BF), ("dp", 1024, BF), ("vg", 1024, BF), ("zp", 1024, BF),
+    ("li", NL + 2, F32), ("lu", NL + 2, U16), ("pi", 16, I32), ("pc", 32, F32), ("rw", 192, F32), ("tmp", 192, F32), ("tmi", 64, I32),
+    ("j16", 256, F32), ("i256", 256, BF), ("eye", 256, F32), ("mk", 256, F32), ("rm", 576, BF), ("d0", 1024, BF),
+    ("ct", 192, F32), ("tau", 192, BF), ("v0", 208, BF), ("va", 208, BF), ("vb", 208, BF),
+    ("t1", 256, F32), ("scn", 256, F32), ("m", 4096, BF), ("acc", 16, F32), ("bm", 256, F32), ("ec", 256, BF), ("es2", 256, BF),
+    ("e32", 16, F32), ("ri", 96, I32), ("pt", 16, U16), ("pz", 16, U16), ("pm", 256, F32), ("sw", 512, F32), ("tr", 512, F32),
+    ("ow", 512, BF), ("otr", 512, BF),
+    ("sm0", 16, F32), ("sm1", 16, F32), ("oo0", 16, BF), ("oo1", 16, BF), ("hl0", 16, U16), ("hl1", 16, U16),
+    ("bn0", 16, F32), ("bn1", 16, F32), ("on0", 16, BF), ("on1", 16, BF), ("hn0", 16, U16), ("hn1", 16, U16),
+    ("at", 192, F32), ("dd", 192, F32), ("gg", 192, F32), ("gh", 1280, F32), ("bb", 2560, BF), ("bt", 1280, BF), ("sc", 1280, BF),
+    ("k0", 192, BF), ("kp", 224, F32), ("dl", 192, BF), ("nk", 384, F32), ("cc", 384, BF), ("yy", 192, BF), ("rr", 192, BF),
+    ("hh", 336, BF), ("he", 384, BF), ("cum", 272, BF), ("sml", 128, BF), ("cn", 16, BF), ("fn", 16, BF), ("tt", 128, BF), ("ux", 48, BF),
+    ("ta", 384, BF), ("tb", 320, BF), ("dnn", 16, BF), ("od", 16, BF), ("mm", 384, BF), ("ss", 384, BF), ("ai", 32, I32), ("al", 16, U16),
+    ("c2", 128, BF), ("ab", 256, BF), ("wj", 256, F32), ("yo", 256, F32),
+]:
+    SCRATCH[_n] = ("sbuf", [128, _w], _d)
+SCRATCH["ps"] = ("psum", [128, 4096], F32)
+POOL = {"v": 14, "s": 10, "t": 8, "g": 6}
+SEMAPHORES = [q + str(i) for q in POOL for i in range(POOL[q])] + ["lx", "lu", "lv", "lw", "loc", "sty", "sts"] + \
+    [n + str(t) for t in range(R) for n in ("aq", "ab", "ao", "ah", "rq", "rs", "rb", "ro")]
+
+
+def relay_of(c, d, T, topo):
+    ok = [e for e in topo.cores_of(c) if T.rank_of(e) is None and topo.may_write(e, d)]
+    return sorted(ok, key=lambda e: topo.die(e) != topo.die(c))[0]
+
+
+def bits(es):
+    return sum(1 << e for e in es)
+
+
+def marks_side(t):
+    return 1 if t % 2 else -1
+
+
+def hand_on(g, core, T, topo):
+    n = len(T.cores)
+    for r in range(n):
+        for side in (1, -1):
+            c, d = T.cores[r], T.cores[(r + side) % n]
+            if topo.may_write(c, d) or relay_of(c, d, T, topo) != core:
+                continue
+            rid, pid = topo.addr(d, core)
+            mask, k = topo.mask(core, d), len(topo.engines(core, d))
+            a = 256 if side == 1 else 0
+            sent = 0
+            for t in range(R):
+                s = str(t)
+                msgs = [("rq", T["lq" + s][:, a:a + 256].bitcast(dt.uint8), T["rq" + s][:].bitcast(dt.uint8), "aq"),
+                        ("rs", T["ls" + s][:, a:a + 256], T["rs" + s][:], "aq")]
+                if side != marks_side(t):
+                    msgs += [("rb", T["hn" + s][:], T["hn" + s][:], "ah")]
+                else:
+                    msgs += [("rb", T["bn" + s][:], T["bn" + s][:], "ab"), ("ro", T["on" + s][:], T["on" + s][:], "ao")]
+                for w, o, i, far in msgs:
+                    g.wait_ge(T.sem[w + s], 8)
+                    g.remote_dma(o, i, T.sem[far + s], T.sem.loc, pid, rid, mask)
+                    sent += k
+            g.wait_ge(T.sem.loc, sent)
+
+
+def rank_program(g, core, T, topo):
+    rank = T.rank_of(core)
+    if rank is None:
+        return hand_on(g, core, T, topo)
+    n = len(T.cores)
+    V, S, P, Y = g.vector, g.scalar, g.tensor, g.sync
+    Q = {"v": V, "s": S, "t": P, "g": g, "y": Y}
+    ev, known, cnt, last, readers = [], {q: 0 for q in Q}, {q: [] for q in POOL}, {}, {}
+
+    def need(q, e):
+        if not known[q] >> e & 1:
+            Q[q].wait_ge(T.sem[ev[e][0]], ev[e][1])
+            known[q] |= ev[e][2]
+
+    def event(sem, val, kn, q):
+        ev.append((sem, val, kn | 1 << len(ev), q))
+        return len(ev) - 1
+
+    def deps(q, rd, wr):
+        d = [last[k] for k in rd + wr if k in last]
+        for k in wr:
+            d += readers.get(k, [])
+        for k in rd:
+            if k[:2] == "ps":
+                d += [e for e in readers.get(k, []) if ev[e][3] != q]
+        for e in sorted(set(d), reverse=True):
+            if not (q == "t" and ev[e][3] == "t"):
+                need(q, e)
+
+    def mark(e, rd, wr):
+        for k in rd:
+            readers.setdefault(k, []).append(e)
+        for k in wr:
+            last[k] = e
+            readers[k] = []
+
+    def op(q, fn, rd, wr):
+        rd, wr = rd.split(), wr.split()
+        deps(q, rd, wr)
+        i, k = len(cnt[q]), POOL[q]
+        if i >= k:
+            need(q, cnt[q][i - k])
+        fn().then_inc(T.sem[q + str(i % k)], 1)
+        e = event(q + str(i % k), i // k + 1, known[q], q)
+        cnt[q].append(e)
+        mark(e, rd, wr)
+
+    tot = {}
+
+    def dma(q, out, in_, sem, rd, wr):
+        rd, wr = rd.split(), wr.split()
+        deps(q, rd, wr)
+        Q[q].dma_start(out, in_).then_inc(T.sem[sem], 16)
+        tot[sem] = tot.get(sem, 0) + 16
+        mark(event(sem, tot[sem], known[q], "d"), [], wr)
+
+    def arrives(key, sem, val):
+        last[key] = event(sem, val, 0, "r")
+
+    def ts(o, i, s1, s2, o0, o1, rd, wr):
+        if s2 is None:
+            op("v", lambda: V.tensor_scalar(o, i, s1, None, o0), rd, wr)
+        else:
+            op("v", lambda: V.tensor_scalar(o, i, s1, s2, o0, o1), rd, wr)
+
+    def tt(o, a, b, f, rd, wr):
+        op("v", lambda: V.tensor_tensor(o, a, b, f), rd, wr)
+
+    def cp(o, i, rd, wr):
+        op("v", lambda: V.tensor_copy(o, i), rd, wr)
+
+    def ms(o, c, wr):
+        op("v", lambda: V.memset(o, c), "", wr)
+
+    def scan(o, a, b, o0, o1, rd, wr):
+        op("v", lambda: V.tensor_tensor_scan(o, a, b, 0.0, o0, o1), rd, wr)
+
+    def act(o, i, rd, wr, f=F.Copy, **kw):
+        op("s", lambda: S.activation(o, i, f, **kw), rd, wr)
+
+    def aff(o, i, scale, bias, rd, wr):
+        act(o, i, rd, wr, f=F.Identity, scale=scale, bias=bias)
+
+    def fill(o, w, c, wr):
+        act(o, T.ones[:, 0:w], "ones", wr, scale=c / 32.0)
+
+    def iota(o, pat, base, wr):
+        op("g", lambda: g.iota(o, pat, base, 0, allow_small_or_imprecise_dtypes=True), "", wr)
+
+    def sel(o, i, pat, cmp, other, base, rd, wr, cm=0):
+        op("g", lambda: g.affine_select(o, i, pat, cmp, other, base, cm), rd, wr)
+
+    def quant(q, s, i, rd, wr):
+        op("v", lambda: V.quantize_mx(q, s, i), rd, wr)
+
+    def mm(bank, w, l, ls, r, rs, rd, start=True, stop=True):
+        op("t", lambda: P.matmul_mx(T.ps[:, 512 * bank:512 * bank + w], l, ls, r, rs, start, stop), rd, "ps%d" % bank)
+
+    def L(a, w):
+        return T.lu[:, a:a + w]
+
+    def ps(b, a, w):
+        return T.ps[:, 512 * b + a:512 * b + a + w]
+
+    way = {}
+    for side in (1, -1):
+        d = T.cores[(rank + side) % n]
+        direct = topo.may_write(core, d)
+        to = d if direct else relay_of(core, d, T, topo)
+        es = topo.engines(core, to)
+        rid, pid = topo.addr(to, core)
+        way[side] = (direct, rid, pid, bits(es[:8] if direct else es[-8:]))
+    sent = [0]
+
+    def send_x(t):
+        s = str(t)
+        deps("g", ["xq" + s], [])
+        for k, (src, far, rel) in enumerate((("xq", "lq", "rq"), ("xs", "ls", "rs"))):
+            tr = []
+            for side in (1, -1):
+                direct, rid, pid, mask = way[side]
+                a = 256 if side == 1 else 0
+                i, o = T[src + s][:], (T[far + s][:, a:a + 256] if direct else T[rel + s][:])
+                if k == 0:
+                    i, o = i.bitcast(dt.uint8), o.bitcast(dt.uint8)
+                tr.append(RemoteDMATransfer(dst_ids=[DstId(rid=rid, pnc=pid)], dma_engine_mask=mask,
+                                            remote_sem=T.sem[("aq" if direct else rel) + s], src=i, dst=o))
+            g.remote_dma_fused(tr, local_sem=T.sem.loc)
+            sent[0] += 16
+
+    def send(side, src, key, far, sem, rel):
+        direct, rid, pid, mask = way[side]
+        deps("g", [key], [])
+        g.remote_dma(far, src, T.sem[sem if direct else rel], T.sem.loc, pid, rid, mask)
+        sent[0] += 8
+
+    for t in range(R):
+        s = str(t)
+        arrives("lq" + s, "aq" + s, 32)
+        arrives("bn" + s, "ab" + s, 8)
+        arrives("on" + s, "ao" + s, 8)
+        arrives("hn" + s, "ah" + s, 8)
+
+    dma("y", T.xt[:], T.x[:], "lx", "", "xt")
+    dma("s", T.ut[:], T.u[:], "lu", "", "ut")
+    dma("y", T.wq[:].bitcast(dt.uint8), T.wc[:], "lw", "", "")
+    dma("y", T.wsc[:], T.ws[:], "lw", "", "wq")
+    dma("y", T.vt[:], T.v[:], "lv", "", "vt")
+
+    li, rw, tmp, tmi, pc, pi = T.li, T.rw, T.tmp, T.tmi, T.pc, T.pi
+    op("g", lambda: g.iota(pi[:, 0:1], [[0, 1]], 0, 1), "", "p")
+    iota(li[:, UP:UP + 8], [[16, 8]], 0, "lup")
+    iota(li[:, EQ:EQ + 16], [[16, 16]], 15, "leq")
+    rows = {}
+    at = [0]
+
+    def row(name, pat, base):
+        w = 1
+        for a, b in pat:
+            w *= b
+        rows[name] = rw[:, at[0]:at[0] + w]
+        iota(rows[name], pat, base, name)
+        at[0] += w
+
+    row("c16", [[1, 16]], 0)
+    iota(T.j16[:], [[0, 16], [1, 16]], 0, "j16")
+    row("bl", [[0, 2], [16, 2], [0, 8]], 0)
+    row("bu", [[0, 2], [8, 8], [0, 2]], 0)
+    row("m0", [[0, 4], [1, 2]], 0)
+    row("m1", [[0, 2], [1, 2], [0, 2]], 0)
+    row("r1", [[2, 4], [-1, 2]], 1)
+    row("r7", [[-1, 8]], 7)
+    row("r37", [[8, 2], [0, 4]], -4)
+    row("u1", [[16, 4]], 136)
+    row("u16", [[0, 2], [-32, 2]], 16)
+    row("u0", [[-64, 2], [0, 2]], 112)
+    row("a8", [[8, 2], [0, 2]], 0)
+    iota(li[:, BL:BL + 8], [[1, 8]], 0, "lbl")
+    iota(li[:, END:END + 8], [[16, 8]], 15, "lend")
+    c16, m04 = rw[:, 0:16], rw[:, 80:84]
+    names = ["q", "e", "h", "q7", "q3", "q2", "a", "a0", "a1", "a3"]
+    col = {k: pc[:, i:i + 1] for i, k in enumerate(names + ["jl", "ju", "b0", "b1", "B0", "B1", "n0", "w", "x1", "x2"])}
+    sh = {"q": (0, 15), "e": (0, 16), "h": (3, 1), "q7": (0, 7), "q3": (0, 3), "q2": (2, 3), "a": (1, 7), "a0": (1, 1), "a1": (2, 1), "a3": (1, 3)}
+
+    ms(T.ones[:], 32.0, "ones")
+    for i, k in enumerate(names):
+        ts(pi[:, i + 1:i + 2], pi[:, 0:1], sh[k][0], sh[k][1], A.logical_shift_right, A.bitwise_and, "p", "pi" + k)
+    ms(li[:, SEL + 1:SEL + 2], 0.0, "ls1")
+    cp(pc[:, 0:10], pi[:, 1:11], " ".join("pi" + k for k in names), "pc")
+    fill(T.rm[:], 576, 1.0, "rm")
+    for a, b, c in ((0, 128, 16), (128, 192, 8), (192, 448, 16), (448, 576, 8)):
+        fill(T.rm[:, a:b:c], (b - a) // c, 0.0, "rm")
+    ts(li[:, SEL:SEL + 1], col["q"], 32.0, col["e"], A.mult, A.add, "pc", "ls0")
+    ts(col["jl"], col["q7"], 0.0, 264.0, A.is_equal, A.mult, "pc", "jl")
+    ts(li[:, SEL:SEL + 1], li[:, SEL:SEL + 1], 1.0, None, A.add, None, "ls0", "ls0")
+    ts(col["ju"], col["q3"], 0.0, 260.0, A.is_equal, A.mult, "pc", "ju")
+    cp(T.lu[:, 0:LO], li[:, 0:LO], "lup leq ls0 ls1", "lu0")
+    ts(T.eye[:], T.j16[:], col["q"], None, A.is_equal, None, "j16 pc", "eye")
+    ts(T.mk[:], T.j16[:], col["q"], 2e29, A.is_ge, A.mult, "j16 pc", "mk")
+
+    late = []
+    XLo, XU = li[:, XL:XL + 16], tmp[:, 0:16]
+
+    def lt(f, *a):
+        late.append(lambda: f(*a))
+
+    a1, a2, a3, a4 = tmp[:, 80:88], tmp[:, 88:96], tmp[:, 96:104], tmp[:, 104:112]
+    u1, u2, u3, u4, u5 = tmp[:, 112:116], tmp[:, 116:120], tmp[:, 120:124], tmp[:, 124:128], tmp[:, 128:132]
+    aff(XLo, c16, 2.0, col["h"], "c16 pc", "xl")
+    aff(XU, c16, 4.0, col["q2"], "c16 pc", "xu")
+    aff(col["b0"], col["q"], 16.0, 16.0, "pc", "cb0")
+    aff(col["x1"], col["a3"], -16.0, 0.0, "pc", "x1")
+    aff(col["x2"], col["h"], -8.0, 0.0, "pc", "x2")
+    aff(li[:, QL:QL + 16], c16, 0.0, col["q"], "c16 pc", "ql")
+    aff(li[:, Q7:Q7 + 8], rw[:, 0:8], 0.0, col["q7"], "c16 pc", "lq7")
+    aff(li[:, BL + 8:BL + 12], li[:, XL:XL + 4], 1.0, 8.0, "xl", "bl2")
+    aff(li[:, END + 8:END + 12], li[:, XL:XL + 4], 8.0, 135.0, "xl", "end2")
+    aff(li[:, CU:CU + 8], li[:, QL:QL + 8], 16.0, 15.0, "ql", "cu")
+    aff(T.mk[:], T.mk[:], 1.0, -1e29, "mk", "mk")
+    fill(T.one[:], 256, 1.0, "one")
+    aff(li[:, AT + 8:AT + 12], rows["a8"], 1.0, col["q7"], "a8 pc", "at")
+    aff(u1, rows["u1"], 1.0, col["x2"], "x2 u1", "U1")
+    aff(u4, rows["u0"], 1.0, col["x1"], "u0 x1", "u4")
+    fill(T.sw[:], 512, 0.0, "sw")
+    lt(ts, col["jl"], col["jl"], col["q7"], -1.0, A.add, A.add, "pc jl", "jl")
+    lt(ts, col["ju"], col["ju"], col["q3"], -1.0, A.add, A.add, "pc ju", "ju")
+    lt(tt, col["w"], col["h"], col["q7"], A.mult, "pc", "w")
+    lt(ts, col["B0"], col["q2"], 3.0, None, A.not_equal, None, "pc", "B0")
+    lt(ts, col["B1"], col["q2"], 2.0, None, A.not_equal, None, "pc", "B1")
+    lt(ts, col["n0"], col["a0"], col["h"], None, A.is_equal, None, "pc", "n0")
+    lt(ts, tmi[:, 0:16], XLo, col["q7"], 1.0, A.add, A.add, "xl pc", "y1")
+    lt(ts, tmi[:, 16:32], XLo, col["q7"], 16.0, A.subtract, A.add, "xl pc", "z1")
+    lt(ts, tmi[:, 32:48], XU, col["q3"], 1.0, A.add, A.add, "xu pc", "y2")
+    lt(ts, tmi[:, 48:64], XU, col["q3"], 8.0, A.subtract, A.add, "xu pc", "z2")
+    lt(ts, tmi[:, 0:32], tmi[:, 0:32], 15, None, A.bitwise_and, None, "z1", "y1")
+    lt(ts, tmi[:, 32:64], tmi[:, 32:64], 7, None, A.bitwise_and, None, "z2", "y2")
+    lt(ts, col["b0"], col["w"], -8.0, col["b0"], A.mult, A.add, "w", "cb0")
+    lt(tt, tmp[:, 16:80], tmi[:], rw[:, 16:80], A.add, "y1 y2 bl bu", "yz")
+    NEARLY = len(late)
+    lt(aff, li[:, BT:BT + 16], tmp[:, 32:48], 8.0, col["jl"], "yz jl", "lbt1")
+    lt(aff, li[:, BT + 16:BT + 32], tmp[:, 64:80], 4.0, col["ju"], "yz ju", "lbt2")
+    lt(aff, col["b1"], col["h"], -8.0, col["b0"], "pc cb0", "cb1")
+    lt(tt, li[:, LO:LO + 16], XLo, tmp[:, 16:32], A.min, "xl yz", "lo1")
+    lt(tt, li[:, LO + 16:LO + 32], XU, tmp[:, 48:64], A.min, "xu yz", "lo2")
+    lt(tt, li[:, HI:HI + 16], XLo, tmp[:, 16:32], A.max, "xl yz", "hi1")
+    lt(tt, li[:, HI + 16:HI + 32], XU, tmp[:, 48:64], A.max, "xu yz", "hi2")
+    lt(ts, a1, rows["m1"], col["a1"], None, A.not_equal, None, "m1 pc", "a1")
+    lt(ts, u2, m04, col["a1"], col["n0"], A.not_equal, A.mult, "m0 pc n0", "u2")
+    lt(ts, a3, rows["m0"], col["a0"], None, A.not_equal, None, "m0 pc", "a3")
+    lt(tt, a1, a1, rows["r37"], A.mult, "r37", "a1")
+    lt(tt, u2, u2, rows["u16"], A.mult, "u16", "u2")
+    lt(ts, u3, m04, col["a1"], col["n0"], A.is_equal, A.mult, "m0 pc n0", "u3")
+    lt(tt, a1, a1, rows["r7"], A.add, "r7", "a1")
+    lt(tt, u1, u1, u2, A.add, "u2", "U1")
+    lt(aff, u5, u3, 8.0, 7.0, "u3", "u5")
+    lt(ts, a4, rw[:, 0:8], col["a"], 192.0, A.is_equal, A.mult, "c16 pc", "a4")
+    lt(tt, a2, rows["r1"], a1, A.subtract, "a1 r1", "a2")
+    lt(tt, u4, u4, u1, A.subtract, "U1", "u4")
+    lt(ts, li[:, HS:HS + 8], rw[:, 0:8], col["b0"], col["B0"], A.add, A.mult, "c16 cb0 B0", "hs1")
+    lt(tt, a2, a2, a3, A.mult, "a3", "a2")
+    lt(tt, u4, u4, u3, A.mult, "u3", "u4")
+    lt(tt, u2, u3, rows["a8"], A.mult, "u3 a8", "u2")
+    lt(tt, a1, a1, a2, A.add, "a2", "a1")
+    lt(tt, u1, u1, u4, A.add, "u4", "U1")
+    lt(aff, li[:, PE:PE + 8], a1, 16.0, 15.0, "a1", "pe1")
+    lt(ts, li[:, HS + 8:HS + 16], rw[:, 8:16], col["b1"], col["B1"], A.add, A.mult, "c16 cb1 B1", "hs2")
+    lt(ts, a2, a1, 16.0, col["q"], A.mult, A.add, "a1 pc", "a2")
+    lt(tt, u2, u2, u1, A.add, "U1", "u2")
+    lt(tt, li[:, PE + 8:PE + 12], u1, u5, A.add, "U1 u5", "pe2")
+    lt(tt, li[:, PV:PV + 8], a2, a4, A.max, "a2 a4", "pv1")
+    lt(ts, li[:, PV + 8:PV + 12], u2, col["q7"], None, A.add, None, "u2 pc", "pv2")
+    lt(cp, T.lu[:, LO:NL], li[:, LO:NL], "xl lo1 lo2 hi1 hi2 lbt1 lbt2 ql at bl2 end2 cu lq7 hs1 hs2 pe1 pe2 pv1 pv2 lbl lend", "lu")
+    d0, one = T.d0, T.one
+
+    def tables_a():
+        iota(T.i256[:], [[1, 256]], 0, "i256")
+        sel(T.fe[:], T.ones[:, 0:528], [[-1, 528]], A.is_equal, 0.0, 3, "ones", "fe", cm=4)
+        sel(d0[:, 0:256], one[:], [[0, 2], [1, 16], [1, 8]], A.not_equal, -1.0, -15, "one", "d0a")
+        sel(d0[:, 256:512], one[:], [[0, 8], [1, 8], [1, 4]], A.not_equal, -1.0, -7, "one", "d0b")
+        sel(d0[:, 512:768], one[:], [[0, 2], [1, 16], [-1, 8]], A.not_equal, -1.0, 1, "one", "d0c")
+        sel(d0[:, 768:1024], one[:], [[0, 8], [1, 8], [-1, 4]], A.not_equal, -1.0, 1, "one", "d0d")
+        iota(d0[:, 0:256:8], [[0, 32]], 0, "d0a")
+        iota(d0[:, 256:512:4], [[0, 64]], 0, "d0b")
+        sel(d0[:, 513:768:8], one[:, 0:32], [[0, 2], [1, 16]], A.is_ge, -1.0, -8, "one", "d0c")
+        sel(d0[:, 769:1024:4], one[:, 0:64], [[0, 8], [1, 8]], A.is_ge, -1.0, -4, "one", "d0d")
+        iota(d0[:, 512:768:8], [[0, 32]], 0, "d0c")
+        iota(d0[:, 768:1024:4], [[0, 64]], 0, "d0d")
+        iota(d0[:, 513:768:128], [[0, 2]], 1, "d0c")
+        iota(d0[:, 769:1024:32], [[0, 8]], 1, "d0d")
+
+    def tables_b():
+        sel(T.tau[:, 128:192], one[:, 0:64], [[0, 8], [1, 8]], A.is_ge, -1.0, -3, "one", "tau2")
+        iota(T.ct[:, 128:192], [[-64, 8], [-1, 8]], 7 - 512, "ct2")
+        sel(T.tau[:, 0:128], one[:, 0:128], [[0, 8], [1, 16]], A.is_ge, -1.0, -7, "one", "tau1")
+        iota(T.ct[:, 0:128], [[-64, 8], [-1, 16]], 15, "ct")
+        sel(T.v0[:, 0:128], T.ones[:, 0:128], [[-1, 8], [1, 8], [0, 2]], A.is_equal, 0.0, 0, "ones", "v0")
+
+    def cells():
+        for o, w, c, k in ((T.kp[:, 0:16], 16, 64.0, "kpa"), (T.kp[:, 208:224], 16, 2000.0, "kpb"), (T.va[:, 192:208], 16, 32.0, "vac"),
+                           (T.vb[:, 128:208], 80, 32.0, "vbc"), (T.v0[:, 128:208], 80, 32.0, "v0c"), (T.yy[:], 192, 0.0, "yy"),
+                           (T.va[:, 128:192], 64, 0.0, "vau"), (T.hh[:, 0:16], 16, 0.0, "hh0"), (T.cum[:, 0:16], 16, 0.0, "cum0"),
+                           (T.cn[:], 16, 0.0, "cn"), (T.fn[:], 16, 0.0, "fn"), (T.ux[:, 0:16], 16, 0.0, "uu0"), (T.dnn[:], 16, 0.0, "dnn")):
+            fill(o, w, c, k)
+
+    for f in late[:NEARLY]:
+        f()
+    quant(T.uq[:], T.us[:], T.ut[:], "ut", "uq")
+    cp(T.ub[:].bitcast(dt.uint32), T.uq[:].bitcast(dt.uint32).indirect(L(UP, 8)), "uq lu0", "ub")
+    cp(T.ubs[:], T.us[:].indirect(L(UP, 8)), "uq lu0", "ubs")
+    quant(T.xq0[:], T.xs0[:], T.xt[:], "xt", "xq0")
+
+    def E(b):
+        return T.eq[:, 128 * b:128 * b + 128], T.es[:, 128 * b:128 * b + 128]
+
+    for t in range(R):
+        s = str(t)
+        xq, xs, lq, ls = T["xq" + s], T["xs" + s], T["lq" + s], T["ls" + s]
+        sm, oo, hl, bn, on, hn = [T[k + s] for k in ("sm", "oo", "hl", "bn", "on", "hn")]
+        side = marks_side(t)
+        mm(0, 256, T.ub[:], T.ubs[:], xq[:], xs[:], "ub ubs xq" + s)
+        mm(1, 256, T.uq[:], T.us[:], xq[:], xs[:], "uq xq" + s)
+        send_x(t)
+        if t == 0:
+            tables_a()
+        tt(T.t1[:], ps(0, 0, 256), T.eye[:], A.mult, "ps0 eye", "t1")
+        act(T.pm[:], ps(1, 0, 256), "ps1", "pm")
+        scan(T.scn[:], T.rm[:, 192:448], T.t1[:], A.mult, A.add, "rm t1", "scn")
+        for c in range(16):
+            sc, m = T.scn[:, 16 * c + 15:16 * c + 16], 256 * c
+            if c:
+                ts(T.m[:, m:m + 16 * c], ps(0, 0, 16 * c), sc, None, A.is_ge, None, "ps0 scn", "ma%d" % c)
+            ts(T.m[:, m + 16 * c:m + 256], ps(0, 16 * c, 256 - 16 * c), sc, None, A.is_gt, None, "ps0 scn", "mb%d" % c)
+            act(T.m[:, m:m + 256], T.m[:, m:m + 256], "", "ma%d mb%d acc%d" % (c, c, c), scale=32.0, accum_out=T.acc[:, c:c + 1])
+        tt(T.bm[:], ps(0, 0, 256), T.mk[:], A.max, "ps0 mk", "bm")
+        if t == 0:
+            fill(T.ow[:], 512, 0.0, "ow")
+        tt(T.ec[:], T.scn[:].indirect(L(EQ, 16)), T.bm[:], A.is_equal, "scn bm lu0", "ec")
+        scan(T.es2[:], T.rm[:, 192:448], T.ec[:], A.mult, A.add, "rm ec", "es2")
+        ts(T.e32[:], T.es2[:, 15:256:16], 32.0, None, A.mult, None, "es2", "e32")
+        ri = T.ri
+        tt(ri[:, 0:16], T.acc[:], T.e32[:], A.add, "e32 " + " ".join("acc%d" % c for c in range(16)), "r32")
+        ts(ri[:, 16:32], ri[:, 0:16], 9, None, A.logical_shift_right, None, "r32", "hi")
+        ts(ri[:, 32:48], ri[:, 16:32], -511.0, col["e"], A.mult, A.add, "hi pc", "h2")
+        tt(ri[:, 48:64], ri[:, 32:48], ri[:, 0:16], A.add, "h2 r32", "pti")
+        cp(T.pt[:], ri[:, 48:64], "pti", "pt")
+        cp(T.sw[:].indirect(T.pt[:]), T.pm[:], "pm pt", "sw")
+        op("v", lambda: V.transpose(T.tr[:], T.sw[:]), "sw", "tr")
+        cp(sm[:], T.tr[:].indirect(L(SEL, 1)), "tr lu0", "sm" + s)
+        send(side, sm[:], "sm" + s, bn[:], "ab" + s, "rb" + s)
+        if t == 0:
+            tables_b()
+            for b in range(4):
+                act(T.et[:, 512 * b:512 * b + 512], T.fe[:, 3 - b:515 - b], "fe", "et%d" % b)
+            for f in late[NEARLY:]:
+                f()
+        act(T.at[:], sm[:].indirect(L(AT if side < 0 else BL, 12)), "lu sm" + s, "at_")
+        if t == 0:
+            cells()
+        else:
+            fill(T.va[:, 128:192], 64, 0.0, "vau")
+        cp(T.ow[:].indirect(T.pt[:]), T.i256[:], "i256 pt", "ow")
+        ts(ri[:, 64:80], ri[:, 0:16], 0.5, None, A.mult, None, "r32", "r16")
+        ts(ri[:, 80:96], ri[:, 16:32], -255.0, None, A.mult, None, "hi", "h3")
+        op("v", lambda: V.transpose(T.otr[:], T.ow[:]), "ow", "otr")
+        tt(ri[:, 64:80], ri[:, 64:80], ri[:, 80:96], A.add, "r16 h3", "r16")
+        cp(oo[:], T.otr[:].indirect(L(SEL, 1)), "otr lu0", "oo" + s)
+        send(side, oo[:], "oo" + s, on[:], "ao" + s, "ro" + s)
+        cp(T.pz[:], ri[:, 64:80], "r16", "pz")
+        (so, sk), (to, tk) = ((oo, "oo" + s), (on, "on" + s))[::-side]
+
+        def dso(j):
+            if j:
+                tt(T.od[:, 1:16], so[:, 1:16], so[:, 0:15], A.subtract, sk, "od1")
+            else:
+                cp(T.od[:, 0:1], so[:, 0:1], sk, "od0")
+
+        def dto(j):
+            if j:
+                tt(T.dnn[:, 1:8], to[:, 9:16], to[:, 8:15], A.subtract, "dnn " + tk, "dx1")
+            else:
+                cp(T.dnn[:, 0:1], to[:, 8:9], "dnn " + tk, "dx0")
+
+        def tab_s():
+            act(T.tb[:, 0:192], so[:].indirect(L(AT, 12)), "lu " + sk, "tb1")
+            act(T.tb[:, 192:320], T.od[:].indirect(L(QL, 8)), "lu od0 od1", "tb2")
+
+        def tab_t():
+            act(T.ta[:, 0:256], to[:].indirect(L(QL, 16)), "lu " + tk, "ta1")
+            act(T.ta[:, 256:384], T.dnn[:].indirect(L(Q7, 8)), "lu dx0 dx1", "ta2")
+
+        own_d, far_d, own_t, far_t = (dso, dto, tab_s, tab_t) if side < 0 else (dto, dso, tab_t, tab_s)
+        own_d(1), own_d(0)
+        if t == 0:
+            for b in range(4):
+                quant(*E(b), T.et[:, 512 * b:512 * b + 512], "et%d" % b, "eq%d" % b)
+        for b in range(4):
+            mm(2 + b, 512, *E(b), lq[:], ls[:], "eq%d lq%s" % (b, s))
+        tt(T.dd[:], bn[:].indirect(L(BL if side < 0 else AT, 12)), T.at[:], A.subtract, "lu at_ bn" + s, "dd")
+
+        def win(buf, i):
+            return buf[:, 128:192] if i == 4 else buf[:, 32 * i:32 * i + 32]
+
+        def hi(i):
+            act(T.gh[:, 256 * i:256 * i + 256], win(T.dd, i).indirect(L(HI + 16 * (i == 4), 16)), "dd lu", "gh%d" % i, f=F.Abs)
+
+        def beat(i):
+            u = 256 * (i == 4)
+            tt(T.bb[:, 512 * i:512 * i + 256], win(T.gg, i).indirect(L(LO + 16 * (i == 4), 16)), T.gh[:, 256 * i:256 * i + 256], A.is_le, "gg lu gh%d" % i, "b%d" % i)
+            scan(T.bb[:, 512 * i + 256:512 * i + 512], d0[:, u:u + 256], T.bb[:, 512 * i:512 * i + 256], A.mult, A.add, "d0a d0b b%d" % i, "br%d" % i)
+
+        def turn(i, q):
+            o, w = T.bt[:, 256 * i:256 * i + 256], T.bb[:, 512 * i:512 * i + 512].indirect(L(BT + 16 * (i == 4), 16))
+            (act if q == "s" else cp)(o, w, "lu b%d br%d" % (i, i), "bt_%d" % i)
+
+        def sums(i):
+            u = 512 + 256 * (i == 4)
+            scan(T.sc[:, 256 * i:256 * i + 256], d0[:, u:u + 256], T.bt[:, 256 * i:256 * i + 256], A.mult, A.add, "d0c d0d bt_%d" % i, "sc%d" % i)
+
+        hi(4)
+        ts(T.nk[:, 0:192], T.dd[:], -1.0, None, A.mult, None, "dd", "nk")
+        tt(T.gg[:], T.nk[:, 0:192], T.dd[:], A.max, "dd nk", "gg")
+        hi(0), beat(4), hi(1), beat(0), hi(2), beat(1), hi(3), turn(4, "s"), beat(2), turn(0, "s"), beat(3)
+        turn(1, "s"), turn(3, "v"), sums(4), turn(2, "s"), sums(0)
+        tt(T.k0[:, 128:192], T.sc[:, 1027:1280:4], T.tau[:, 128:192], A.mult, "sc4 tau2", "k0b")
+        sums(3), sums(1)
+        kp = T.kp
+        tt(kp[:, 144:208], T.k0[:, 128:192], T.ct[:, 128:192], A.add, "k0b ct2", "kp2")
+        sums(2)
+        tt(T.k0[:, 0:128], T.sc[:, 7:1024:8], T.tau[:, 0:128], A.mult, "sc0 sc1 sc2 sc3 tau1", "k0a")
+        tt(kp[:, 16:144], T.k0[:, 0:128], T.ct[:, 0:128], A.add, "k0a ct", "kp1")
+        KP = "kp1 kp2 kpa kpb lu"
+        aff(T.nk[:, 0:192], kp[:, 16:224].indirect(L(PV, 12)), -1.0, 32.0, KP, "nk")
+        tt(T.dl[:], kp[:, 16:208], kp[:, 15:207], A.subtract, KP, "dl")
+        aff(T.nk[:, 192:384], kp[:, 16:208], -1.0, 32.0, KP, "nk2")
+        for b in range(4):
+            act(T.gt[:, b:1024:4], ps(2 + b, 256, 256), "ps%d" % (2 + b), "gt%d" % b, scale=0.03125)
+        own_t()
+        for b in range(4):
+            act(T.dn[:, 256 * b:256 * b + 256], ps(2 + b, 0, 256), "ps%d" % (2 + b), "dn%d" % b, scale=0.03125)
+        for k in range(12):
+            src, sn = (T.v0, "v0 v0c") if k == 0 else (T.va, "va vac vau") if k % 2 else (T.vb, "vb vbc")
+            dst, dn_ = (T.vb, "vb") if k % 2 else (T.va, "va")
+            w, w2 = (128 if k < 8 else 192), (128 if k < 7 else 192)
+            scan(T.yy[:, 0:w], T.dl[:, 0:w], src[:, 0:w], A.add, A.max, "dl " + sn, "yy")
+            if k == 0:
+                tt(T.cc[:, 0:192], kp[:, 16:224].indirect(L(PE, 12)), T.nk[:, 0:192], A.add, KP + " nk", "cc")
+            if k == 11:
+                break
+            tt(T.rr[:, 0:w2], T.yy[:].indirect(L(PE, w2 // 16)), T.cc[:, 0:w2], A.is_gt, "yy cc lu", "rr")
+            if k == 2:
+                tt(T.cc[:, 192:384], kp[:, 16:224].indirect(L(END, 12)), T.nk[:, 192:384], A.add, KP + " nk2", "cf")
+            if k == 4:
+                quant(T.gq[:], T.gs[:], T.gt[:], "gt0 gt1 gt2 gt3", "gq")
+                for b in range(4):
+                    bank = (6, 7, 0, 1)[b]
+                    mm(bank, 256, *E(b), T.gq[:], T.gs[:], "eq%d gq" % b)
+                    act(T.dp[:, 256 * b:256 * b + 256], ps(bank, 0, 256), "ps%d" % bank, "dp%d" % b, scale=0.03125)
+                for b in range(4):
+                    mm(2 + b, 256, *E(b), xq[:], xs[:], "eq%d xq%s" % (b, s), True, False)
+            if k in (6, 7):
+                far_d(k - 6)
+            if k == 7:
+                far_t()
+            tt(dst[:, 0:w2], src[:].indirect(L(PV, w2 // 16)), T.rr[:, 0:w2], A.mult, "rr lu " + sn, dn_ + (" vau" if k % 2 == 0 and w2 > 128 else ""))
+        sml, hh, cum, ux = T.sml, T.hh, T.cum, T.ux
+        tt(T.rr[:], T.yy[:].indirect(L(END, 12)), T.cc[:, 192:384], A.is_le, "yy cf lu", "rr")
+        ts(sml[:, 0:8], T.yy[:, 135:192:8], 16.0, None, A.is_lt, None, "yy", "fr")
+        tt(hh[:, 16:208], T.va[:, 0:192], T.rr[:], A.min, "va vau rr", "hh")
+        scan(T.cn[:, 1:9], sml[:, 0:8], sml[:, 0:8], A.add, A.max, "fr cn", "cn1")
+        cp(T.he[:, 0:256], hh[:, 0:208].indirect(L(HS, 16)), "hh hh0 lu", "he")
+        act(T.c2[:], T.cn[:].indirect(L(Q7, 8)), "cn1 lu", "c2")
+
+        def free_seats():
+            ts(sml[:, 16:24], T.yy[:, 135:192:8], 16.0, -1.0, A.is_lt, A.mult, "yy", "frn")
+            tt(T.fn[:, 0:8], T.cn[:, 1:9], sml[:, 16:24], A.mult, "cn1 frn fn", "fn1")
+
+        def seats(out, key):
+            tt(T.tt[:], T.fn[:].indirect(L(BL, 8)), T.j16[:, 0:128], A.add, "fn1 j16 lu", "tt")
+            tt(hh[:, 208:336], cum[:].indirect(L(CU, 8)), T.tt[:], A.is_gt, "cum cum0 tt lu", "hh2")
+            tt(T.mm[:, 0:320], hh[:, 16:336], T.tb[:], A.mult, "hh hh2 tb1 tb2", "mm")
+            scan(T.ss[:, 0:320], T.rm[:, 0:320], T.mm[:, 0:320], A.mult, A.add, "rm mm", "ss")
+            tt(T.ai[:, 8:16], T.ss[:, 135:192:8], T.ss[:, 207:320:16], A.add, "ss", "ai2")
+            cp(T.ai[:, 0:8], T.ss[:, 15:128:16], "ss", "ai1")
+            cp(out, T.ai[:, 0:16], "ai1 ai2", key)
+
+        def suitors(out, key):
+            tt(ux[:, 16:32], T.i256[:, 1:17], cum[:, 31:272:16], A.subtract, "cum i256", "uu")
+            tt(sml[:, 32:48], ux[:, 16:32], ux[:, 15:31], A.subtract, "uu uu0", "un")
+            tt(ux[:, 32:48], ux[:, 16:32], sml[:, 32:48], A.mult, "uu un", "uv")
+            tt(T.he[:, 256:384], ux[:, 32:48].indirect(L(XL, 8)), T.c2[:], A.is_gt, "uv c2 lu", "he2")
+            tt(T.mm[:], T.he[:], T.ta[:], A.mult, "he he2 ta1 ta2", "mm")
+            scan(T.ss[:], T.rm[:, 192:576], T.mm[:], A.mult, A.add, "rm mm", "ss")
+            tt(T.ai[:, 16:32], T.ss[:, 15:256:16], T.ss[:, 263:384:8], A.add, "ss", "ai3")
+            cp(out, T.ai[:, 16:32], "ai3", key)
+
+        if side < 0:
+            free_seats()
+        scan(cum[:, 16:272], T.he[:, 0:256], T.he[:, 0:256], A.add, A.max, "he", "cum")
+        (seats if side < 0 else suitors)(hl[:], "hl" + s)
+        send(-side, hl[:], "hl" + s, hn[:], "ah" + s, "rb" + s)
+        if side > 0:
+            free_seats()
+        (suitors if side < 0 else seats)(T.al[:], "al")
+        (d1, k1), (d2, k2) = ((T.dn, "dn"), (T.dp, "dp"))[::-side]
+        for b in range(4):
+            o, w = T.vg[:, 256 * b:256 * b + 256], d1[:, 256 * b:256 * b + 256].indirect(T.al[:])
+            (act if b % 2 else cp)(o, w, "al %s%d" % (k1, b), "vg%d" % b)
+        if t == 0:
+            quant(T.vq[:], T.vs[:], T.vt[:], "vt", "vq")
+        if t == R - 1:
+            act(T.ab[:], T.i256[:].indirect(T.al[:] if side < 0 else hn[:]), "al i256 hn" + s, "ab")
+        for b in range(4):
+            tt(T.zp[:, 256 * b:256 * b + 256], d2[:, 256 * b:256 * b + 256].indirect(hn[:]), T.vg[:, 256 * b:256 * b + 256], A.max,
+               "%s%d vg%d hn%s" % (k2, b, b, s), "zp%d" % b)
+            if b < 3:
+                act(T.zt[:, b:1024:4], T.zp[:, 256 * b:256 * b + 256].indirect(T.pz[:]), "pz zp%d" % b, "zt%d" % b)
+        cp(T.zt[:, 3:1024:4], T.zp[:, 768:1024].indirect(T.pz[:]), "pz zp3", "zt3")
+        if t == R - 1:
+            act(T.wj[:], T.ab[:].indirect(T.pz[:]), "ab pz", "wj")
+            for k in range(8):
+                dma("y", T.ol[k:k + 1, :], T.wj[16 * k:16 * k + 1, :], "sty", "wj", "")
+        quant(T.zq[:], T.zs[:], T.zt[:], "zt0 zt1 zt2 zt3", "zq")
+        for b in (0, 2, 1, 3):
+            mm(2 + b, 256, T.wq[:, 128 * b:128 * b + 128], T.wsc[:, 128 * b:128 * b + 128], T.zq[:], T.zs[:], "wq zq", False, True)
+        for b in (0, 2, 1, 3):
+            if b < 2:
+                act(T.xn[:, b:1024:4], ps(2 + b, 0, 256), "ps%d" % (2 + b), "xn%d" % b, scale=0.03125)
+            else:
+                ts(T.xn[:, b:1024:4], ps(2 + b, 0, 256), 0.03125, None, A.mult, None, "ps%d" % (2 + b), "xn%d" % b)
+        s2 = str(t + 1)
+        quant(T["xq" + s2][:], T["xs" + s2][:], T.xn[:], "xn0 xn1 xn2 xn3", "xq" + s2)
+
+    s = str(R)
+    xq, xs = T["xq" + s], T["xs" + s]
+    mm(6, 128, T.vq[:], T.vs[:], xq[:, 0:128], xs[:, 0:128], "vq xq" + s)
+    mm(7, 128, T.vq[:], T.vs[:], xq[:, 128:256], xs[:, 128:256], "vq xq" + s)
+    dma("y", T.oc[:], xq[:].bitcast(dt.uint8), "sty", "xq" + s, "")
+    cp(T.yo[:, 0:128], ps(6, 0, 128), "ps6", "yo1")
+    dma("s", T.osc[0:4, :], xs[0:4, :], "sts", "xq" + s, "")
+    act(T.yo[:, 128:256], ps(7, 0, 128), "ps7", "yo2")
+    dma("s", T.y[:], T.yo[:], "sts", "yo1 yo2", "")
+    for k in range(1, 4):
+        dma("y", T.osc[4 * k:4 * k + 4, :], xs[32 * k:32 * k + 4, :], "sty", "xq" + s, "")
+    for q in POOL:
+        for e in cnt[q][-POOL[q]:]:
+            need("g", e)
+    g.wait_ge(T.sem.loc, sent[0])
+    g.wait_ge(T.sem.sty, tot["sty"])
+    g.wait_ge(T.sem.sts, tot["sts"])

@@ -3,7 +3,7 @@ from concourse.mybir import dt, AluOpType as A, ActivationFunctionType as F
 
 R, C = 2, 256
 X4, U8, BF, F32, I32, U16 = "float8_e4m3fn_x4", "uint8", "bfloat16", "float32", "int32", "uint16"
-UP, EQ, SEL, LO, HI, BT, QL, AT, BL, END, PV, PE, CU, HS, XL, Q7, NL = 0, 8, 24, 26, 58, 90, 122, 130, 142, 154, 166, 178, 190, 198, 214, 230, 238
+UP, EQ, SEL, LO, HI, BT, QL, AT, BL, PV, CU, HS, XL, Q7, NL = 0, 8, 24, 26, 58, 90, 122, 130, 142, 154, 166, 174, 190, 206, 214
 SCRATCH = {}
 for _n, _w, _d in [
     ("xt", 1024, BF), ("ut", 512, BF), ("vt", 512, BF), ("uq", 128, X4), ("us", 128, U8), ("ub", 128, X4), ("ubs", 128, U8),
@@ -16,14 +16,14 @@ for _n, _w, _d in [
     ("dn", 1024, BF), ("dp", 1024, BF), ("vg", 1024, BF), ("zp", 1024, BF),
     ("li", NL + 2, F32), ("lu", NL + 2, U16), ("pi", 16, I32), ("pc", 32, F32), ("rw", 192, F32), ("tmp", 192, F32), ("tmi", 64, I32),
     ("j16", 256, F32), ("i256", 256, BF), ("eye", 256, F32), ("mk", 256, F32), ("rm", 576, BF), ("d0", 1024, BF),
-    ("ct", 192, F32), ("tau", 192, BF), ("v0", 208, BF), ("va", 208, BF), ("vb", 208, BF),
+    ("cd", 192, BF), ("tau", 192, BF), ("v0", 208, BF), ("va", 208, BF), ("vb", 208, BF),
     ("t1", 256, F32), ("scn", 256, F32), ("m", 4096, BF), ("acc", 16, F32), ("bm", 256, F32), ("ec", 256, BF), ("es2", 256, BF),
     ("e32", 16, F32), ("ri", 96, I32), ("pt", 16, U16), ("pz", 16, U16), ("pm", 256, F32), ("sw", 512, F32), ("tr", 512, F32),
     ("ow", 512, BF), ("otr", 512, BF),
     ("sm0", 16, F32), ("sm1", 16, F32), ("oo0", 16, BF), ("oo1", 16, BF), ("hl0", 16, U16), ("hl1", 16, U16),
     ("bn0", 16, F32), ("bn1", 16, F32), ("on0", 16, BF), ("on1", 16, BF), ("hn0", 16, U16), ("hn1", 16, U16),
     ("at", 192, F32), ("dd", 192, F32), ("gg", 192, F32), ("gh", 1280, F32), ("bb", 2560, BF), ("bt", 1280, BF), ("sc", 1280, BF),
-    ("k0", 192, BF), ("kp", 224, F32), ("dl", 192, BF), ("nk", 384, F32), ("cc", 384, BF), ("yy", 192, BF), ("rr", 192, BF),
+    ("k0", 208, BF), ("k1", 192, BF), ("dl", 208, BF), ("db", 192, BF), ("sg", 192, BF), ("yy", 192, BF), ("zz", 224, BF), ("rr", 192, BF),
     ("hh", 336, BF), ("he", 384, BF), ("cum", 272, BF), ("sml", 128, BF), ("cn", 16, BF), ("fn", 16, BF), ("tt", 128, BF), ("ux", 48, BF),
     ("ta", 384, BF), ("tb", 320, BF), ("dnn", 16, BF), ("od", 16, BF), ("mm", 384, BF), ("ss", 384, BF), ("ai", 32, I32), ("al", 16, U16),
     ("c2", 128, BF), ("ab", 256, BF), ("wj", 256, F32), ("yo", 256, F32),
@@ -68,7 +68,7 @@ def hand_on(g, core, T, topo):
                 else:
                     msgs += [("rb", T["bn" + s][:], T["bn" + s][:], "ab"), ("ro", T["on" + s][:], T["on" + s][:], "ao")]
                 for w, o, i, far in msgs:
-                    g.wait_ge(T.sem[w + s], 8)
+                    g.wait_ge(T.sem[w + s], 8 if w in ("rq", "rs") else len(topo.engines(c, core)))
                     g.remote_dma(o, i, T.sem[far + s], T.sem.loc, pid, rid, mask)
                     sent += k
             g.wait_ge(T.sem.loc, sent)
@@ -185,16 +185,16 @@ def rank_program(g, core, T, topo):
         to = d if direct else relay_of(core, d, T, topo)
         es = topo.engines(core, to)
         rid, pid = topo.addr(to, core)
-        way[side] = (direct, rid, pid, bits(es[:8] if direct else es[-8:]))
+        way[side] = (direct, rid, pid, bits(es[:8] if direct else es[-8:]), es)
     sent = [0]
 
     def send_x(t):
         s = str(t)
-        deps("g", ["xq" + s], [])
+        deps("g", ["xq" + s, "xr" + s], [])
         for k, (src, far, rel) in enumerate((("xq", "lq", "rq"), ("xs", "ls", "rs"))):
             tr = []
             for side in (1, -1):
-                direct, rid, pid, mask = way[side]
+                direct, rid, pid, mask, es = way[side]
                 a = 256 if side == 1 else 0
                 i, o = T[src + s][:], (T[far + s][:, a:a + 256] if direct else T[rel + s][:])
                 if k == 0:
@@ -205,21 +205,25 @@ def rank_program(g, core, T, topo):
             sent[0] += 16
 
     def send(side, src, key, far, sem, rel):
-        direct, rid, pid, mask = way[side]
+        direct, rid, pid, mask, es = way[side]
         deps("g", [key], [])
-        g.remote_dma(far, src, T.sem[sem if direct else rel], T.sem.loc, pid, rid, mask)
-        sent[0] += 8
+        g.remote_dma(far, src, T.sem[sem if direct else rel], T.sem.loc, pid, rid, bits(es))
+        sent[0] += len(es)
+
+    def brought(side):
+        c = T.cores[(rank + side) % n]
+        return len(topo.engines(c if topo.may_write(c, core) else relay_of(c, core, T, topo), core))
 
     for t in range(R):
         s = str(t)
         arrives("lq" + s, "aq" + s, 32)
-        arrives("bn" + s, "ab" + s, 8)
-        arrives("on" + s, "ao" + s, 8)
-        arrives("hn" + s, "ah" + s, 8)
+        arrives("bn" + s, "ab" + s, brought(-marks_side(t)))
+        arrives("on" + s, "ao" + s, brought(-marks_side(t)))
+        arrives("hn" + s, "ah" + s, brought(marks_side(t)))
 
     dma("y", T.xt[:], T.x[:], "lx", "", "xt")
     dma("s", T.ut[:], T.u[:], "lu", "", "ut")
-    dma("y", T.wq[:].bitcast(dt.uint8), T.wc[:], "lw", "", "")
+    dma("y", T.wq[:].bitcast(dt.uint8), T.wc[:], "lw", "xt", "")
     dma("y", T.wsc[:], T.ws[:], "lw", "", "wq")
     dma("y", T.vt[:], T.v[:], "lv", "", "vt")
 
@@ -252,7 +256,6 @@ def rank_program(g, core, T, topo):
     row("u0", [[-64, 2], [0, 2]], 112)
     row("a8", [[8, 2], [0, 2]], 0)
     iota(li[:, BL:BL + 8], [[1, 8]], 0, "lbl")
-    iota(li[:, END:END + 8], [[16, 8]], 15, "lend")
     c16, m04 = rw[:, 0:16], rw[:, 80:84]
     names = ["q", "e", "h", "q7", "q3", "q2", "a", "a0", "a1", "a3"]
     col = {k: pc[:, i:i + 1] for i, k in enumerate(names + ["jl", "ju", "b0", "b1", "B0", "B1", "n0", "w", "x1", "x2"])}
@@ -281,7 +284,7 @@ def rank_program(g, core, T, topo):
         late.append(lambda: f(*a))
 
     a1, a2, a3, a4 = tmp[:, 80:88], tmp[:, 88:96], tmp[:, 96:104], tmp[:, 104:112]
-    u1, u2, u3, u4, u5 = tmp[:, 112:116], tmp[:, 116:120], tmp[:, 120:124], tmp[:, 124:128], tmp[:, 128:132]
+    u1, u2, u3, u4 = tmp[:, 112:116], tmp[:, 116:120], tmp[:, 120:124], tmp[:, 124:128]
     aff(XLo, c16, 2.0, col["h"], "c16 pc", "xl")
     aff(XU, c16, 4.0, col["q2"], "c16 pc", "xu")
     aff(col["b0"], col["q"], 16.0, 16.0, "pc", "cb0")
@@ -290,7 +293,6 @@ def rank_program(g, core, T, topo):
     aff(li[:, QL:QL + 16], c16, 0.0, col["q"], "c16 pc", "ql")
     aff(li[:, Q7:Q7 + 8], rw[:, 0:8], 0.0, col["q7"], "c16 pc", "lq7")
     aff(li[:, BL + 8:BL + 12], li[:, XL:XL + 4], 1.0, 8.0, "xl", "bl2")
-    aff(li[:, END + 8:END + 12], li[:, XL:XL + 4], 8.0, 135.0, "xl", "end2")
     aff(li[:, CU:CU + 8], li[:, QL:QL + 8], 16.0, 15.0, "ql", "cu")
     aff(T.mk[:], T.mk[:], 1.0, -1e29, "mk", "mk")
     fill(T.one[:], 256, 1.0, "one")
@@ -310,42 +312,39 @@ def rank_program(g, core, T, topo):
     lt(ts, tmi[:, 48:64], XU, col["q3"], 8.0, A.subtract, A.add, "xu pc", "z2")
     lt(ts, tmi[:, 0:32], tmi[:, 0:32], 15, None, A.bitwise_and, None, "z1", "y1")
     lt(ts, tmi[:, 32:64], tmi[:, 32:64], 7, None, A.bitwise_and, None, "z2", "y2")
+    NEARLY = len(late)
     lt(ts, col["b0"], col["w"], -8.0, col["b0"], A.mult, A.add, "w", "cb0")
     lt(tt, tmp[:, 16:80], tmi[:], rw[:, 16:80], A.add, "y1 y2 bl bu", "yz")
-    NEARLY = len(late)
+    lt(ts, a1, rows["m1"], col["a1"], None, A.not_equal, None, "m1 pc", "a1")
     lt(aff, li[:, BT:BT + 16], tmp[:, 32:48], 8.0, col["jl"], "yz jl", "lbt1")
     lt(aff, li[:, BT + 16:BT + 32], tmp[:, 64:80], 4.0, col["ju"], "yz ju", "lbt2")
     lt(aff, col["b1"], col["h"], -8.0, col["b0"], "pc cb0", "cb1")
-    lt(tt, li[:, LO:LO + 16], XLo, tmp[:, 16:32], A.min, "xl yz", "lo1")
-    lt(tt, li[:, LO + 16:LO + 32], XU, tmp[:, 48:64], A.min, "xu yz", "lo2")
-    lt(tt, li[:, HI:HI + 16], XLo, tmp[:, 16:32], A.max, "xl yz", "hi1")
-    lt(tt, li[:, HI + 16:HI + 32], XU, tmp[:, 48:64], A.max, "xu yz", "hi2")
-    lt(ts, a1, rows["m1"], col["a1"], None, A.not_equal, None, "m1 pc", "a1")
     lt(ts, u2, m04, col["a1"], col["n0"], A.not_equal, A.mult, "m0 pc n0", "u2")
-    lt(ts, a3, rows["m0"], col["a0"], None, A.not_equal, None, "m0 pc", "a3")
+    lt(tt, li[:, LO:LO + 16], XLo, tmp[:, 16:32], A.min, "xl yz", "lo1")
     lt(tt, a1, a1, rows["r37"], A.mult, "r37", "a1")
     lt(tt, u2, u2, rows["u16"], A.mult, "u16", "u2")
     lt(ts, u3, m04, col["a1"], col["n0"], A.is_equal, A.mult, "m0 pc n0", "u3")
     lt(tt, a1, a1, rows["r7"], A.add, "r7", "a1")
     lt(tt, u1, u1, u2, A.add, "u2", "U1")
-    lt(aff, u5, u3, 8.0, 7.0, "u3", "u5")
-    lt(ts, a4, rw[:, 0:8], col["a"], 192.0, A.is_equal, A.mult, "c16 pc", "a4")
+    lt(ts, a3, rows["m0"], col["a0"], None, A.not_equal, None, "m0 pc", "a3")
     lt(tt, a2, rows["r1"], a1, A.subtract, "a1 r1", "a2")
     lt(tt, u4, u4, u1, A.subtract, "U1", "u4")
-    lt(ts, li[:, HS:HS + 8], rw[:, 0:8], col["b0"], col["B0"], A.add, A.mult, "c16 cb0 B0", "hs1")
+    lt(ts, a4, rw[:, 0:8], col["a"], 192.0, A.is_equal, A.mult, "c16 pc", "a4")
     lt(tt, a2, a2, a3, A.mult, "a3", "a2")
     lt(tt, u4, u4, u3, A.mult, "u3", "u4")
     lt(tt, u2, u3, rows["a8"], A.mult, "u3 a8", "u2")
     lt(tt, a1, a1, a2, A.add, "a2", "a1")
     lt(tt, u1, u1, u4, A.add, "u4", "U1")
-    lt(aff, li[:, PE:PE + 8], a1, 16.0, 15.0, "a1", "pe1")
-    lt(ts, li[:, HS + 8:HS + 16], rw[:, 8:16], col["b1"], col["B1"], A.add, A.mult, "c16 cb1 B1", "hs2")
+    lt(tt, li[:, LO + 16:LO + 32], XU, tmp[:, 48:64], A.min, "xu yz", "lo2")
     lt(ts, a2, a1, 16.0, col["q"], A.mult, A.add, "a1 pc", "a2")
     lt(tt, u2, u2, u1, A.add, "U1", "u2")
-    lt(tt, li[:, PE + 8:PE + 12], u1, u5, A.add, "U1 u5", "pe2")
+    lt(tt, li[:, HI:HI + 16], XLo, tmp[:, 16:32], A.max, "xl yz", "hi1")
     lt(tt, li[:, PV:PV + 8], a2, a4, A.max, "a2 a4", "pv1")
     lt(ts, li[:, PV + 8:PV + 12], u2, col["q7"], None, A.add, None, "u2 pc", "pv2")
-    lt(cp, T.lu[:, LO:NL], li[:, LO:NL], "xl lo1 lo2 hi1 hi2 lbt1 lbt2 ql at bl2 end2 cu lq7 hs1 hs2 pe1 pe2 pv1 pv2 lbl lend", "lu")
+    lt(tt, li[:, HI + 16:HI + 32], XU, tmp[:, 48:64], A.max, "xu yz", "hi2")
+    lt(ts, li[:, HS:HS + 8], rw[:, 0:8], col["b0"], col["B0"], A.add, A.mult, "c16 cb0 B0", "hs1")
+    lt(ts, li[:, HS + 8:HS + 16], rw[:, 8:16], col["b1"], col["B1"], A.add, A.mult, "c16 cb1 B1", "hs2")
+    lt(cp, T.lu[:, LO:NL], li[:, LO:NL], "xl lo1 lo2 hi1 hi2 lbt1 lbt2 ql at bl2 cu lq7 hs1 hs2 pv1 pv2 lbl", "lu")
     d0, one = T.d0, T.one
 
     def tables_a():
@@ -359,42 +358,47 @@ def rank_program(g, core, T, topo):
         iota(d0[:, 256:512:4], [[0, 64]], 0, "d0b")
         sel(d0[:, 513:768:8], one[:, 0:32], [[0, 2], [1, 16]], A.is_ge, -1.0, -8, "one", "d0c")
         sel(d0[:, 769:1024:4], one[:, 0:64], [[0, 8], [1, 8]], A.is_ge, -1.0, -4, "one", "d0d")
+
+    def tables_b():
         iota(d0[:, 512:768:8], [[0, 32]], 0, "d0c")
         iota(d0[:, 768:1024:4], [[0, 64]], 0, "d0d")
         iota(d0[:, 513:768:128], [[0, 2]], 1, "d0c")
         iota(d0[:, 769:1024:32], [[0, 8]], 1, "d0d")
-
-    def tables_b():
-        sel(T.tau[:, 128:192], one[:, 0:64], [[0, 8], [1, 8]], A.is_ge, -1.0, -3, "one", "tau2")
-        iota(T.ct[:, 128:192], [[-64, 8], [-1, 8]], 7 - 512, "ct2")
-        sel(T.tau[:, 0:128], one[:, 0:128], [[0, 8], [1, 16]], A.is_ge, -1.0, -7, "one", "tau1")
-        iota(T.ct[:, 0:128], [[-64, 8], [-1, 16]], 15, "ct")
-        sel(T.v0[:, 0:128], T.ones[:, 0:128], [[-1, 8], [1, 8], [0, 2]], A.is_equal, 0.0, 0, "ones", "v0")
+        sel(T.tau[:, 128:192], T.rr[:, 0:64], [[0, 8], [1, 8]], A.is_ge, -0.03125, -3, "rr", "tau2")
+        sel(T.tau[:, 0:128], T.rr[:, 0:128], [[0, 8], [1, 16]], A.is_ge, -0.03125, -7, "rr", "tau1")
+        sel(T.v0[:, 0:128], one[:, 0:128], [[-1, 8], [1, 8], [0, 2]], A.is_equal, 0.0, 0, "one", "v0")
 
     def cells():
-        for o, w, c, k in ((T.kp[:, 0:16], 16, 64.0, "kpa"), (T.kp[:, 208:224], 16, 2000.0, "kpb"), (T.va[:, 192:208], 16, 32.0, "vac"),
-                           (T.vb[:, 128:208], 80, 32.0, "vbc"), (T.v0[:, 128:208], 80, 32.0, "v0c"), (T.yy[:], 192, 0.0, "yy"),
-                           (T.va[:, 128:192], 64, 0.0, "vau"), (T.hh[:, 0:16], 16, 0.0, "hh0"), (T.cum[:, 0:16], 16, 0.0, "cum0"),
+        for o, w, c, k in ((T.cd[:], 192, -0.03125, "cd"), (T.va[:, 192:208], 16, 1.0, "vac"), (T.sg[:], 192, -1.0, "sg"),
+                           (T.vb[:, 128:208], 80, 1.0, "vbc"), (T.v0[:, 128:208], 80, 1.0, "v0c"), (T.zz[:, 0:208], 208, 0.0, "zz"),
+                           (T.cd[:, 0:128:16], 8, -2.5, "cd"), (T.zz[:, 208:224], 16, 5.0, "zc"), (T.dl[:, 192:208], 16, -2.0, "dlc"),
+                           (T.sg[:, 15:128:16], 8, 2.0, "sg"), (T.cd[:, 128:192:8], 8, -2.5, "cd"), (T.k0[:, 0:16], 16, 0.0, "k0c"),
+                           (T.va[:, 128:192], 64, 0.0, "vau"), (T.cum[:, 0:16], 16, 0.0, "cum0"), (T.sg[:, 135:192:8], 8, 2.0, "sg"),
                            (T.cn[:], 16, 0.0, "cn"), (T.fn[:], 16, 0.0, "fn"), (T.ux[:, 0:16], 16, 0.0, "uu0"), (T.dnn[:], 16, 0.0, "dnn")):
             fill(o, w, c, k)
 
-    for f in late[:NEARLY]:
+    fill(T.rr[:, 0:128], 128, 0.03125, "rr")
+    for f in late[:6]:
         f()
     quant(T.uq[:], T.us[:], T.ut[:], "ut", "uq")
     cp(T.ub[:].bitcast(dt.uint32), T.uq[:].bitcast(dt.uint32).indirect(L(UP, 8)), "uq lu0", "ub")
     cp(T.ubs[:], T.us[:].indirect(L(UP, 8)), "uq lu0", "ubs")
     quant(T.xq0[:], T.xs0[:], T.xt[:], "xt", "xq0")
+    for f in late[6:NEARLY]:
+        f()
 
     def E(b):
         return T.eq[:, 128 * b:128 * b + 128], T.es[:, 128 * b:128 * b + 128]
 
+    BANK = ((2, 3, 4, 5), (6, 7, 0, 1))
     for t in range(R):
         s = str(t)
         xq, xs, lq, ls = T["xq" + s], T["xs" + s], T["lq" + s], T["ls" + s]
         sm, oo, hl, bn, on, hn = [T[k + s] for k in ("sm", "oo", "hl", "bn", "on", "hn")]
         side = marks_side(t)
-        mm(0, 256, T.ub[:], T.ubs[:], xq[:], xs[:], "ub ubs xq" + s)
-        mm(1, 256, T.uq[:], T.us[:], xq[:], xs[:], "uq xq" + s)
+        XK = " xq%s xr%s" % (s, s)
+        mm(0, 256, T.ub[:], T.ubs[:], xq[:], xs[:], "ub ubs" + XK)
+        mm(1, 256, T.uq[:], T.us[:], xq[:], xs[:], "uq" + XK)
         send_x(t)
         if t == 0:
             tables_a()
@@ -444,17 +448,13 @@ def rank_program(g, core, T, topo):
         cp(T.pz[:], ri[:, 64:80], "r16", "pz")
         (so, sk), (to, tk) = ((oo, "oo" + s), (on, "on" + s))[::-side]
 
-        def dso(j):
-            if j:
-                tt(T.od[:, 1:16], so[:, 1:16], so[:, 0:15], A.subtract, sk, "od1")
-            else:
-                cp(T.od[:, 0:1], so[:, 0:1], sk, "od0")
+        def dso():
+            tt(T.od[:, 1:16], so[:, 1:16], so[:, 0:15], A.subtract, sk, "od1")
+            cp(T.od[:, 0:1], so[:, 0:1], sk, "od0")
 
-        def dto(j):
-            if j:
-                tt(T.dnn[:, 1:8], to[:, 9:16], to[:, 8:15], A.subtract, "dnn " + tk, "dx1")
-            else:
-                cp(T.dnn[:, 0:1], to[:, 8:9], "dnn " + tk, "dx0")
+        def dto():
+            tt(T.dnn[:, 1:8], to[:, 9:16], to[:, 8:15], A.subtract, "dnn " + tk, "dx1")
+            cp(T.dnn[:, 0:1], to[:, 8:9], "dnn " + tk, "dx0")
 
         def tab_s():
             act(T.tb[:, 0:192], so[:].indirect(L(AT, 12)), "lu " + sk, "tb1")
@@ -465,7 +465,9 @@ def rank_program(g, core, T, topo):
             act(T.ta[:, 256:384], T.dnn[:].indirect(L(Q7, 8)), "lu dx0 dx1", "ta2")
 
         own_d, far_d, own_t, far_t = (dso, dto, tab_s, tab_t) if side < 0 else (dto, dso, tab_t, tab_s)
-        own_d(1), own_d(0)
+        own_d()
+        if t:
+            own_t()
         if t == 0:
             for b in range(4):
                 quant(*E(b), T.et[:, 512 * b:512 * b + 512], "et%d" % b, "eq%d" % b)
@@ -480,8 +482,10 @@ def rank_program(g, core, T, topo):
             act(T.gh[:, 256 * i:256 * i + 256], win(T.dd, i).indirect(L(HI + 16 * (i == 4), 16)), "dd lu", "gh%d" % i, f=F.Abs)
 
         def beat(i):
-            u = 256 * (i == 4)
             tt(T.bb[:, 512 * i:512 * i + 256], win(T.gg, i).indirect(L(LO + 16 * (i == 4), 16)), T.gh[:, 256 * i:256 * i + 256], A.is_le, "gg lu gh%d" % i, "b%d" % i)
+
+        def rsum(i):
+            u = 256 * (i == 4)
             scan(T.bb[:, 512 * i + 256:512 * i + 512], d0[:, u:u + 256], T.bb[:, 512 * i:512 * i + 256], A.mult, A.add, "d0a d0b b%d" % i, "br%d" % i)
 
         def turn(i, q):
@@ -492,90 +496,81 @@ def rank_program(g, core, T, topo):
             u = 512 + 256 * (i == 4)
             scan(T.sc[:, 256 * i:256 * i + 256], d0[:, u:u + 256], T.bt[:, 256 * i:256 * i + 256], A.mult, A.add, "d0c d0d bt_%d" % i, "sc%d" % i)
 
-        hi(4)
-        ts(T.nk[:, 0:192], T.dd[:], -1.0, None, A.mult, None, "dd", "nk")
-        tt(T.gg[:], T.nk[:, 0:192], T.dd[:], A.max, "dd nk", "gg")
-        hi(0), beat(4), hi(1), beat(0), hi(2), beat(1), hi(3), turn(4, "s"), beat(2), turn(0, "s"), beat(3)
-        turn(1, "s"), turn(3, "v"), sums(4), turn(2, "s"), sums(0)
-        tt(T.k0[:, 128:192], T.sc[:, 1027:1280:4], T.tau[:, 128:192], A.mult, "sc4 tau2", "k0b")
-        sums(3), sums(1)
-        kp = T.kp
-        tt(kp[:, 144:208], T.k0[:, 128:192], T.ct[:, 128:192], A.add, "k0b ct2", "kp2")
-        sums(2)
-        tt(T.k0[:, 0:128], T.sc[:, 7:1024:8], T.tau[:, 0:128], A.mult, "sc0 sc1 sc2 sc3 tau1", "k0a")
-        tt(kp[:, 16:144], T.k0[:, 0:128], T.ct[:, 0:128], A.add, "k0a ct", "kp1")
-        KP = "kp1 kp2 kpa kpb lu"
-        aff(T.nk[:, 0:192], kp[:, 16:224].indirect(L(PV, 12)), -1.0, 32.0, KP, "nk")
-        tt(T.dl[:], kp[:, 16:208], kp[:, 15:207], A.subtract, KP, "dl")
-        aff(T.nk[:, 192:384], kp[:, 16:208], -1.0, 32.0, KP, "nk2")
-        for b in range(4):
-            act(T.gt[:, b:1024:4], ps(2 + b, 256, 256), "ps%d" % (2 + b), "gt%d" % b, scale=0.03125)
-        own_t()
-        for b in range(4):
-            act(T.dn[:, 256 * b:256 * b + 256], ps(2 + b, 0, 256), "ps%d" % (2 + b), "dn%d" % b, scale=0.03125)
+        act(T.gg[:], T.dd[:], "dd", "gg", f=F.Abs)
+        hi(4), hi(0), beat(4), hi(1), beat(0), rsum(4), hi(2), beat(1), rsum(0), hi(3), turn(4, "s"), beat(2), rsum(1), turn(0, "s"), beat(3)
+        rsum(2), turn(1, "s"), rsum(3), sums(4), turn(3, "v"), turn(2, "s"), sums(0)
+        tt(T.k0[:, 144:208], T.sc[:, 1027:1280:4], T.tau[:, 128:192], A.mult, "sc4 tau2", "k0b")
+        sums(1), sums(3), sums(2)
+        tt(T.k0[:, 16:144], T.sc[:, 7:1024:8], T.tau[:, 0:128], A.mult, "sc0 sc1 sc2 sc3 tau1", "k0a")
+        tt(T.k1[:], T.k0[:, 16:208], T.k0[:, 15:207], A.subtract, "k0a k0b k0c", "k1")
+        tt(T.dl[:, 0:192], T.k1[:], T.cd[:], A.add, "k1 cd", "dl")
+
+        def unpack(o, bank, a, key):
+            return lambda: act(o, ps(bank, a, 256), "ps%d" % bank, key, scale=0.03125)
+
+        gts = [unpack(T.gt[:, b:1024:4], 2 + b, 256, "gt%d" % b) for b in range(4)]
+        dns = [unpack(T.dn[:, 256 * b:256 * b + 256], 2 + b, 0, "dn%d" % b) for b in range(4)]
+        dps = [unpack(T.dp[:, 256 * b:256 * b + 256], BANK[1][b], 0, "dp%d" % b) for b in range(4)]
+        beside = gts + dns[:2] + dps + dns[2:]
+        zz = T.zz
         for k in range(12):
             src, sn = (T.v0, "v0 v0c") if k == 0 else (T.va, "va vac vau") if k % 2 else (T.vb, "vb vbc")
             dst, dn_ = (T.vb, "vb") if k % 2 else (T.va, "va")
             w, w2 = (128 if k < 8 else 192), (128 if k < 7 else 192)
+            if k < 11:
+                aff(T.rr[:, 0:w2], src[:].indirect(L(PV, w2 // 16)), -8.0, 9.0, "lu " + sn, "rr")
+            if k == 0 and t == 0:
+                own_t()
+            beside[k]()
             scan(T.yy[:, 0:w], T.dl[:, 0:w], src[:, 0:w], A.add, A.max, "dl " + sn, "yy")
             if k == 0:
-                tt(T.cc[:, 0:192], kp[:, 16:224].indirect(L(PE, 12)), T.nk[:, 0:192], A.add, KP + " nk", "cc")
+                tt(T.db[:], T.dl[:, 1:193], T.sg[:], A.mult, "dl dlc sg", "db")
+            scan(zz[:, 15 + w:15:-1], T.db[:, w - 1::-1], T.yy[:, w - 1::-1], A.add, A.max, "db yy", "zz")
             if k == 11:
                 break
-            tt(T.rr[:, 0:w2], T.yy[:].indirect(L(PE, w2 // 16)), T.cc[:, 0:w2], A.is_gt, "yy cc lu", "rr")
-            if k == 2:
-                tt(T.cc[:, 192:384], kp[:, 16:224].indirect(L(END, 12)), T.nk[:, 192:384], A.add, KP + " nk2", "cf")
             if k == 4:
                 quant(T.gq[:], T.gs[:], T.gt[:], "gt0 gt1 gt2 gt3", "gq")
                 for b in range(4):
-                    bank = (6, 7, 0, 1)[b]
-                    mm(bank, 256, *E(b), T.gq[:], T.gs[:], "eq%d gq" % b)
-                    act(T.dp[:, 256 * b:256 * b + 256], ps(bank, 0, 256), "ps%d" % bank, "dp%d" % b, scale=0.03125)
-                for b in range(4):
-                    mm(2 + b, 256, *E(b), xq[:], xs[:], "eq%d xq%s" % (b, s), True, False)
-            if k in (6, 7):
-                far_d(k - 6)
-            if k == 7:
-                far_t()
-            tt(dst[:, 0:w2], src[:].indirect(L(PV, w2 // 16)), T.rr[:, 0:w2], A.mult, "rr lu " + sn, dn_ + (" vau" if k % 2 == 0 and w2 > 128 else ""))
+                    mm(BANK[1][b], 256, *E(b), T.gq[:], T.gs[:], "eq%d gq" % b)
+            tt(dst[:, 0:w2], zz[:, 16:224].indirect(L(PV, w2 // 16)), T.rr[:, 0:w2], A.is_gt, "rr lu zz zc", dn_ + (" vau" if k % 2 == 0 and w2 > 128 else ""))
+        for h in range(2):
+            for b in range(4):
+                mm(BANK[1 - h][b], 128, *E(b), xq[:, 128 - 128 * h:256 - 128 * h], xs[:, 128 - 128 * h:256 - 128 * h], "eq%d" % b + XK, True, False)
         sml, hh, cum, ux = T.sml, T.hh, T.cum, T.ux
-        tt(T.rr[:], T.yy[:].indirect(L(END, 12)), T.cc[:, 192:384], A.is_le, "yy cf lu", "rr")
-        ts(sml[:, 0:8], T.yy[:, 135:192:8], 16.0, None, A.is_lt, None, "yy", "fr")
-        tt(hh[:, 16:208], T.va[:, 0:192], T.rr[:], A.min, "va vau rr", "hh")
+        ts(T.he[:, 0:256], zz[:, 0:208].indirect(L(HS, 16)), 1.0, None, A.is_equal, None, "zz lu", "he")
+        ts(sml[:, 0:8], T.yy[:, 135:192:8], 0.5, None, A.is_lt, None, "yy", "fr")
+        scan(cum[:, 16:272], T.he[:, 0:256], T.he[:, 0:256], A.add, A.max, "he", "cum")
         scan(T.cn[:, 1:9], sml[:, 0:8], sml[:, 0:8], A.add, A.max, "fr cn", "cn1")
-        cp(T.he[:, 0:256], hh[:, 0:208].indirect(L(HS, 16)), "hh hh0 lu", "he")
         act(T.c2[:], T.cn[:].indirect(L(Q7, 8)), "cn1 lu", "c2")
 
-        def free_seats():
-            ts(sml[:, 16:24], T.yy[:, 135:192:8], 16.0, -1.0, A.is_lt, A.mult, "yy", "frn")
-            tt(T.fn[:, 0:8], T.cn[:, 1:9], sml[:, 16:24], A.mult, "cn1 frn fn", "fn1")
-
         def seats(out, key):
+            ts(sml[:, 16:24], T.yy[:, 135:192:8], 0.5, -1.0, A.is_lt, A.mult, "yy", "frn")
+            ts(hh[:, 16:208], zz[:, 16:208], 1.0, None, A.is_equal, None, "zz", "hh")
+            tt(T.fn[:, 0:8], T.cn[:, 1:9], sml[:, 16:24], A.mult, "cn1 frn fn", "fn1")
+            tt(T.mm[:, 0:192], hh[:, 16:208], T.tb[:, 0:192], A.mult, "hh tb1", "mm mm2")
             tt(T.tt[:], T.fn[:].indirect(L(BL, 8)), T.j16[:, 0:128], A.add, "fn1 j16 lu", "tt")
             tt(hh[:, 208:336], cum[:].indirect(L(CU, 8)), T.tt[:], A.is_gt, "cum cum0 tt lu", "hh2")
-            tt(T.mm[:, 0:320], hh[:, 16:336], T.tb[:], A.mult, "hh hh2 tb1 tb2", "mm")
-            scan(T.ss[:, 0:320], T.rm[:, 0:320], T.mm[:, 0:320], A.mult, A.add, "rm mm", "ss")
+            tt(T.mm[:, 192:320], hh[:, 208:336], T.tb[:, 192:320], A.mult, "hh2 tb2", "mm2")
+            scan(T.ss[:, 0:320], T.rm[:, 0:320], T.mm[:, 0:320], A.mult, A.add, "rm mm mm2", "ss")
             tt(T.ai[:, 8:16], T.ss[:, 135:192:8], T.ss[:, 207:320:16], A.add, "ss", "ai2")
             cp(T.ai[:, 0:8], T.ss[:, 15:128:16], "ss", "ai1")
             cp(out, T.ai[:, 0:16], "ai1 ai2", key)
 
         def suitors(out, key):
             tt(ux[:, 16:32], T.i256[:, 1:17], cum[:, 31:272:16], A.subtract, "cum i256", "uu")
+            tt(T.mm[:, 0:128], T.he[:, 0:128], T.ta[:, 0:128], A.mult, "he ta1", "mm mm2")
             tt(sml[:, 32:48], ux[:, 16:32], ux[:, 15:31], A.subtract, "uu uu0", "un")
+            tt(T.mm[:, 128:256], T.he[:, 128:256], T.ta[:, 128:256], A.mult, "he ta1", "mm1")
             tt(ux[:, 32:48], ux[:, 16:32], sml[:, 32:48], A.mult, "uu un", "uv")
             tt(T.he[:, 256:384], ux[:, 32:48].indirect(L(XL, 8)), T.c2[:], A.is_gt, "uv c2 lu", "he2")
-            tt(T.mm[:], T.he[:], T.ta[:], A.mult, "he he2 ta1 ta2", "mm")
-            scan(T.ss[:], T.rm[:, 192:576], T.mm[:], A.mult, A.add, "rm mm", "ss")
+            tt(T.mm[:, 256:384], T.he[:, 256:384], T.ta[:, 256:384], A.mult, "he2 ta2", "mm2")
+            scan(T.ss[:], T.rm[:, 192:576], T.mm[:], A.mult, A.add, "rm mm mm1 mm2", "ss")
             tt(T.ai[:, 16:32], T.ss[:, 15:256:16], T.ss[:, 263:384:8], A.add, "ss", "ai3")
             cp(out, T.ai[:, 16:32], "ai3", key)
 
-        if side < 0:
-            free_seats()
-        scan(cum[:, 16:272], T.he[:, 0:256], T.he[:, 0:256], A.add, A.max, "he", "cum")
         (seats if side < 0 else suitors)(hl[:], "hl" + s)
         send(-side, hl[:], "hl" + s, hn[:], "ah" + s, "rb" + s)
-        if side > 0:
-            free_seats()
+        far_d(), far_t()
         (suitors if side < 0 else seats)(T.al[:], "al")
         (d1, k1), (d2, k2) = ((T.dn, "dn"), (T.dp, "dp"))[::-side]
         for b in range(4):
@@ -590,33 +585,41 @@ def rank_program(g, core, T, topo):
                "%s%d vg%d hn%s" % (k2, b, b, s), "zp%d" % b)
             if b < 3:
                 act(T.zt[:, b:1024:4], T.zp[:, 256 * b:256 * b + 256].indirect(T.pz[:]), "pz zp%d" % b, "zt%d" % b)
-        cp(T.zt[:, 3:1024:4], T.zp[:, 768:1024].indirect(T.pz[:]), "pz zp3", "zt3")
         if t == R - 1:
             act(T.wj[:], T.ab[:].indirect(T.pz[:]), "ab pz", "wj")
             for k in range(8):
                 dma("y", T.ol[k:k + 1, :], T.wj[16 * k:16 * k + 1, :], "sty", "wj", "")
-        quant(T.zq[:], T.zs[:], T.zt[:], "zt0 zt1 zt2 zt3", "zq")
-        for b in (0, 2, 1, 3):
-            mm(2 + b, 256, T.wq[:, 128 * b:128 * b + 128], T.wsc[:, 128 * b:128 * b + 128], T.zq[:], T.zs[:], "wq zq", False, True)
-        for b in (0, 2, 1, 3):
-            if b < 2:
-                act(T.xn[:, b:1024:4], ps(2 + b, 0, 256), "ps%d" % (2 + b), "xn%d" % b, scale=0.03125)
-            else:
-                ts(T.xn[:, b:1024:4], ps(2 + b, 0, 256), 0.03125, None, A.mult, None, "ps%d" % (2 + b), "xn%d" % b)
         s2 = str(t + 1)
-        quant(T["xq" + s2][:], T["xs" + s2][:], T.xn[:], "xn0 xn1 xn2 xn3", "xq" + s2)
+        for h in range(2):
+            a = 128 * h
+            cp(T.zt[:, 4 * a + 3:4 * a + 512:4], T.zp[:, 768:1024].indirect(T.pz[:, 8 * h:8 * h + 8]), "pz zp3", "zu%d" % h)
+            quant(T.zq[:, a:a + 128], T.zs[:, a:a + 128], T.zt[:, 4 * a:4 * a + 512], "zt0 zt1 zt2 zu%d" % h, "zq%d" % h)
+            for b in range(4):
+                mm(BANK[h][b], 128, T.wq[:, 128 * b:128 * b + 128], T.wsc[:, 128 * b:128 * b + 128], T.zq[:, a:a + 128], T.zs[:, a:a + 128],
+                   "wq zq%d" % h, False, True)
+        for h in range(2):
+            a = 128 * h
+            for b in range(4):
+                o, bank, key = T.xn[:, 4 * a + b:4 * a + 512:4], BANK[h][b], "xn%d%d" % (h, b)
+                if b % 2 == 0:
+                    act(o, ps(bank, 0, 128), "ps%d" % bank, key, scale=0.03125)
+                else:
+                    ts(o, ps(bank, 0, 128), 0.03125, None, A.mult, None, "ps%d" % bank, key)
+            quant(T["xq" + s2][:, a:a + 128], T["xs" + s2][:, a:a + 128], T.xn[:, 4 * a:4 * a + 512],
+                  " ".join("xn%d%d" % (h, b) for b in range(4)), ("xq", "xr")[h] + s2)
 
     s = str(R)
     xq, xs = T["xq" + s], T["xs" + s]
-    mm(6, 128, T.vq[:], T.vs[:], xq[:, 0:128], xs[:, 0:128], "vq xq" + s)
-    mm(7, 128, T.vq[:], T.vs[:], xq[:, 128:256], xs[:, 128:256], "vq xq" + s)
-    dma("y", T.oc[:], xq[:].bitcast(dt.uint8), "sty", "xq" + s, "")
-    cp(T.yo[:, 0:128], ps(6, 0, 128), "ps6", "yo1")
-    dma("s", T.osc[0:4, :], xs[0:4, :], "sts", "xq" + s, "")
-    act(T.yo[:, 128:256], ps(7, 0, 128), "ps7", "yo2")
+    XK = "xq%s xr%s" % (s, s)
+    mm(2, 128, T.vq[:], T.vs[:], xq[:, 0:128], xs[:, 0:128], "vq xq" + s)
+    mm(3, 128, T.vq[:], T.vs[:], xq[:, 128:256], xs[:, 128:256], "vq xr" + s)
+    act(T.yo[:, 0:128], ps(2, 0, 128), "ps2", "yo1")
+    dma("y", T.oc[:], xq[:].bitcast(dt.uint8), "sty", XK, "")
+    cp(T.yo[:, 128:256], ps(3, 0, 128), "ps3", "yo2")
+    dma("s", T.osc[0:4, :], xs[0:4, :], "sts", XK, "")
     dma("s", T.y[:], T.yo[:], "sts", "yo1 yo2", "")
     for k in range(1, 4):
-        dma("y", T.osc[4 * k:4 * k + 4, :], xs[32 * k:32 * k + 4, :], "sty", "xq" + s, "")
+        dma("y", T.osc[4 * k:4 * k + 4, :], xs[32 * k:32 * k + 4, :], "sty", XK, "")
     for q in POOL:
         for e in cnt[q][-POOL[q]:]:
             need("g", e)

@@ -3,41 +3,45 @@ from concourse.mybir import dt, AluOpType as A, ActivationFunctionType as F
 
 R, C = 2, 256
 X4, U8, BF, F32, I32, U16 = "float8_e4m3fn_x4", "uint8", "bfloat16", "float32", "int32", "uint16"
-UP, EQ, SEL, LO, HI, BT, QL, AT, BL, PV, CU, HS, XL, Q7, NL = 0, 8, 24, 26, 58, 90, 122, 130, 142, 154, 166, 174, 190, 206, 214
+UP, SEL, AT, XL, YL, LO, HI, TI, TX, PV, PN, PU, VA, CU, C8, Q7, UE, HB, TB, NL = \
+    0, 8, 12, 20, 36, 52, 68, 84, 116, 132, 140, 144, 148, 172, 180, 188, 196, 204, 220, 236
+WHO = "sssssbbbvvvvvvvv"
+NS = WHO.index("v")
 SCRATCH = {}
 for _n, _w, _d in [
     ("xt", 1024, BF), ("ut", 512, BF), ("vt", 512, BF), ("uq", 128, X4), ("us", 128, U8), ("ub", 128, X4), ("ubs", 128, U8),
     ("vq", 128, X4), ("vs", 128, U8), ("wq", 512, X4), ("wsc", 512, U8), ("eq", 512, X4), ("es", 512, U8),
-    ("ones", 576, BF), ("one", 256, BF), ("fe", 528, BF), ("et", 2048, BF),
+    ("ones", 528, BF), ("one", 256, BF), ("fe", 528, BF),
     ("xq0", 256, X4), ("xs0", 256, U8), ("xq1", 256, X4), ("xs1", 256, U8), ("xq2", 256, X4), ("xs2", 256, U8),
-    ("lq0", 512, X4), ("ls0", 512, U8), ("lq1", 512, X4), ("ls1", 512, U8),
+    ("nq0", 256, X4), ("ns0", 256, U8), ("nq1", 256, X4), ("ns1", 256, U8),
+    ("pq0", 256, X4), ("pr0", 256, U8), ("pq1", 256, X4), ("pr1", 256, U8),
     ("rq0", 256, X4), ("rs0", 256, U8), ("rq1", 256, X4), ("rs1", 256, U8),
     ("gt", 1024, BF), ("gq", 256, X4), ("gs", 256, U8), ("zt", 1024, BF), ("zq", 256, X4), ("zs", 256, U8), ("xn", 1024, BF),
-    ("dn", 1024, BF), ("dp", 1024, BF), ("vg", 1024, BF), ("zp", 1024, BF),
-    ("li", NL + 2, F32), ("lu", NL + 2, U16), ("pi", 16, I32), ("pc", 32, F32), ("rw", 192, F32), ("tmp", 192, F32), ("tmi", 64, I32),
-    ("j16", 256, F32), ("i256", 256, BF), ("eye", 256, F32), ("mk", 256, F32), ("rm", 576, BF), ("d0", 1024, BF),
-    ("cd", 192, BF), ("tau", 192, BF), ("v0", 208, BF), ("va", 208, BF), ("vb", 208, BF),
-    ("t1", 256, F32), ("scn", 256, F32), ("m", 4096, BF), ("acc", 16, F32), ("bm", 256, F32), ("ec", 256, BF), ("es2", 256, BF),
-    ("e32", 16, F32), ("ri", 96, I32), ("pt", 16, U16), ("pz", 16, U16), ("pm", 256, F32), ("sw", 512, F32), ("tr", 512, F32),
-    ("ow", 512, BF), ("otr", 512, BF),
+    ("dn", 1024, BF), ("dp", 1024, BF), ("vg", 1024, BF), ("zp", 1024, BF), ("vc", 512, BF),
+    ("li", NL + 4, F32), ("lu", NL + 4, U16), ("pi", 16, I32), ("pc", 64, F32), ("rw", 128, F32), ("tmp", 224, F32), ("tmi", 128, I32),
+    ("j16", 256, BF), ("px", 256, F32), ("eye", 256, F32), ("ne", 256, BF), ("rm", 256, BF), ("r8", 256, BF), ("c12", 256, BF),
+    ("di", 256, BF), ("df", 256, BF), ("sg", 192, BF), ("v0", 144, BF), ("va", 208, BF), ("vb", 208, BF),
+    ("t1", 256, F32), ("t2", 256, F32), ("scn", 256, F32), ("row", 512, F32), ("m", 4096, BF), ("mo", 256 * (16 - NS), BF),
+    ("acc", 16, F32), ("ec", 256, BF), ("es2", 256, BF), ("e32", 16, F32), ("ri", 112, I32), ("pt", 16, U16), ("pz", 16, U16), ("pm", 256, F32), ("sw", 512, F32),
+    ("tr", 512, F32),
     ("sm0", 16, F32), ("sm1", 16, F32), ("oo0", 16, BF), ("oo1", 16, BF), ("hl0", 16, U16), ("hl1", 16, U16),
     ("bn0", 16, F32), ("bn1", 16, F32), ("on0", 16, BF), ("on1", 16, BF), ("hn0", 16, U16), ("hn1", 16, U16),
-    ("at", 192, F32), ("dd", 192, F32), ("gg", 192, F32), ("gh", 1280, F32), ("bb", 2560, BF), ("bt", 1280, BF), ("sc", 1280, BF),
-    ("k0", 208, BF), ("k1", 192, BF), ("dl", 208, BF), ("db", 192, BF), ("sg", 192, BF), ("yy", 192, BF), ("zz", 224, BF), ("rr", 192, BF),
-    ("hh", 336, BF), ("he", 384, BF), ("cum", 272, BF), ("sml", 128, BF), ("cn", 16, BF), ("fn", 16, BF), ("tt", 128, BF), ("ux", 48, BF),
-    ("ta", 384, BF), ("tb", 320, BF), ("dnn", 16, BF), ("od", 16, BF), ("mm", 384, BF), ("ss", 384, BF), ("ai", 32, I32), ("al", 16, U16),
-    ("c2", 128, BF), ("ab", 256, BF), ("wj", 256, F32), ("yo", 256, F32),
+    ("at", 192, F32), ("dd", 256, F32), ("gg", 192, F32), ("gh", 1280, F32), ("bb", 1328, BF), ("bt", 2048, BF), ("sc", 2576, BF),
+    ("kn", 128, BF), ("dl", 304, BF), ("db", 256, BF), ("yy", 192, BF), ("zz", 224, BF), ("r0", 64, BF), ("rr", 208, BF),
+    ("na", 384, BF), ("nb", 256, BF), ("val", 400, BF), ("da", 384, BF), ("dts", 32, BF), ("dz", 384, BF), ("cum", 272, BF),
+    ("sml", 48, BF), ("fb", 128, BF), ("c2", 128, BF), ("n2", 128, BF), ("ss", 768, BF), ("al", 16, U16),
+    ("ab", 256, BF), ("wj", 256, F32), ("yo", 256, F32),
 ]:
     SCRATCH[_n] = ("sbuf", [128, _w], _d)
 SCRATCH["ps"] = ("psum", [128, 4096], F32)
 POOL = {"v": 14, "s": 10, "t": 8, "g": 6}
-SEMAPHORES = [q + str(i) for q in POOL for i in range(POOL[q])] + ["lx", "lu", "lv", "lw", "loc", "sty", "sts"] + \
-    [n + str(t) for t in range(R) for n in ("aq", "ab", "ao", "ah", "rq", "rs", "rb", "ro")]
+SEMAPHORES = [q + str(i) for q in POOL for i in range(POOL[q])] + ["lx", "lu", "lv", "lw", "lp", "loc", "sty", "sts"] + \
+    [n + str(t) for t in range(R) for n in ("an", "ap", "ab", "ao", "ah", "rq", "rs", "rb", "ro")]
 
 
-def relay_of(c, d, T, topo):
+def relays_of(c, d, T, topo):
     ok = [e for e in topo.cores_of(c) if T.rank_of(e) is None and topo.may_write(e, d)]
-    return sorted(ok, key=lambda e: topo.die(e) != topo.die(c))[0]
+    return sorted(ok, key=lambda e: topo.die(e) != topo.die(c))[:2]
 
 
 def bits(es):
@@ -48,28 +52,34 @@ def marks_side(t):
     return 1 if t % 2 else -1
 
 
+def landing(T, side, s):
+    return (T["pq" + s], T["pr" + s], "ap" + s) if side == 1 else (T["nq" + s], T["ns" + s], "an" + s)
+
+
 def hand_on(g, core, T, topo):
     n = len(T.cores)
     for r in range(n):
         for side in (1, -1):
             c, d = T.cores[r], T.cores[(r + side) % n]
-            if topo.may_write(c, d) or relay_of(c, d, T, topo) != core:
+            if topo.may_write(c, d) or core not in relays_of(c, d, T, topo):
                 continue
             rid, pid = topo.addr(d, core)
             mask, k = topo.mask(core, d), len(topo.engines(core, d))
-            a = 256 if side == 1 else 0
             sent = 0
             for t in range(R):
                 s = str(t)
-                msgs = [("rq", T["lq" + s][:, a:a + 256].bitcast(dt.uint8), T["rq" + s][:].bitcast(dt.uint8), "aq"),
-                        ("rs", T["ls" + s][:, a:a + 256], T["rs" + s][:], "aq")]
-                if side != marks_side(t):
-                    msgs += [("rb", T["hn" + s][:], T["hn" + s][:], "ah")]
+                q, sc, far = landing(T, side, s)
+                if core == relays_of(c, d, T, topo)[0]:
+                    msgs = [("rq", q[:].bitcast(dt.uint8), T["rq" + s][:].bitcast(dt.uint8), far)]
                 else:
-                    msgs += [("rb", T["bn" + s][:], T["bn" + s][:], "ab"), ("ro", T["on" + s][:], T["on" + s][:], "ao")]
+                    msgs = [("rs", sc[:], T["rs" + s][:], far)]
+                    if side != marks_side(t):
+                        msgs += [("rb", T["hn" + s][:], T["hn" + s][:], "ah" + s)]
+                    else:
+                        msgs += [("rb", T["bn" + s][:], T["bn" + s][:], "ab" + s), ("ro", T["on" + s][:], T["on" + s][:], "ao" + s)]
                 for w, o, i, far in msgs:
                     g.wait_ge(T.sem[w + s], 8 if w in ("rq", "rs") else len(topo.engines(c, core)))
-                    g.remote_dma(o, i, T.sem[far + s], T.sem.loc, pid, rid, mask)
+                    g.remote_dma(o, i, T.sem[far], T.sem.loc, pid, rid, mask)
                     sent += k
             g.wait_ge(T.sem.loc, sent)
 
@@ -172,51 +182,68 @@ def rank_program(g, core, T, topo):
     def mm(bank, w, l, ls, r, rs, rd, start=True, stop=True):
         op("t", lambda: P.matmul_mx(T.ps[:, 512 * bank:512 * bank + w], l, ls, r, rs, start, stop), rd, "ps%d" % bank)
 
+    def scaled(q, o, i, rd, wr):
+        if q == "s":
+            act(o, i, rd, wr, scale=0.03125)
+        else:
+            ts(o, i, 0.03125, None, A.mult, None, rd, wr)
+
+    def of(f, *a):
+        return lambda: f(*a)
+
+    def run(fs):
+        for f in fs:
+            f()
+
     def L(a, w):
         return T.lu[:, a:a + w]
 
     def ps(b, a, w):
         return T.ps[:, 512 * b + a:512 * b + a + w]
 
+    def E(b):
+        return T.eq[:, 128 * b:128 * b + 128], T.es[:, 128 * b:128 * b + 128]
+
     way = {}
     for side in (1, -1):
         d = T.cores[(rank + side) % n]
         direct = topo.may_write(core, d)
-        to = d if direct else relay_of(core, d, T, topo)
-        es = topo.engines(core, to)
-        rid, pid = topo.addr(to, core)
-        way[side] = (direct, rid, pid, bits(es[:8] if direct else es[-8:]), es)
+        way[side] = (direct, [d, d] if direct else relays_of(core, d, T, topo))
     sent = [0]
 
     def send_x(t):
         s = str(t)
         deps("g", ["xq" + s, "xr" + s], [])
-        for k, (src, far, rel) in enumerate((("xq", "lq", "rq"), ("xs", "ls", "rs"))):
+        for k, src, rel in ((1, "xs", "rs"), (0, "xq", "rq")):
             tr = []
             for side in (1, -1):
-                direct, rid, pid, mask, es = way[side]
-                a = 256 if side == 1 else 0
-                i, o = T[src + s][:], (T[far + s][:, a:a + 256] if direct else T[rel + s][:])
+                direct, to = way[side]
+                es = topo.engines(core, to[k])
+                rid, pid = topo.addr(to[k], core)
+                far = landing(T, side, s)
+                i, o = T[src + s][:], (far[k] if direct else T[rel + s])[:]
                 if k == 0:
                     i, o = i.bitcast(dt.uint8), o.bitcast(dt.uint8)
-                tr.append(RemoteDMATransfer(dst_ids=[DstId(rid=rid, pnc=pid)], dma_engine_mask=mask,
-                                            remote_sem=T.sem[("aq" if direct else rel) + s], src=i, dst=o))
+                tr.append(RemoteDMATransfer(dst_ids=[DstId(rid=rid, pnc=pid)], dma_engine_mask=bits(es[:8] if direct else es[-8:]),
+                                            remote_sem=T.sem[far[2] if direct else rel + s], src=i, dst=o))
             g.remote_dma_fused(tr, local_sem=T.sem.loc)
             sent[0] += 16
 
     def send(side, src, key, far, sem, rel):
-        direct, rid, pid, mask, es = way[side]
-        deps("g", [key], [])
-        g.remote_dma(far, src, T.sem[sem if direct else rel], T.sem.loc, pid, rid, bits(es))
-        sent[0] += len(es)
+        direct, to = way[side]
+        rid, pid = topo.addr(to[1], core)
+        deps("g", key.split(), [])
+        g.remote_dma(far, src, T.sem[sem if direct else rel], T.sem.loc, pid, rid, topo.mask(core, to[1]))
+        sent[0] += len(topo.engines(core, to[1]))
 
     def brought(side):
         c = T.cores[(rank + side) % n]
-        return len(topo.engines(c if topo.may_write(c, core) else relay_of(c, core, T, topo), core))
+        return len(topo.engines(c if topo.may_write(c, core) else relays_of(c, core, T, topo)[1], core))
 
     for t in range(R):
         s = str(t)
-        arrives("lq" + s, "aq" + s, 32)
+        arrives("nq" + s, "an" + s, 16)
+        arrives("pq" + s, "ap" + s, 16)
         arrives("bn" + s, "ab" + s, brought(-marks_side(t)))
         arrives("on" + s, "ao" + s, brought(-marks_side(t)))
         arrives("hn" + s, "ah" + s, brought(marks_side(t)))
@@ -227,399 +254,565 @@ def rank_program(g, core, T, topo):
     dma("y", T.wsc[:], T.ws[:], "lw", "", "wq")
     dma("y", T.vt[:], T.v[:], "lv", "", "vt")
 
-    li, rw, tmp, tmi, pc, pi = T.li, T.rw, T.tmp, T.tmi, T.pc, T.pi
+    li, rw, tmp, tmi, pc, pi, one = T.li, T.rw, T.tmp, T.tmi, T.pc, T.pi, T.one
+    c16, n23, m32, bu, r82, rx = rw[:, 0:16], rw[:, 16:48], rw[:, 48:80], rw[:, 80:96], rw[:, 96:112], rw[:, 112:128]
+    eight = rw[:, 100:104]
     op("g", lambda: g.iota(pi[:, 0:1], [[0, 1]], 0, 1), "", "p")
     iota(li[:, UP:UP + 8], [[16, 8]], 0, "lup")
-    iota(li[:, EQ:EQ + 16], [[16, 16]], 15, "leq")
-    rows = {}
-    at = [0]
-
-    def row(name, pat, base):
-        w = 1
-        for a, b in pat:
-            w *= b
-        rows[name] = rw[:, at[0]:at[0] + w]
-        iota(rows[name], pat, base, name)
-        at[0] += w
-
-    row("c16", [[1, 16]], 0)
     iota(T.j16[:], [[0, 16], [1, 16]], 0, "j16")
-    row("bl", [[0, 2], [16, 2], [0, 8]], 0)
-    row("bu", [[0, 2], [8, 8], [0, 2]], 0)
-    row("m0", [[0, 4], [1, 2]], 0)
-    row("m1", [[0, 2], [1, 2], [0, 2]], 0)
-    row("r1", [[2, 4], [-1, 2]], 1)
-    row("r7", [[-1, 8]], 7)
-    row("r37", [[8, 2], [0, 4]], -4)
-    row("u1", [[16, 4]], 136)
-    row("u16", [[0, 2], [-32, 2]], 16)
-    row("u0", [[-64, 2], [0, 2]], 112)
-    row("a8", [[8, 2], [0, 2]], 0)
-    iota(li[:, BL:BL + 8], [[1, 8]], 0, "lbl")
-    c16, m04 = rw[:, 0:16], rw[:, 80:84]
-    names = ["q", "e", "h", "q7", "q3", "q2", "a", "a0", "a1", "a3"]
-    col = {k: pc[:, i:i + 1] for i, k in enumerate(names + ["jl", "ju", "b0", "b1", "B0", "B1", "n0", "w", "x1", "x2"])}
-    sh = {"q": (0, 15), "e": (0, 16), "h": (3, 1), "q7": (0, 7), "q3": (0, 3), "q2": (2, 3), "a": (1, 7), "a0": (1, 1), "a1": (2, 1), "a3": (1, 3)}
+    iota(c16, [[1, 16]], 0, "c16")
+    op("g", lambda: g.iota(tmi[:, 48:56], [[1, 8]], 0, 0), "", "mi1")
+    iota(r82, [[8, 4], [0, 4]], 0, "r82")
+    iota(n23, [[0, 8], [-2, 4]], 8, "n23")
+    iota(rx, [[64, 4], [2, 4]], 0, "rx")
+    iota(bu, [[8, 8], [0, 2]], 0, "bu")
+    iota(T.px[:], [[1, 256]], 0, "px")
+    iota(m32, [[32, 8], [0, 4]], -1, "m32")
+    sh = {"q": (0, 15), "e": (0, 16), "h": (3, 1), "q7": (0, 7), "q3": (0, 3), "q2": (2, 3), "q1": (1, 7), "o": (0, 1), "b1": (1, 1), "b2": (2, 1)}
+    col = {}
+
+    def cl(k):
+        return col.setdefault(k, pc[:, len(col):len(col) + 1])
+
+    def arg(x):
+        return cl(x) if x in col else x
+
+    def lin(q, k, a, s1, s2, o0=A.mult, o1=A.add):
+        rd = "pq pc %s %s %s" % (a, s1, s2)
+        if q == "s":
+            aff(cl(k), cl(a), arg(s1), arg(s2), rd, k)
+        else:
+            ts(cl(k), cl(a), arg(s1), arg(s2), o0, o1, rd, k)
+
+    def flat(a, b, step, row, s1, s2, wr, q="s"):
+        rd = "one r82 c16 n23 xl pq pc %s %s" % (s1, s2)
+        if q == "s":
+            aff(li[:, a:b:step], row, arg(s1), arg(s2), rd, wr)
+        else:
+            ts(li[:, a:b:step], row, arg(s1), arg(s2), A.mult, A.add, rd, wr)
+
+    def digits(a, b, wr):
+        for i, k in list(enumerate(sh))[a:b]:
+            ts(pi[:, i + 1:i + 2], pi[:, 0:1], sh[k][0], sh[k][1], A.logical_shift_right, A.bitwise_and, "p", "pi" + k)
+            cl(k)
+        cp(pc[:, a:b], pi[:, a + 1:b + 1], " ".join("pi" + k for k in list(sh)[a:b]), wr)
 
     ms(T.ones[:], 32.0, "ones")
-    for i, k in enumerate(names):
-        ts(pi[:, i + 1:i + 2], pi[:, 0:1], sh[k][0], sh[k][1], A.logical_shift_right, A.bitwise_and, "p", "pi" + k)
-    ms(li[:, SEL + 1:SEL + 2], 0.0, "ls1")
-    cp(pc[:, 0:10], pi[:, 1:11], " ".join("pi" + k for k in names), "pc")
-    fill(T.rm[:], 576, 1.0, "rm")
-    for a, b, c in ((0, 128, 16), (128, 192, 8), (192, 448, 16), (448, 576, 8)):
-        fill(T.rm[:, a:b:c], (b - a) // c, 0.0, "rm")
-    ts(li[:, SEL:SEL + 1], col["q"], 32.0, col["e"], A.mult, A.add, "pc", "ls0")
-    ts(col["jl"], col["q7"], 0.0, 264.0, A.is_equal, A.mult, "pc", "jl")
-    ts(li[:, SEL:SEL + 1], li[:, SEL:SEL + 1], 1.0, None, A.add, None, "ls0", "ls0")
-    ts(col["ju"], col["q3"], 0.0, 260.0, A.is_equal, A.mult, "pc", "ju")
-    cp(T.lu[:, 0:LO], li[:, 0:LO], "lup leq ls0 ls1", "lu0")
-    ts(T.eye[:], T.j16[:], col["q"], None, A.is_equal, None, "j16 pc", "eye")
-    ts(T.mk[:], T.j16[:], col["q"], 2e29, A.is_ge, A.mult, "j16 pc", "mk")
-
-    late = []
-    XLo, XU = li[:, XL:XL + 16], tmp[:, 0:16]
-
-    def lt(f, *a):
-        late.append(lambda: f(*a))
-
-    a1, a2, a3, a4 = tmp[:, 80:88], tmp[:, 88:96], tmp[:, 96:104], tmp[:, 104:112]
-    u1, u2, u3, u4 = tmp[:, 112:116], tmp[:, 116:120], tmp[:, 120:124], tmp[:, 124:128]
-    aff(XLo, c16, 2.0, col["h"], "c16 pc", "xl")
-    aff(XU, c16, 4.0, col["q2"], "c16 pc", "xu")
-    aff(col["b0"], col["q"], 16.0, 16.0, "pc", "cb0")
-    aff(col["x1"], col["a3"], -16.0, 0.0, "pc", "x1")
-    aff(col["x2"], col["h"], -8.0, 0.0, "pc", "x2")
-    aff(li[:, QL:QL + 16], c16, 0.0, col["q"], "c16 pc", "ql")
-    aff(li[:, Q7:Q7 + 8], rw[:, 0:8], 0.0, col["q7"], "c16 pc", "lq7")
-    aff(li[:, BL + 8:BL + 12], li[:, XL:XL + 4], 1.0, 8.0, "xl", "bl2")
-    aff(li[:, CU:CU + 8], li[:, QL:QL + 8], 16.0, 15.0, "ql", "cu")
-    aff(T.mk[:], T.mk[:], 1.0, -1e29, "mk", "mk")
-    fill(T.one[:], 256, 1.0, "one")
-    aff(li[:, AT + 8:AT + 12], rows["a8"], 1.0, col["q7"], "a8 pc", "at")
-    aff(u1, rows["u1"], 1.0, col["x2"], "x2 u1", "U1")
-    aff(u4, rows["u0"], 1.0, col["x1"], "u0 x1", "u4")
+    fill(T.rm[:], 256, 1.0, "rm")
+    fill(one[:], 256, 1.0, "one")
+    fill(T.rm[:, 0:256:16], 16, 0.0, "rm")
+    digits(0, 2, "pq")
+    cp(L(UP, 8), li[:, UP:UP + 8], "lup", "lu0")
+    digits(2, 10, "pc")
+    ts(T.eye[:], T.j16[:], cl("q"), None, A.is_equal, None, "j16 pq", "eye")
+    ms(li[:, SEL:SEL + 4], 0.0, "ls")
+    lin("v", "u", "q2", 1.0, 1.0, A.is_equal, A.mult)
+    lin("v", "q=3", "q", 3.0, 1.0, A.is_equal, A.mult)
+    lin("v", "w129", "q2", 0.0, 129.0, A.is_equal, A.mult)
+    lin("v", "vd", "q2", "q1", "o", A.subtract, A.mult)
     fill(T.sw[:], 512, 0.0, "sw")
-    lt(ts, col["jl"], col["jl"], col["q7"], -1.0, A.add, A.add, "pc jl", "jl")
-    lt(ts, col["ju"], col["ju"], col["q3"], -1.0, A.add, A.add, "pc ju", "ju")
-    lt(tt, col["w"], col["h"], col["q7"], A.mult, "pc", "w")
-    lt(ts, col["B0"], col["q2"], 3.0, None, A.not_equal, None, "pc", "B0")
-    lt(ts, col["B1"], col["q2"], 2.0, None, A.not_equal, None, "pc", "B1")
-    lt(ts, col["n0"], col["a0"], col["h"], None, A.is_equal, None, "pc", "n0")
-    lt(ts, tmi[:, 0:16], XLo, col["q7"], 1.0, A.add, A.add, "xl pc", "y1")
-    lt(ts, tmi[:, 16:32], XLo, col["q7"], 16.0, A.subtract, A.add, "xl pc", "z1")
-    lt(ts, tmi[:, 32:48], XU, col["q3"], 1.0, A.add, A.add, "xu pc", "y2")
-    lt(ts, tmi[:, 48:64], XU, col["q3"], 8.0, A.subtract, A.add, "xu pc", "z2")
-    lt(ts, tmi[:, 0:32], tmi[:, 0:32], 15, None, A.bitwise_and, None, "z1", "y1")
-    lt(ts, tmi[:, 32:64], tmi[:, 32:64], 7, None, A.bitwise_and, None, "z2", "y2")
-    NEARLY = len(late)
-    lt(ts, col["b0"], col["w"], -8.0, col["b0"], A.mult, A.add, "w", "cb0")
-    lt(tt, tmp[:, 16:80], tmi[:], rw[:, 16:80], A.add, "y1 y2 bl bu", "yz")
-    lt(ts, a1, rows["m1"], col["a1"], None, A.not_equal, None, "m1 pc", "a1")
-    lt(aff, li[:, BT:BT + 16], tmp[:, 32:48], 8.0, col["jl"], "yz jl", "lbt1")
-    lt(aff, li[:, BT + 16:BT + 32], tmp[:, 64:80], 4.0, col["ju"], "yz ju", "lbt2")
-    lt(aff, col["b1"], col["h"], -8.0, col["b0"], "pc cb0", "cb1")
-    lt(ts, u2, m04, col["a1"], col["n0"], A.not_equal, A.mult, "m0 pc n0", "u2")
-    lt(tt, li[:, LO:LO + 16], XLo, tmp[:, 16:32], A.min, "xl yz", "lo1")
-    lt(tt, a1, a1, rows["r37"], A.mult, "r37", "a1")
-    lt(tt, u2, u2, rows["u16"], A.mult, "u16", "u2")
-    lt(ts, u3, m04, col["a1"], col["n0"], A.is_equal, A.mult, "m0 pc n0", "u3")
-    lt(tt, a1, a1, rows["r7"], A.add, "r7", "a1")
-    lt(tt, u1, u1, u2, A.add, "u2", "U1")
-    lt(ts, a3, rows["m0"], col["a0"], None, A.not_equal, None, "m0 pc", "a3")
-    lt(tt, a2, rows["r1"], a1, A.subtract, "a1 r1", "a2")
-    lt(tt, u4, u4, u1, A.subtract, "U1", "u4")
-    lt(ts, a4, rw[:, 0:8], col["a"], 192.0, A.is_equal, A.mult, "c16 pc", "a4")
-    lt(tt, a2, a2, a3, A.mult, "a3", "a2")
-    lt(tt, u4, u4, u3, A.mult, "u3", "u4")
-    lt(tt, u2, u3, rows["a8"], A.mult, "u3 a8", "u2")
-    lt(tt, a1, a1, a2, A.add, "a2", "a1")
-    lt(tt, u1, u1, u4, A.add, "u4", "U1")
-    lt(tt, li[:, LO + 16:LO + 32], XU, tmp[:, 48:64], A.min, "xu yz", "lo2")
-    lt(ts, a2, a1, 16.0, col["q"], A.mult, A.add, "a1 pc", "a2")
-    lt(tt, u2, u2, u1, A.add, "U1", "u2")
-    lt(tt, li[:, HI:HI + 16], XLo, tmp[:, 16:32], A.max, "xl yz", "hi1")
-    lt(tt, li[:, PV:PV + 8], a2, a4, A.max, "a2 a4", "pv1")
-    lt(ts, li[:, PV + 8:PV + 12], u2, col["q7"], None, A.add, None, "u2 pc", "pv2")
-    lt(tt, li[:, HI + 16:HI + 32], XU, tmp[:, 48:64], A.max, "xu yz", "hi2")
-    lt(ts, li[:, HS:HS + 8], rw[:, 0:8], col["b0"], col["B0"], A.add, A.mult, "c16 cb0 B0", "hs1")
-    lt(ts, li[:, HS + 8:HS + 16], rw[:, 8:16], col["b1"], col["B1"], A.add, A.mult, "c16 cb1 B1", "hs2")
-    lt(cp, T.lu[:, LO:NL], li[:, LO:NL], "xl lo1 lo2 hi1 hi2 lbt1 lbt2 ql at bl2 cu lq7 hs1 hs2 pv1 pv2 lbl", "lu")
-    d0, one = T.d0, T.one
-
-    def tables_a():
-        iota(T.i256[:], [[1, 256]], 0, "i256")
-        sel(T.fe[:], T.ones[:, 0:528], [[-1, 528]], A.is_equal, 0.0, 3, "ones", "fe", cm=4)
-        sel(d0[:, 0:256], one[:], [[0, 2], [1, 16], [1, 8]], A.not_equal, -1.0, -15, "one", "d0a")
-        sel(d0[:, 256:512], one[:], [[0, 8], [1, 8], [1, 4]], A.not_equal, -1.0, -7, "one", "d0b")
-        sel(d0[:, 512:768], one[:], [[0, 2], [1, 16], [-1, 8]], A.not_equal, -1.0, 1, "one", "d0c")
-        sel(d0[:, 768:1024], one[:], [[0, 8], [1, 8], [-1, 4]], A.not_equal, -1.0, 1, "one", "d0d")
-        iota(d0[:, 0:256:8], [[0, 32]], 0, "d0a")
-        iota(d0[:, 256:512:4], [[0, 64]], 0, "d0b")
-        sel(d0[:, 513:768:8], one[:, 0:32], [[0, 2], [1, 16]], A.is_ge, -1.0, -8, "one", "d0c")
-        sel(d0[:, 769:1024:4], one[:, 0:64], [[0, 8], [1, 8]], A.is_ge, -1.0, -4, "one", "d0d")
-
-    def tables_b():
-        iota(d0[:, 512:768:8], [[0, 32]], 0, "d0c")
-        iota(d0[:, 768:1024:4], [[0, 64]], 0, "d0d")
-        iota(d0[:, 513:768:128], [[0, 2]], 1, "d0c")
-        iota(d0[:, 769:1024:32], [[0, 8]], 1, "d0d")
-        sel(T.tau[:, 128:192], T.rr[:, 0:64], [[0, 8], [1, 8]], A.is_ge, -0.03125, -3, "rr", "tau2")
-        sel(T.tau[:, 0:128], T.rr[:, 0:128], [[0, 8], [1, 16]], A.is_ge, -0.03125, -7, "rr", "tau1")
-        sel(T.v0[:, 0:128], one[:, 0:128], [[-1, 8], [1, 8], [0, 2]], A.is_equal, 0.0, 0, "one", "v0")
-
-    def cells():
-        for o, w, c, k in ((T.cd[:], 192, -0.03125, "cd"), (T.va[:, 192:208], 16, 1.0, "vac"), (T.sg[:], 192, -1.0, "sg"),
-                           (T.vb[:, 128:208], 80, 1.0, "vbc"), (T.v0[:, 128:208], 80, 1.0, "v0c"), (T.zz[:, 0:208], 208, 0.0, "zz"),
-                           (T.cd[:, 0:128:16], 8, -2.5, "cd"), (T.zz[:, 208:224], 16, 5.0, "zc"), (T.dl[:, 192:208], 16, -2.0, "dlc"),
-                           (T.sg[:, 15:128:16], 8, 2.0, "sg"), (T.cd[:, 128:192:8], 8, -2.5, "cd"), (T.k0[:, 0:16], 16, 0.0, "k0c"),
-                           (T.va[:, 128:192], 64, 0.0, "vau"), (T.cum[:, 0:16], 16, 0.0, "cum0"), (T.sg[:, 135:192:8], 8, 2.0, "sg"),
-                           (T.cn[:], 16, 0.0, "cn"), (T.fn[:], 16, 0.0, "fn"), (T.ux[:, 0:16], 16, 0.0, "uu0"), (T.dnn[:], 16, 0.0, "dnn")):
-            fill(o, w, c, k)
-
-    fill(T.rr[:, 0:128], 128, 0.03125, "rr")
-    for f in late[:6]:
-        f()
+    for k, a, b, c in (("8q7", "q7", 8.0, 0.0), ("4h+32", "h", 4.0, 32.0), ("4q7+8", "q7", 4.0, 8.0), ("256+q7", "q7", 1.0, 256.0),
+                       ("1-o", "o", -1.0, 1.0), ("2q7+112", "q7", 2.0, 112.0), ("87-q7", "q7", -1.0, 87.0), ("1-o/2", "o", -0.5, 1.0),
+                       ("q+112", "q", 1.0, 112.0), ("128(1-o)", "o", -128.0, 128.0),
+                       ("1+o/2", "o", 0.5, 1.0), ("16q+15", "q", 16.0, 15.0), ("16q7+b2", "q7", 16.0, "b2"), ("8q+112", "q", 8.0, 112.0),
+                       ("1-2b2", "b2", -2.0, 1.0), ("q+4", "q", 1.0, 4.0), ("ha", "h", 2.0, "u"), ("24q3", "q=3", 24.0, 0.0),
+                       ("hb", "16q7+b2", "h", "w129"), ("tu", "q+4", "u", "24q3"), ("hu", "8q+112", "u", "hb"), ("tb0", "q7", "h", "tu")):
+        lin("s", k, a, b, c)
+    XLo, XU = li[:, XL:XL + 16], tmp[:, 0:16]
+    ts(li[:, SEL + 2:SEL + 3], cl("q"), 32.0, cl("e"), A.mult, A.add, "pq ls", "ls2")
+    ts(T.ne[:], T.j16[:], cl("q"), None, A.not_equal, None, "j16 pq", "ne")
+    ts(li[:, SEL:SEL + 1], li[:, SEL + 2:SEL + 3], 1.0, None, A.add, None, "ls2", "ls0")
+    ts(XLo, c16, 2.0, cl("h"), A.mult, A.add, "c16 pc", "xl")
+    ts(XU, c16, 4.0, cl("q2"), A.mult, A.add, "c16 pc", "xu")
+    cp(T.lu[:, SEL:AT], li[:, SEL:AT], "ls0 ls2", "lu1")
     quant(T.uq[:], T.us[:], T.ut[:], "ut", "uq")
+    lin("v", "e-32", "e", 1.0, -32.0)
     cp(T.ub[:].bitcast(dt.uint32), T.uq[:].bitcast(dt.uint32).indirect(L(UP, 8)), "uq lu0", "ub")
     cp(T.ubs[:], T.us[:].indirect(L(UP, 8)), "uq lu0", "ubs")
+    ts(tmi[:, 0:16], XU, cl("q3"), 1.0, A.add, A.add, "xu pc", "y2")
+    ts(tmi[:, 16:48], n23, cl("q7"), cl("h"), A.add, A.subtract, "n23 pc", "dx")
+    ms(T.va[:], 0.0, "vaL vaU vac"), ms(T.vb[:], 0.0, "vbL vbU vbc"), ms(T.zz[:], 0.0, "zL zU zc")
     quant(T.xq0[:], T.xs0[:], T.xt[:], "xt", "xq0")
-    for f in late[6:NEARLY]:
-        f()
+    flat(AT, AT + 8, 1, one[:, 0:8], "q7", 8.0, "lat", "v")
+    ts(li[:, YL:YL + 16], r82, cl("q7"), None, A.add, None, "r82 pc", "lyl")
+    flat(AT + 2, AT + 6, 1, one[:, 0:4], "q7", 0.0, "lat", "v")
+    ts(li[:, TX:TX + 16], rx, cl("h"), cl("8q7"), A.add, A.add, "rx pc 8q7", "ltx")
+    lin("v", "vb", "vd", 1.0, "q1")
 
-    def E(b):
-        return T.eq[:, 128 * b:128 * b + 128], T.es[:, 128 * b:128 * b + 128]
+    late = []
 
-    BANK = ((2, 3, 4, 5), (6, 7, 0, 1))
+    def lt(f, *a):
+        late.append(of(f, *a))
+
+    y2, dx, x4, bv, gz = tmi[:, 0:16], tmi[:, 16:48], tmp[:, 16:48], tmp[:, 48:80], tmp[:, 80:112]
+    mi, m0, m1, m2 = tmi[:, 48:64], tmi[:, 64:80], tmi[:, 80:96], tmi[:, 96:112]
+    k0, k1, kx, sp, nk, w1 = [tmp[:, 128 + 16 * i:144 + 16 * i] for i in range(6)]
+    aff(x4, n23, -4.0, cl("4h+32"), "n23 4h+32", "x4")
+    lt(ts, tmi[:, 56:64], tmp[:, 16:24], 0.25, None, A.mult, None, "x4", "mi2")
+    lt(ts, y2, y2, 7, None, A.bitwise_and, None, "y2", "y2")
+    lt(ts, dx, dx, 7, None, A.bitwise_and, None, "dx", "dx")
+    lt(ts, m0, mi, 1, None, A.bitwise_and, None, "mi1 mi2", "m0")
+    lt(ts, m1, mi, 1, 1, A.logical_shift_right, A.bitwise_and, "mi1 mi2", "m1")
+    lt(ts, m2, mi, 2, 1, A.logical_shift_right, A.bitwise_and, "mi1 mi2", "m2")
+    lt(tt, tmp[:, 112:128], y2, bu, A.add, "y2 bu", "yz")
+    lt(tt, x4, x4, dx, A.add, "dx", "x4")
+    lt(ts, bv, dx, -1.0, cl("4q7+8"), A.mult, A.add, "dx 4q7+8", "bv")
+    lt(ts, gz, dx, 4.0, None, A.is_gt, None, "dx", "gz")
+    lt(tt, li[:, LO:LO + 16], XU, tmp[:, 112:128], A.min, "xu yz", "llo")
+    lt(tt, li[:, HI:HI + 16], XU, tmp[:, 112:128], A.max, "xu yz", "lhi")
+    lt(tt, bv, bv, x4, A.subtract, "x4", "bv")
+    lt(ts, tmp[:, 128:136], tmi[:, 64:72], cl("b2"), None, A.not_equal, None, "m0 pc", "k0a")
+    lt(ts, tmp[:, 136:144], tmi[:, 72:80], cl("b1"), None, A.not_equal, None, "m0 pc", "k0b")
+    lt(tt, bv, bv, gz, A.mult, "gz", "bv")
+    lt(ts, tmp[:, 144:152], tmi[:, 80:88], cl("h"), None, A.not_equal, None, "m1 pc", "k1a")
+    lt(ts, tmp[:, 152:160], tmi[:, 88:96], cl("b2"), None, A.not_equal, None, "m1 pc", "k1b")
+    lt(tt, x4, x4, bv, A.add, "bv", "x4")
+    lt(ts, gz, dx, 0.0, cl("256+q7"), A.is_equal, A.mult, "dx 256+q7", "gz")
+    lt(ts, sp, m1, 4.0, -2.0, A.mult, A.add, "m1", "sp")
+    lt(tt, x4, x4, m32, A.add, "m32", "x4")
+    lt(tt, kx, k0, k1, A.max, "k0a k0b k1a k1b", "kx")
+    lt(ts, w1, m2, 8.0, -4.0, A.mult, A.add, "m2", "w1")
+    lt(tt, sp, sp, k0, A.mult, "k0a k0b", "sp")
+    lt(tt, li[:, TI:TI + 32], x4, gz, A.max, "x4 gz", "lti")
+    lt(tt, w1, w1, kx, A.mult, "kx", "w1")
+    lt(tt, sp, sp, mi, A.subtract, "mi1 mi2", "sp")
+    lt(ts, nk, kx, -1.0, 1.0, A.mult, A.add, "kx", "nk")
+    lt(tt, sp, sp, w1, A.add, "w1", "sp")
+    lt(ts, tmp[:, 216:220], tmp[:, 200:204], 128.0, None, A.mult, None, "nk sp", "w2")
+    lt(ts, tmp[:, 128:136], tmp[:, 176:184], 16.0, cl("q+112"), A.mult, A.add, "sp q+112", "k0a")
+    lt(ts, tmp[:, 136:144], tmp[:, 184:192], 16.0, cl("2q7+112"), A.mult, A.add, "sp 2q7+112", "k0b")
+    lt(ts, tmp[:, 156:160], tmp[:, 188:192], -8.0, cl("87-q7"), A.mult, A.add, "sp 87-q7", "k1b")
+    lt(ts, tmp[:, 208:216], tmp[:, 192:200], cl("128(1-o)"), None, A.mult, None, "nk 128(1-o)", "w1")
+    lt(tt, tmp[:, 128:136], tmp[:, 128:136], tmp[:, 192:200], A.subtract, "nk", "k0a")
+    lt(tt, tmp[:, 156:160], tmp[:, 156:160], tmp[:, 172:176], A.mult, "kx", "k1b")
+    lt(tt, li[:, PV:PV + 12], tmp[:, 128:140], tmp[:, 208:220], A.max, "k0a k0b w1 w2", "lpv")
+    lt(tt, tmp[:, 156:160], tmp[:, 156:160], tmp[:, 140:144], A.add, "k0b", "k1b")
+    lt(ts, li[:, PU:PU + 4], tmp[:, 156:160], 1.0, None, A.add, None, "k1b", "lpu")
+    lt(cp, T.lu[:, AT:VA], li[:, AT:VA], "lat xl lyl llo lhi lti ltx lpv lpu", "lu")
+    slots = [of(lin, "s", "hb0", "q=3", -1.0, "hu"), of(lin, "s", "td", "u", 4.0, "q=3"), of(lin, "s", "32u", "u", 32.0, "hb0"),
+             of(flat, VA, VA + 4, 1, eight, "o", "q1", "lva1"), of(flat, VA + 4, VA + 8, 1, eight, "1-o", "q1", "lva2"),
+             of(lin, "s", "hb1", "1-2b2", "h", "32u"),
+             of(flat, VA + 8, VA + 16, 2, one[:, 0:4], "vb", 0.0, "lv0"), of(flat, VA + 9, VA + 16, 2, eight, "1-o/2", "vb", "lv1"),
+             of(flat, VA + 16, VA + 24, 2, eight, "o", "vb", "lv2"), of(flat, VA + 17, VA + 24, 2, eight, "1+o/2", "vb", "lv3"),
+             of(flat, CU, CU + 8, 1, one[:, 0:8], "16q+15", 0.0, "lcu"), of(flat, Q7, Q7 + 8, 1, one[:, 0:8], "q7", 0.0, "lq7"),
+             of(flat, UE, UE + 8, 1, li[:, XL:XL + 8], 16.0, 31.0, "lue"),
+             of(flat, TB, TB + 8, 1, one[:, 0:8], "tb0", 0.0, "ltb0"), of(flat, TB + 8, TB + 16, 1, one[:, 0:8], "tb0", "td", "ltb1"),
+             of(flat, HB, HB + 8, 1, rw[:, 0:8], "ha", "hb0", "lhb0"), of(flat, HB + 8, HB + 16, 1, rw[:, 0:8], "ha", "hb1", "lhb1"),
+             of(cp, T.lu[:, VA:NL], li[:, VA:NL], "lva1 lva2 lv0 lv1 lv2 lv3 lcu lc8 lq7 lue lhb0 lhb1 ltb0 ltb1", "lu2")]
+
+    def tables():
+        sel(T.fe[:], T.ones[:], [[-1, 528]], A.is_equal, 0.0, 3, "ones", "fe", cm=4)
+        sel(T.di[:], one[:], [[0, 4], [-1, 8], [1, 8]], A.not_equal, -1.0, 0, "one", "di")
+        sel(T.df[:], one[:], [[0, 2], [2, 8], [-1, 16]], A.is_ge, -1.0, 0, "one", "df")
+        sel(T.sg[:, 0:64], one[:, 0:64], [[0, 8], [1, 8]], A.is_equal, -1.0, -7, "one", "sgN")
+
+    def small():
+        for o, st, w, c, k in ((T.va[:, 128:144], 0, 16, 1, "vac"), (T.v0[:, 128:144], 0, 16, 1, "v0c"), (li[:, C8:C8 + 8], 1, 8, 0, "lc8"),
+                               (T.val[:, 384:400], 0, 16, 0, "valc"), (T.bb[:, 256:272], 1, 16, 0, "bcN"), (T.di[:, 0:256:8], 0, 32, 0, "di"),
+                               (T.sc[:, 15:16], 0, 1, 0, "sc0"), (T.dl[:, 64:145:80], 0, 2, -2, "dlc"), (T.zz[:, 144:160], 0, 16, 5, "zc"),
+                               (T.vb[:, 128:144], 0, 16, 1, "vbc")):
+            iota(o, [[st, w]], c, k)
+        sel(T.r8[:], one[:], [[0, 32], [1, 8]], A.not_equal, 0.0, 0, "one", "r8")
+        for o, st, w, c, k in ((T.bb[:, 800:816], 1, 16, 8, "bcF"), (T.df[:, 0:256:16], 0, 16, 0, "df"), (T.dl[:, 288:289], 0, 1, -2, "dlcF")):
+            iota(o, [[st, w]], c, k)
+        sel(T.sg[:, 64:192], one[:, 0:128], [[0, 8], [1, 16]], A.is_equal, -1.0, -15, "one", "sgF")
+        for o, st, w, c, k in ((T.bb[:, 528:544], 1, 16, 0, "bcU"), (T.dts[:], 0, 32, 0, "dts"), (T.sml[:], 0, 48, -1, "sml"),
+                               (T.zz[:, 145:146], 0, 1, 1, "zc"), (T.cum[:, 0:16], 0, 16, -1, "cum0"), (T.na[:, 131:384:4], 0, 64, 1, "nac"),
+                               (T.c12[:], 0, 256, 0, "c12"), (T.c12[:, 0:256:16], 0, 16, -12, "c12")):
+            iota(o, [[st, w]], c, k)
+
     for t in range(R):
         s = str(t)
-        xq, xs, lq, ls = T["xq" + s], T["xs" + s], T["lq" + s], T["ls" + s]
+        xq, xs = T["xq" + s], T["xs" + s]
         sm, oo, hl, bn, on, hn = [T[k + s] for k in ("sm", "oo", "hl", "bn", "on", "hn")]
         side = marks_side(t)
         XK = " xq%s xr%s" % (s, s)
         mm(0, 256, T.ub[:], T.ubs[:], xq[:], xs[:], "ub ubs" + XK)
-        mm(1, 256, T.uq[:], T.us[:], xq[:], xs[:], "uq" + XK)
+        mm(1, 256, T.ub[:], T.ubs[:], xq[:], xs[:], "ub ubs" + XK)
+        mm(2, 256, T.uq[:], T.us[:], xq[:], xs[:], "uq" + XK)
         send_x(t)
         if t == 0:
-            tables_a()
+            tables()
+        act(T.t2[:], ps(1, 0, 256), "ps1", "t2", f=F.Abs, scale=1.25 * 2.0 ** -24, bias=2.0 ** -120)
         tt(T.t1[:], ps(0, 0, 256), T.eye[:], A.mult, "ps0 eye", "t1")
-        act(T.pm[:], ps(1, 0, 256), "ps1", "pm")
-        scan(T.scn[:], T.rm[:, 192:448], T.t1[:], A.mult, A.add, "rm t1", "scn")
-        for c in range(16):
-            sc, m = T.scn[:, 16 * c + 15:16 * c + 16], 256 * c
-            if c:
-                ts(T.m[:, m:m + 16 * c], ps(0, 0, 16 * c), sc, None, A.is_ge, None, "ps0 scn", "ma%d" % c)
-            ts(T.m[:, m + 16 * c:m + 256], ps(0, 16 * c, 256 - 16 * c), sc, None, A.is_gt, None, "ps0 scn", "mb%d" % c)
-            act(T.m[:, m:m + 256], T.m[:, m:m + 256], "", "ma%d mb%d acc%d" % (c, c, c), scale=32.0, accum_out=T.acc[:, c:c + 1])
-        tt(T.bm[:], ps(0, 0, 256), T.mk[:], A.max, "ps0 mk", "bm")
-        if t == 0:
-            fill(T.ow[:], 512, 0.0, "ow")
-        tt(T.ec[:], T.scn[:].indirect(L(EQ, 16)), T.bm[:], A.is_equal, "scn bm lu0", "ec")
-        scan(T.es2[:], T.rm[:, 192:448], T.ec[:], A.mult, A.add, "rm ec", "es2")
-        ts(T.e32[:], T.es2[:, 15:256:16], 32.0, None, A.mult, None, "es2", "e32")
-        ri = T.ri
-        tt(ri[:, 0:16], T.acc[:], T.e32[:], A.add, "e32 " + " ".join("acc%d" % c for c in range(16)), "r32")
-        ts(ri[:, 16:32], ri[:, 0:16], 9, None, A.logical_shift_right, None, "r32", "hi")
-        ts(ri[:, 32:48], ri[:, 16:32], -511.0, col["e"], A.mult, A.add, "hi pc", "h2")
-        tt(ri[:, 48:64], ri[:, 32:48], ri[:, 0:16], A.add, "h2 r32", "pti")
+        act(T.row[:, 0:256], ps(1, 0, 256), "ps1", "row")
+        scan(T.scn[:, ::-1], T.rm[:], T.t1[:, ::-1], A.mult, A.add, "rm t1", "scn")
+        tt(T.row[:, 256:512], ps(0, 0, 256), T.t2[:], A.add, "ps0 t2", "up")
+        act(T.pm[:], ps(2, 0, 256), "ps2", "pm")
+        dma("y", T.px[1:128:16, :], T.pm[1:128:16, :], "lp", "pm", "px")
+        ri, e32, acc = T.ri, T.e32, T.acc
+
+        def ahead(c):
+            o, w, sc = T.m[:, 256 * c:256 * c + 256], T.row[:, 16 * c:16 * c + 256], T.scn[:, 16 * c:16 * c + 1]
+            if WHO[c] == "s":
+                act(o, w, "row up scn", "m%d" % c, f=F.Sign, scale=-1.0, bias=sc)
+            else:
+                ts(o, w, sc, 32.0, A.is_gt, A.mult, "row up scn", "m%d" % c)
+
+        def count(c):
+            w = T.m[:, 256 * c:256 * c + 256]
+            if WHO[c] == "v":
+                scan(T.mo[:, 256 * (c - NS):256 * (c - NS) + 256], w, w, A.add, A.max, "m%d" % c, "mo%d" % c)
+            else:
+                act(w, w, "", "m%d ar%d" % (c, c), f=F.Relu, scale=-32.0 if WHO[c] == "s" else 1.0, accum_out=acc[:, c:c + 1])
+
+        alone, both = [c for c in range(NS) if WHO[c] == "s"], [c for c in range(NS) if WHO[c] == "b"]
+        tt(T.ec[:], ps(0, 0, 256), T.scn[:], A.is_equal, "ps0 scn", "ec")
+        for c in both:
+            ahead(c)
+        for i, c in enumerate(alone):
+            ahead(c)
+            if i:
+                count(alone[i - 1])
+            if i == len(alone) - 1:
+                for b in both:
+                    count(b)
+        count(alone[-1])
+        equal = [of(scan, T.es2[:, ::-1], T.ne[:, ::-1], T.ec[:, ::-1], A.mult, A.add, "ne ec", "es2"),
+                 of(ts, e32[:, 0:16], T.es2[:, 0:256:16], 32.0, cl("e-32"), A.mult, A.add, "es2 e-32", "e32")]
+        for c in range(NS, 17):
+            if c < 16:
+                ahead(c)
+            if c > NS:
+                count(c - 1)
+            run(equal[c - NS:c - NS + 1])
+        tt(ri[:, 0:NS], acc[:, 0:NS], e32[:, 0:NS], A.add, "e32 " + " ".join("ar%d" % c for c in range(NS)), "xb")
+        tt(ri[:, NS:16], T.mo[:, 255:256 * (16 - NS):256], e32[:, NS:16], A.add, "e32 " + " ".join("mo%d" % c for c in range(NS, 16)), "xa")
+        ts(ri[:, 16:32], ri[:, 0:16], 9, None, A.logical_shift_right, None, "xa xb", "hi")
+        ts(ri[:, 32:48], ri[:, 0:16], 496, None, A.bitwise_and, None, "xa xb", "lo")
+        ts(ri[:, 64:80], ri[:, 0:16], 480, None, A.bitwise_and, None, "xa xb", "r16")
+        tt(ri[:, 48:64], ri[:, 32:48], ri[:, 16:32], A.add, "hi lo", "pti")
+        ts(ri[:, 80:96], ri[:, 64:80], 0.5, None, A.mult, None, "r16", "r17")
         cp(T.pt[:], ri[:, 48:64], "pti", "pt")
-        cp(T.sw[:].indirect(T.pt[:]), T.pm[:], "pm pt", "sw")
+        tt(ri[:, 96:112], ri[:, 80:96], ri[:, 16:32], A.add, "r17 hi", "r18")
+        cp(T.sw[:].indirect(T.pt[:]), T.px[:], "px pt", "sw")
+        cp(T.pz[:], ri[:, 96:112], "r18", "pz")
         op("v", lambda: V.transpose(T.tr[:], T.sw[:]), "sw", "tr")
-        cp(sm[:], T.tr[:].indirect(L(SEL, 1)), "tr lu0", "sm" + s)
+        cp(sm[:], T.tr[:].indirect(L(SEL, 1)), "tr lu1", "sm" + s)
         send(side, sm[:], "sm" + s, bn[:], "ab" + s, "rb" + s)
-        if t == 0:
-            tables_b()
-            for b in range(4):
-                act(T.et[:, 512 * b:512 * b + 512], T.fe[:, 3 - b:515 - b], "fe", "et%d" % b)
-            for f in late[NEARLY:]:
-                f()
-        act(T.at[:], sm[:].indirect(L(AT if side < 0 else BL, 12)), "lu sm" + s, "at_")
-        if t == 0:
-            cells()
-        else:
-            fill(T.va[:, 128:192], 64, 0.0, "vau")
-        cp(T.ow[:].indirect(T.pt[:]), T.i256[:], "i256 pt", "ow")
-        ts(ri[:, 64:80], ri[:, 0:16], 0.5, None, A.mult, None, "r32", "r16")
-        ts(ri[:, 80:96], ri[:, 16:32], -255.0, None, A.mult, None, "hi", "h3")
-        op("v", lambda: V.transpose(T.otr[:], T.ow[:]), "ow", "otr")
-        tt(ri[:, 64:80], ri[:, 64:80], ri[:, 80:96], A.add, "r16 h3", "r16")
-        cp(oo[:], T.otr[:].indirect(L(SEL, 1)), "otr lu0", "oo" + s)
+        cp(oo[:], T.tr[:].indirect(L(SEL + 2, 1)), "tr lu1", "oo" + s)
         send(side, oo[:], "oo" + s, on[:], "ao" + s, "ro" + s)
-        cp(T.pz[:], ri[:, 64:80], "r16", "pz")
         (so, sk), (to, tk) = ((oo, "oo" + s), (on, "on" + s))[::-side]
+        dts, val, da, dz = T.dts, T.val, T.da, T.dz
+        of_so = [of(act, val[:, 0:128], so[:].indirect(L(VA, 8)), "lu2 " + sk, "val1"),
+                 of(act, val[:, 128:384], so[:].indirect(L(VA + 8, 16)), "lu2 " + sk, "val2"),
+                 of(tt, da[:], val[:, 0:384], val[:, 1:385], A.subtract, "val1 val2 valc", "da"),
+                 of(cp, da[:, 15:128:16], val[:, 15:128:16], "val1 da", "da1"),
+                 of(cp, da[:, 159:384:32], val[:, 159:384:32], "val2 da", "da2")]
+        of_to = [of(tt, dts[:, 0:15], to[:, 0:15], to[:, 1:16], A.subtract, tk, "dts"),
+                 of(tt, dts[:, 16:23], to[:, 8:15], to[:, 9:16], A.subtract, tk, "dt1"),
+                 of(ts, dts[:, 24:26], to[:, 8:16:4], -1.0, None, A.mult, None, tk, "dt2"),
+                 of(cp, dts[:, 7:24:16], to[:, 7:16:8], "dts " + tk, "dt3"),
+                 of(ts, dts[:, 11:16:4], to[:, 11:16:4], to[:, 0:1], None, A.subtract, None, "dts " + tk, "dt4"),
+                 of(act, dz[:, 0:256], dts[:].indirect(L(TB, 16)), "lu2 dts dt1 dt2 dt3 dt4", "dz dz2"),
+                 of(act, dz[:, 256:384], dts[:, 16:32].indirect(L(Q7, 8)), "lu2 dts dt1 dt2 dt3 dt4", "dz3")]
+        of_own, of_far = (of_so, of_to) if side < 0 else (of_to, of_so)
 
-        def dso():
-            tt(T.od[:, 1:16], so[:, 1:16], so[:, 0:15], A.subtract, sk, "od1")
-            cp(T.od[:, 0:1], so[:, 0:1], sk, "od0")
+        def out_of(q, sc, key, bank, dst, qs):
+            fs = [lambda: [mm(bank + b, 256, *E(b), q[:], sc[:], "eq%d %s" % (b, key)) for b in range(4)]]
+            return fs + [of(scaled, qs[b], dst(b)[0], ps(bank + b, 0, 256), "ps%d" % (bank + b), dst(b)[1]) for b in range(4)]
 
-        def dto():
-            tt(T.dnn[:, 1:8], to[:, 9:16], to[:, 8:15], A.subtract, "dnn " + tk, "dx1")
-            cp(T.dnn[:, 0:1], to[:, 8:9], "dnn " + tk, "dx0")
+        def from_next(qs):
+            return out_of(T["nq" + s], T["ns" + s], "nq" + s, 4, lambda b: (T.dn[:, 256 * b:256 * b + 256], "dn%d" % b), qs)
 
-        def tab_s():
-            act(T.tb[:, 0:192], so[:].indirect(L(AT, 12)), "lu " + sk, "tb1")
-            act(T.tb[:, 192:320], T.od[:].indirect(L(QL, 8)), "lu od0 od1", "tb2")
+        def from_prev(qs):
+            return out_of(T["pq" + s], T["pr" + s], "pq" + s, 0, lambda b: (T.gt[:, b:1024:4], "gt%d" % b), qs) + \
+                [of(quant, T.gq[:], T.gs[:], T.gt[:], "gt0 gt1 gt2 gt3", "gq")]
 
-        def tab_t():
-            act(T.ta[:, 0:256], to[:].indirect(L(QL, 16)), "lu " + tk, "ta1")
-            act(T.ta[:, 256:384], T.dnn[:].indirect(L(Q7, 8)), "lu dx0 dx1", "ta2")
+        def once_more(qs):
+            return out_of(T.gq, T.gs, "gq", 0, lambda b: (T.dp[:, 256 * b:256 * b + 256], "dp%d" % b), qs)
 
-        own_d, far_d, own_t, far_t = (dso, dto, tab_s, tab_t) if side < 0 else (dto, dso, tab_t, tab_s)
-        own_d()
-        if t:
-            own_t()
+        whom = {-1: (L(AT + 4, 4), L(AT, 8)), 1: (L(XL, 4), L(XL, 8))}
+        mine = [of(act, T.at[:, 0:64], sm[:].indirect(whom[side][0]), "lu sm" + s, "atN"),
+                of(act, T.at[:, 64:192], sm[:].indirect(whom[side][1]), "lu sm" + s, "atF")]
+        after = []
         if t == 0:
-            for b in range(4):
-                quant(*E(b), T.et[:, 512 * b:512 * b + 512], "et%d" % b, "eq%d" % b)
-        for b in range(4):
-            mm(2 + b, 512, *E(b), lq[:], ls[:], "eq%d lq%s" % (b, s))
-        tt(T.dd[:], bn[:].indirect(L(BL if side < 0 else AT, 12)), T.at[:], A.subtract, "lu at_ bn" + s, "dd")
+            small()
+            run([of(quant, *E(b), T.fe[:, 3 - b:515 - b], "fe", "eq%d" % b) for b in range(4)])
+            soon, again = (from_prev("ssss"), once_more("ssss")) if way[-1][0] else ([], [])
+            run(slots[:-1] + soon[:5] + late[:10] + slots[-1:] + of_own[:2] + late[10:20] + soon[5:] + again + late[20:])
+            run(mine)
+            act(T.v0[:, 0:128], T.va[:, 0:144].indirect(L(PV, 8)), "vaL vac lu", "v0L")
+            run(of_own[2:])
+            aff(T.r0[:], T.v0[:].indirect(L(PN, 4)), -8.0, 9.0, "lu v0L v0c", "r0")
+            during = from_next("ssss")
+            if not soon:
+                after = from_prev("svsv") + once_more("svsv")
+        else:
+            ms(T.va[:, 0:128], 0.0, "vaL"), ms(T.va[:, 144:208], 0.0, "vaU")
+            a, b = from_prev("ssss"), from_next("ssvv")
+            run(a[:5] + b[:3] + mine + of_own[:5] + a[5:] + of_own[5:] + b[3:])
+            during = once_more("ssss")
+            if not way[-side][0]:
+                during[0]()
+                during = [lambda: None] + during[1:]
+            else:
+                run(during)
+                during = []
+            quant(T.vq[:], T.vs[:], T.vt[:], "vt", "vq")
 
-        def win(buf, i):
-            return buf[:, 128:192] if i == 4 else buf[:, 32 * i:32 * i + 32]
+        gg, gh, bb, bt, sc, kn, dl, db, yy, zz = T.gg, T.gh, T.bb, T.bt, T.sc, T.kn, T.dl, T.db, T.yy, T.zz
+        SETS = {"N": 0, "U": 1, "F": 2}
+        CELL = {"N": 0, "F": 64, "U": 128}
+        SUMS = {"N": 16, "F": 528, "U": 1552, "X": 2064}
 
-        def hi(i):
-            act(T.gh[:, 256 * i:256 * i + 256], win(T.dd, i).indirect(L(HI + 16 * (i == 4), 16)), "dd lu", "gh%d" % i, f=F.Abs)
+        def dist(k):
+            a, b = (0, 64) if k == "N" else (64, 192)
+            tt(T.dd[:, a:b], bn[:].indirect(whom[-side][k != "N"]), T.at[:, a:b], A.subtract, "lu at%s bn%s" % (k, s), "dd" + k)
 
-        def beat(i):
-            tt(T.bb[:, 512 * i:512 * i + 256], win(T.gg, i).indirect(L(LO + 16 * (i == 4), 16)), T.gh[:, 256 * i:256 * i + 256], A.is_le, "gg lu gh%d" % i, "b%d" % i)
+        def high(k):
+            i, a = SETS[k], CELL[k]
+            act(gh[:, 256 * i:256 * i + 256], T.dd[:, a:a + 64].indirect(L(HI, 16)), "lu dd" + "NF"[k != "N"], "gh" + k, f=F.Abs)
 
-        def rsum(i):
-            u = 256 * (i == 4)
-            scan(T.bb[:, 512 * i + 256:512 * i + 512], d0[:, u:u + 256], T.bb[:, 512 * i:512 * i + 256], A.mult, A.add, "d0a d0b b%d" % i, "br%d" % i)
+        def beat(k):
+            i, a = SETS[k], CELL[k]
+            tt(bb[:, 272 * i:272 * i + 256], gg[:, a:a + 64].indirect(L(LO, 16)), gh[:, 256 * i:256 * i + 256], A.is_le,
+               "lu gh%s gg%s" % (k, "NF"[k != "N"]), "b" + k)
 
-        def turn(i, q):
-            o, w = T.bt[:, 256 * i:256 * i + 256], T.bb[:, 512 * i:512 * i + 512].indirect(L(BT + 16 * (i == 4), 16))
-            (act if q == "s" else cp)(o, w, "lu b%d br%d" % (i, i), "bt_%d" % i)
+        def turn(k, h, q="s"):
+            i = SETS[k]
+            o = bt[:, 1025 + 512 * h:1536 + 512 * h:2] if k == "F" else bt[:, 512 * i + 256 * h:512 * i + 256 * h + 256]
+            scaled(q, o, bb[:, 272 * i:272 * i + 272].indirect(L(TI + 16 * h, 16)), "lu bc%s b%s" % (k, k), "t%s%d" % (k, h))
 
-        def sums(i):
-            u = 512 + 256 * (i == 4)
-            scan(T.sc[:, 256 * i:256 * i + 256], d0[:, u:u + 256], T.bt[:, 256 * i:256 * i + 256], A.mult, A.add, "d0c d0d bt_%d" % i, "sc%d" % i)
+        def wins(k, h):
+            a, b = SUMS[k] + 256 * h, 512 * SETS[k] + 256 * h
+            if k == "F":
+                scan(sc[:, a:a + 256], T.df[:], bt[:, b:b + 256], A.mult, A.add, "df tF%d tX%d" % (h // 2, h // 2), "wF%d" % h)
+            else:
+                scan(sc[:, a:a + 256], T.di[:], bt[:, b:b + 256], A.mult, A.add, "di t%s%d" % (k, h), "w%s%d" % (k, h))
 
-        act(T.gg[:], T.dd[:], "dd", "gg", f=F.Abs)
-        hi(4), hi(0), beat(4), hi(1), beat(0), rsum(4), hi(2), beat(1), rsum(0), hi(3), turn(4, "s"), beat(2), rsum(1), turn(0, "s"), beat(3)
-        rsum(2), turn(1, "s"), rsum(3), sums(4), turn(3, "v"), turn(2, "s"), sums(0)
-        tt(T.k0[:, 144:208], T.sc[:, 1027:1280:4], T.tau[:, 128:192], A.mult, "sc4 tau2", "k0b")
-        sums(1), sums(3), sums(2)
-        tt(T.k0[:, 16:144], T.sc[:, 7:1024:8], T.tau[:, 0:128], A.mult, "sc0 sc1 sc2 sc3 tau1", "k0a")
-        tt(T.k1[:], T.k0[:, 16:208], T.k0[:, 15:207], A.subtract, "k0a k0b k0c", "k1")
-        tt(T.dl[:, 0:192], T.k1[:], T.cd[:], A.add, "k1 cd", "dl")
+        def step(k):
+            a, b = 80 * SETS[k], SUMS[k]
+            tt(dl[:, a:a + 64], sc[:, b - 1:b + 504:8], sc[:, b + 7:b + 512:8], A.subtract, "sc0 wF3 w%s0 w%s1" % (k, k), "dl" + k)
 
-        def unpack(o, bank, a, key):
-            return lambda: act(o, ps(bank, a, 256), "ps%d" % bank, key, scale=0.03125)
+        def anew(k):
+            a = 80 * SETS[k]
+            ms(dl[:, a:a + 128:16] if k == "F" else dl[:, a:a + 64:8], -2.0, "dl" + k)
 
-        gts = [unpack(T.gt[:, b:1024:4], 2 + b, 256, "gt%d" % b) for b in range(4)]
-        dns = [unpack(T.dn[:, 256 * b:256 * b + 256], 2 + b, 0, "dn%d" % b) for b in range(4)]
-        dps = [unpack(T.dp[:, 256 * b:256 * b + 256], BANK[1][b], 0, "dp%d" % b) for b in range(4)]
-        beside = gts + dns[:2] + dps + dns[2:]
-        zz = T.zz
+        def back(k):
+            i = SETS[k]
+            w, a = (128, 64) if k == "F" else (64, 0)
+            tt(db[:, 64 * i:64 * i + w], dl[:, 80 * i + 1:80 * i + w + 1], T.sg[:, a:a + w], A.mult, "dlc dlcF sgN sgF dlF2 dl" + k, "db" + k)
+
+        def far_of(h):
+            act(gh[:, 768 + 256 * h:1024 + 256 * h], T.dd[:, 64 + 32 * h:96 + 32 * h].indirect(L(YL, 16)), "lu ddF", "ghX%d" % h, f=F.Abs)
+
+        def cross(h):
+            tt(bb[:, 816 + 256 * h:1072 + 256 * h], gg[:, 32 * h:32 * h + 32].indirect(L(XL, 16)), gh[:, 768 + 256 * h:1024 + 256 * h],
+               A.is_lt if h else A.is_le, "lu ggN ghX%d" % h, "bX%d" % h)
+
+        def rows(h):
+            a = SUMS["X"] + 256 * h
+            scan(sc[:, a:a + 256], T.r8[:], bb[:, 816 + 256 * h:1072 + 256 * h], A.mult, A.add, "r8 bX%d" % h, "wX%d" % h)
+
+        def turn_x(h):
+            scaled("s", bt[:, 1024 + 512 * h:1536 + 512 * h:2], bb[:, 816 + 256 * h:1072 + 256 * h].indirect(L(TX, 16)), "lu bX%d" % h, "tX%d" % h)
+
+        near = [of(scaled, "v", kn[:, 64:128], sc[:, SUMS["X"] + 7:SUMS["X"] + 512:8], "wX0 wX1", "x32"),
+                of(tt, kn[:, 0:64], sc[:, 23:528:8], kn[:, 64:128], A.add, "wN0 wN1 x32", "kn")]
+        WF = "kn wN1 wF0 wF1 wF2 wF3"
+        whole = [of(tt, dl[:, 160:288:2], sc[:, 527:1536:16], kn[:, 0:64], A.subtract, WF, "dlF"),
+                 of(tt, dl[:, 161:288:2], kn[:, 0:64], sc[:, 543:1552:16], A.subtract, WF, "dlF2"), of(anew, "F")]
+
+        def state(k):
+            return (T.v0, "v0") if k == 0 else (T.va, "va") if k % 2 else (T.vb, "vb")
+
+        def forth(k, p):
+            src, sn = state(k)
+            if p == "N":
+                scan(yy[:, 0:64], dl[:, 0:64], src[:, 0:128:2], A.add, A.max, "dlN %sL" % sn, "yL")
+            elif p == "F":
+                scan(yy[:, 0:128], dl[:, 160:288], src[:, 0:128], A.add, A.max, "dlF dlF2 %sL" % sn, "yL")
+            else:
+                scan(yy[:, 128:192], dl[:, 80:144], src[:, 144:208], A.add, A.max, "dlU %sU" % sn, "yU")
+
+        def backw(p):
+            if p == "N":
+                scan(zz[:, 142:15:-2], db[:, 63::-1], yy[:, 63::-1], A.add, A.max, "dbN yL", "zL")
+            elif p == "F":
+                scan(zz[:, 143:15:-1], db[:, 255:127:-1], yy[:, 127::-1], A.add, A.max, "dbF yL", "zL")
+            else:
+                scan(zz[:, 223:159:-1], db[:, 127:63:-1], yy[:, 191:127:-1], A.add, A.max, "dbU yU", "zU")
+
+        MOVE = {"N": (PN, 4, 0, 128, 2, 144), "F": (PV, 8, 0, 128, 1, 144), "U": (PU, 4, 144, 208, 1, 208)}
+
+        def stood(k, p):
+            src, sn = state(k)
+            lst, w, a, b, st, win = MOVE[p]
+            aff(T.rr[:, a:a + 16 * w], src[:, 0:win].indirect(L(lst, w)), -8.0, 9.0, "lu %sL %sc" % (sn, sn) + (" %sU" % sn) * (p == "U"),
+                "rr" + "LU"[p == "U"])
+
+        def move(k, p):
+            dst, dn_ = state(k + 1)
+            lst, w, a, b, st, win = MOVE[p]
+            r, rk = (T.r0[:], "r0") if k == 0 else (T.rr[:, a:a + 16 * w], "rr" + "LU"[p == "U"])
+            tt(dst[:, a:b:st], zz[:, 16:16 + win].indirect(L(lst, w)), r, A.is_gt, rk + " lu zL zc" + " zU" * (p == "U"), dn_ + "LU"[p == "U"])
+
+        dist("N"), high("N")
+        ts(T.dd[:, 192:256], T.dd[:, 0:64], -1.0, None, A.mult, None, "ddN", "nd")
+        dist("F")
+        tt(gg[:, 0:64], T.dd[:, 0:64], T.dd[:, 192:256], A.max, "ddN nd", "ggN")
+        far_of(0), beat("N"), turn("N", 0), turn("N", 1, "v")
+        act(gg[:, 64:192], T.dd[:, 64:192], "ddF", "ggF", f=F.Abs)
+        high("F"), cross(0), wins("N", 1), wins("N", 0), far_of(1), rows(0), step("N"), turn_x(0), anew("N")
+        FORTH = {0: [of(back, "N")], 2: [of(wins, "F", 0)], 3: near[1:], 4: [of(back, "F")], 7: [of(wins, "U", 1)]}
+        BACK = {0: [of(beat, "F")], 1: [of(cross, 1)], 2: [of(wins, "F", 1)], 4: [of(beat, "U")], 6: [of(wins, "U", 0)], 7: [of(step, "U")]}
+        MOVED = {1: [of(rows, 1), of(turn, "F", 0), of(turn_x, 1)], 2: near[:1] + [of(turn, "F", 1)],
+                 3: [of(wins, "F", 2), of(wins, "F", 3), of(high, "U")] + whole,
+                 5: [of(turn, "U", 0)], 6: [of(turn, "U", 1)], 7: [of(anew, "U"), of(back, "U")]}
+        if during:
+            MOVED[4] = during[0:2]
+            MOVED[7] += during[2:3]
+            MOVED[8], MOVED[9] = during[3:4], during[4:5]
+        if t == 0 and not after:
+            MOVED[8] += of_far[0:3]
+            MOVED[9] += of_far[3:5]
+            MOVED[10] = of_far[5:7]
+            of_far = []
         for k in range(12):
-            src, sn = (T.v0, "v0 v0c") if k == 0 else (T.va, "va vac vau") if k % 2 else (T.vb, "vb vbc")
-            dst, dn_ = (T.vb, "vb") if k % 2 else (T.va, "va")
-            w, w2 = (128 if k < 8 else 192), (128 if k < 7 else 192)
-            if k < 11:
-                aff(T.rr[:, 0:w2], src[:].indirect(L(PV, w2 // 16)), -8.0, 9.0, "lu " + sn, "rr")
-            if k == 0 and t == 0:
-                own_t()
-            beside[k]()
-            scan(T.yy[:, 0:w], T.dl[:, 0:w], src[:, 0:w], A.add, A.max, "dl " + sn, "yy")
-            if k == 0:
-                tt(T.db[:], T.dl[:, 1:193], T.sg[:], A.mult, "dl dlc sg", "db")
-            scan(zz[:, 15 + w:15:-1], T.db[:, w - 1::-1], T.yy[:, w - 1::-1], A.add, A.max, "db yy", "zz")
+            p = "N" if k < 4 else "F"
+            to_ = "N" if k < 3 else "F"
+            if 0 < k < 11:
+                stood(k, to_)
+            if 7 <= k < 11:
+                stood(k, "U")
             if k == 11:
-                break
-            if k == 4:
-                quant(T.gq[:], T.gs[:], T.gt[:], "gt0 gt1 gt2 gt3", "gq")
-                for b in range(4):
-                    mm(BANK[1][b], 256, *E(b), T.gq[:], T.gs[:], "eq%d gq" % b)
-            tt(dst[:, 0:w2], zz[:, 16:224].indirect(L(PV, w2 // 16)), T.rr[:, 0:w2], A.is_gt, "rr lu zz zc", dn_ + (" vau" if k % 2 == 0 and w2 > 128 else ""))
+                forth(k, "U")
+            forth(k, p)
+            if 7 < k < 11:
+                forth(k, "U")
+            if k == 11:
+                ts(T.sml[:, 0:8], yy[:, 135:192:8], 0.5, None, A.is_lt, None, "yU sml", "fr")
+            run(FORTH.get(k, []))
+            backw(p)
+            if k > 7:
+                backw("U")
+            run(BACK.get(k, []))
+            if k < 11:
+                move(k, to_)
+            if 7 <= k < 11:
+                move(k, "U")
+            run(MOVED.get(k, []))
+        sml, cum, na, nb, ss = T.sml, T.cum, T.na, T.nb, T.ss
+        scan(sml[:, 17:25], sml[:, 0:8], sml[:, 0:8], A.add, A.max, "fr", "cn")
+
+        def held():
+            ts(nb[:], zz[:, 16:224].indirect(L(HB, 16)), 1.0, None, A.not_equal, None, "zL zU zc lu2", "nb")
+
+        def left():
+            scan(cum[:, 16:272], T.c12[:], nb[:], A.add, A.add, "c12 nb", "cum")
+
+        def seats(out, key, first):
+            if first:
+                held()
+            ts(na[:, 0:128], zz[:, 16:144], 1.0, None, A.not_equal, None, "zL", "na1")
+            if first:
+                left()
+            ts(na[:, 129:384:4], zz[:, 160:224], 1.0, None, A.not_equal, None, "zU", "na2")
+            tt(na[:, 128:384:2], cum[:].indirect(L(CU, 8)), T.fb[:], A.is_ge, "cum cum0 fb lu2", "na3")
+            scan(ss[:, 0:128], na[:, 0:128], da[:, 0:128], A.mult, A.add, "na1 da da1", "ss1")
+            scan(ss[:, 128:384], na[:, 128:384], da[:, 128:384], A.mult, A.add, "na2 na3 nac da da2", "ss2")
+            cp(out[:, 0:8], ss[:, 15:128:16], "ss1", key)
+            cp(out[:, 8:16], ss[:, 159:384:32], "ss2", key + "b")
+
+        def free_before():
+            act(T.c2[:], sml[:, 16:32].indirect(L(Q7, 8)), "cn lu2", "c2")
+
+        def free_turn():
+            tt(sml[:, 32:40], sml[:, 17:25], sml[:, 0:8], A.mult, "cn fr", "fn")
+            act(T.fb[:], sml[:, 32:48].indirect(L(C8, 8)), "fn lu2", "fb")
+
+        def suitors(out, key, first):
+            if first:
+                held(), left()
+            tt(T.n2[:], cum[:].indirect(L(UE, 8)), T.c2[:], A.is_le, "cum cum0 c2 lu2", "n2")
+            scan(ss[:, 384:512], T.n2[:], dz[:, 256:384], A.mult, A.add, "n2 dz3", "ss3")
+            cp(dz[:, 2:256:16], ss[:, 391:512:8], "ss3", "dz2")
+            scan(ss[:, 512:768], nb[:], dz[:, 0:256], A.mult, A.add, "nb dz dz2", "ss4")
+            cp(out[:], ss[:, 527:768:16], "ss4", key + " " + key + "b")
+
+        if side < 0:
+            free_turn(), free_before(), seats(hl, "hl" + s, True)
+        else:
+            free_before(), run(of_far[:2]), suitors(hl, "hl" + s, True), free_turn()
+            of_far = of_far[2:]
+        send(-side, hl[:], "hl%s hl%sb" % (s, s), hn[:], "ah" + s, "rb" + s)
+        (d1, n1), (d2, n2) = ((T.dn, "dn"), (T.dp, "dp"))[::-side]
+        own, far = (d1, n1, T.al, "al alb"), (d2, n2, hn, "hn" + s)
+        early, late_ = (far, own) if way[side][0] else (own, far)
+
+        def part(b, how, q, o, key):
+            w = how[0][:, 256 * b:256 * b + 256].indirect(how[2][:])
+            (act if q == "s" else cp)(o, w, "%s %s%d" % (how[3], how[1], b), key)
+
+        def blk(buf, b):
+            return buf[:, 256 * b:256 * b + 256]
+
+        run(after[:1] + of_far)
+        if early is far:
+            for b in range(4):
+                part(b, early, "s", blk(T.vg, b), "vg%d" % b)
+        (suitors if side < 0 else seats)(T.al, "al", False)
+        run(after[1:])
         for h in range(2):
             for b in range(4):
-                mm(BANK[1 - h][b], 128, *E(b), xq[:, 128 - 128 * h:256 - 128 * h], xs[:, 128 - 128 * h:256 - 128 * h], "eq%d" % b + XK, True, False)
-        sml, hh, cum, ux = T.sml, T.hh, T.cum, T.ux
-        ts(T.he[:, 0:256], zz[:, 0:208].indirect(L(HS, 16)), 1.0, None, A.is_equal, None, "zz lu", "he")
-        ts(sml[:, 0:8], T.yy[:, 135:192:8], 0.5, None, A.is_lt, None, "yy", "fr")
-        scan(cum[:, 16:272], T.he[:, 0:256], T.he[:, 0:256], A.add, A.max, "he", "cum")
-        scan(T.cn[:, 1:9], sml[:, 0:8], sml[:, 0:8], A.add, A.max, "fr cn", "cn1")
-        act(T.c2[:], T.cn[:].indirect(L(Q7, 8)), "cn1 lu", "c2")
+                mm(4 * h + b, 128, *E(b), xq[:, 128 * h:128 * h + 128], xs[:, 128 * h:128 * h + 128], "eq%d" % b + XK, True, False)
 
-        def seats(out, key):
-            ts(sml[:, 16:24], T.yy[:, 135:192:8], 0.5, -1.0, A.is_lt, A.mult, "yy", "frn")
-            ts(hh[:, 16:208], zz[:, 16:208], 1.0, None, A.is_equal, None, "zz", "hh")
-            tt(T.fn[:, 0:8], T.cn[:, 1:9], sml[:, 16:24], A.mult, "cn1 frn fn", "fn1")
-            tt(T.mm[:, 0:192], hh[:, 16:208], T.tb[:, 0:192], A.mult, "hh tb1", "mm mm2")
-            tt(T.tt[:], T.fn[:].indirect(L(BL, 8)), T.j16[:, 0:128], A.add, "fn1 j16 lu", "tt")
-            tt(hh[:, 208:336], cum[:].indirect(L(CU, 8)), T.tt[:], A.is_gt, "cum cum0 tt lu", "hh2")
-            tt(T.mm[:, 192:320], hh[:, 208:336], T.tb[:, 192:320], A.mult, "hh2 tb2", "mm2")
-            scan(T.ss[:, 0:320], T.rm[:, 0:320], T.mm[:, 0:320], A.mult, A.add, "rm mm mm2", "ss")
-            tt(T.ai[:, 8:16], T.ss[:, 135:192:8], T.ss[:, 207:320:16], A.add, "ss", "ai2")
-            cp(T.ai[:, 0:8], T.ss[:, 15:128:16], "ss", "ai1")
-            cp(out, T.ai[:, 0:16], "ai1 ai2", key)
+        def larger(b):
+            tt(blk(T.zp, b), blk(late_[0], b).indirect(late_[2][:]), blk(T.vg, b), A.max, "%s%d vg%d %s" % (late_[1], b, b, late_[3]), "zp%d" % b)
 
-        def suitors(out, key):
-            tt(ux[:, 16:32], T.i256[:, 1:17], cum[:, 31:272:16], A.subtract, "cum i256", "uu")
-            tt(T.mm[:, 0:128], T.he[:, 0:128], T.ta[:, 0:128], A.mult, "he ta1", "mm mm2")
-            tt(sml[:, 32:48], ux[:, 16:32], ux[:, 15:31], A.subtract, "uu uu0", "un")
-            tt(T.mm[:, 128:256], T.he[:, 128:256], T.ta[:, 128:256], A.mult, "he ta1", "mm1")
-            tt(ux[:, 32:48], ux[:, 16:32], sml[:, 32:48], A.mult, "uu un", "uv")
-            tt(T.he[:, 256:384], ux[:, 32:48].indirect(L(XL, 8)), T.c2[:], A.is_gt, "uv c2 lu", "he2")
-            tt(T.mm[:, 256:384], T.he[:, 256:384], T.ta[:, 256:384], A.mult, "he2 ta2", "mm2")
-            scan(T.ss[:], T.rm[:, 192:576], T.mm[:], A.mult, A.add, "rm mm mm1 mm2", "ss")
-            tt(T.ai[:, 16:32], T.ss[:, 15:256:16], T.ss[:, 263:384:8], A.add, "ss", "ai3")
-            cp(out, T.ai[:, 16:32], "ai3", key)
+        def home(b, h, q, other=False):
+            o, w, key = T.zt[:, 512 * h + b:512 * h + 512:4], blk(T.zp, b).indirect(T.pz[:, 8 * h:8 * h + 8]), "zt%d%d" % (b, h)
+            if other:
+                a = 256 * (b - 2) + 128 * h
+                tt(o, w, T.vc[:, a:a + 128], A.max, "pz zp%d vc%d" % (b, b), key)
+            else:
+                (act if q == "s" else cp)(o, w, "pz zp%d" % b, key)
 
-        (seats if side < 0 else suitors)(hl[:], "hl" + s)
-        send(-side, hl[:], "hl" + s, hn[:], "ah" + s, "rb" + s)
-        far_d(), far_t()
-        (suitors if side < 0 else seats)(T.al[:], "al")
-        (d1, k1), (d2, k2) = ((T.dn, "dn"), (T.dp, "dp"))[::-side]
-        for b in range(4):
-            o, w = T.vg[:, 256 * b:256 * b + 256], d1[:, 256 * b:256 * b + 256].indirect(T.al[:])
-            (act if b % 2 else cp)(o, w, "al %s%d" % (k1, b), "vg%d" % b)
-        if t == 0:
-            quant(T.vq[:], T.vs[:], T.vt[:], "vt", "vq")
-        if t == R - 1:
-            act(T.ab[:], T.i256[:].indirect(T.al[:] if side < 0 else hn[:]), "al i256 hn" + s, "ab")
-        for b in range(4):
-            tt(T.zp[:, 256 * b:256 * b + 256], d2[:, 256 * b:256 * b + 256].indirect(hn[:]), T.vg[:, 256 * b:256 * b + 256], A.max,
-               "%s%d vg%d hn%s" % (k2, b, b, s), "zp%d" % b)
-            if b < 3:
-                act(T.zt[:, b:1024:4], T.zp[:, 256 * b:256 * b + 256].indirect(T.pz[:]), "pz zp%d" % b, "zt%d" % b)
-        if t == R - 1:
-            act(T.wj[:], T.ab[:].indirect(T.pz[:]), "ab pz", "wj")
-            for k in range(8):
-                dma("y", T.ol[k:k + 1, :], T.wj[16 * k:16 * k + 1, :], "sty", "wj", "")
+        def product(h):
+            a = 128 * h
+            quant(T.zq[:, a:a + 128], T.zs[:, a:a + 128], T.zt[:, 4 * a:4 * a + 512], " ".join("zt%d%d" % (b, h) for b in range(4)), "zq%d" % h)
+            for b in range(4):
+                mm(4 * h + b, 128, T.wq[:, 128 * b:128 * b + 128], T.wsc[:, 128 * b:128 * b + 128], T.zq[:, a:a + 128], T.zs[:, a:a + 128],
+                   "wq zq%d" % h, False, True)
+
+        if early is far:
+            for b in range(4):
+                larger(b)
+            home(0, 0, "s"), home(1, 0, "s"), home(2, 0, "v"), home(0, 1, "s"), home(3, 0, "v"), home(1, 1, "s"), product(0)
+            home(2, 1, "s"), home(3, 1, "v"), product(1)
+        else:
+            part(2, early, "v", blk(T.vg, 2), "vg2"), part(3, early, "s", blk(T.vg, 3), "vg3")
+            part(0, early, "v", blk(T.vg, 0), "vg0"), part(1, early, "s", blk(T.vg, 1), "vg1")
+            cp(blk(T.vc, 0), blk(T.vg, 2).indirect(T.pz[:]), "vg2 pz", "vc2")
+            act(blk(T.vc, 1), blk(T.vg, 3).indirect(T.pz[:]), "vg3 pz", "vc3")
+            larger(0), part(2, late_, "s", blk(T.zp, 2), "zp2"), larger(1), part(3, late_, "s", blk(T.zp, 3), "zp3")
+            for h in range(2):
+                home(0, h, "s"), home(2, h, "v", True), home(1, h, "s"), home(3, h, "v", True), product(h)
         s2 = str(t + 1)
         for h in range(2):
             a = 128 * h
-            cp(T.zt[:, 4 * a + 3:4 * a + 512:4], T.zp[:, 768:1024].indirect(T.pz[:, 8 * h:8 * h + 8]), "pz zp3", "zu%d" % h)
-            quant(T.zq[:, a:a + 128], T.zs[:, a:a + 128], T.zt[:, 4 * a:4 * a + 512], "zt0 zt1 zt2 zu%d" % h, "zq%d" % h)
             for b in range(4):
-                mm(BANK[h][b], 128, T.wq[:, 128 * b:128 * b + 128], T.wsc[:, 128 * b:128 * b + 128], T.zq[:, a:a + 128], T.zs[:, a:a + 128],
-                   "wq zq%d" % h, False, True)
-        for h in range(2):
-            a = 128 * h
-            for b in range(4):
-                o, bank, key = T.xn[:, 4 * a + b:4 * a + 512:4], BANK[h][b], "xn%d%d" % (h, b)
-                if b % 2 == 0:
-                    act(o, ps(bank, 0, 128), "ps%d" % bank, key, scale=0.03125)
-                else:
-                    ts(o, ps(bank, 0, 128), 0.03125, None, A.mult, None, "ps%d" % bank, key)
+                scaled(("svsv", "svvv")[h][b], T.xn[:, 4 * a + b:4 * a + 512:4], ps(4 * h + b, 0, 128), "ps%d" % (4 * h + b), "xn%d%d" % (h, b))
             quant(T["xq" + s2][:, a:a + 128], T["xs" + s2][:, a:a + 128], T.xn[:, 4 * a:4 * a + 512],
                   " ".join("xn%d%d" % (h, b) for b in range(4)), ("xq", "xr")[h] + s2)
 
     s = str(R)
     xq, xs = T["xq" + s], T["xs" + s]
-    XK = "xq%s xr%s" % (s, s)
-    mm(2, 128, T.vq[:], T.vs[:], xq[:, 0:128], xs[:, 0:128], "vq xq" + s)
-    mm(3, 128, T.vq[:], T.vs[:], xq[:, 128:256], xs[:, 128:256], "vq xr" + s)
-    act(T.yo[:, 0:128], ps(2, 0, 128), "ps2", "yo1")
-    dma("y", T.oc[:], xq[:].bitcast(dt.uint8), "sty", XK, "")
-    cp(T.yo[:, 128:256], ps(3, 0, 128), "ps3", "yo2")
-    dma("s", T.osc[0:4, :], xs[0:4, :], "sts", XK, "")
-    dma("s", T.y[:], T.yo[:], "sts", "yo1 yo2", "")
-    for k in range(1, 4):
-        dma("y", T.osc[4 * k:4 * k + 4, :], xs[32 * k:32 * k + 4, :], "sty", XK, "")
+    w, wk = (T.al, "al alb") if side < 0 else (hn, "hn%d" % (R - 1))
+    act(T.ab[:], T.px[:].indirect(w[:]), "px " + wk, "ab")
+    for h in range(2):
+        a, key = 128 * h, ("xq", "xr")[h] + s
+        mm(h, 128, T.vq[:], T.vs[:], xq[:, a:a + 128], xs[:, a:a + 128], "vq " + key)
+        dma("y", T.oc[:, 4 * a:4 * a + 512], xq[:, a:a + 128].bitcast(dt.uint8), "sty", key, "")
+        for k in range(4 * h):
+            dma("y", T.osc[4 * k:4 * k + 4, :], xs[32 * k:32 * k + 4, :], "sty", "xq%s xr%s" % (s, s), "")
+    for h in range(2):
+        a = 128 * h
+        cp(T.yo[:, a:a + 128], ps(h, 0, 128), "ps%d" % h, "yo%d" % h)
+    dma("y", T.y[:], T.yo[:], "sty", "yo0 yo1", "")
+    act(T.wj[:], T.ab[:].indirect(T.pz[:]), "ab pz", "wj")
+    dma("s", T.ol[:], T.wj[0:128:16, :], "sts", "wj", "")
     for q in POOL:
         for e in cnt[q][-POOL[q]:]:
             need("g", e)

@@ -5,7 +5,7 @@ R, C = 2, 256
 X4, U8, BF, F32, I32, U16 = "float8_e4m3fn_x4", "uint8", "bfloat16", "float32", "int32", "uint16"
 UP, SEL, AT, XL, YL, LO, HI, TI, TX, PV, PN, PU, VA, CU, C8, Q7, UE, HB, TB, NL = \
     0, 8, 12, 20, 36, 52, 68, 84, 116, 132, 140, 144, 148, 172, 180, 188, 196, 204, 220, 236
-WHO = "sssssbbbvvvvvvvv"
+WHO = "sssssbbvvvvvvvvv"
 NS = WHO.index("v")
 SCRATCH = {}
 for _n, _w, _d in [
@@ -19,9 +19,9 @@ for _n, _w, _d in [
     ("gt", 1024, BF), ("gq", 256, X4), ("gs", 256, U8), ("zt", 1024, BF), ("zq", 256, X4), ("zs", 256, U8), ("xn", 1024, BF),
     ("dn", 1024, BF), ("dp", 1024, BF), ("vg", 1024, BF), ("zp", 1024, BF), ("vc", 512, BF),
     ("li", NL + 4, F32), ("lu", NL + 4, U16), ("pi", 16, I32), ("pc", 64, F32), ("rw", 128, F32), ("tmp", 224, F32), ("tmi", 128, I32),
-    ("j16", 256, BF), ("px", 256, F32), ("eye", 256, F32), ("ne", 256, BF), ("rm", 256, BF), ("r8", 256, BF), ("c12", 256, BF),
-    ("di", 256, BF), ("df", 256, BF), ("sg", 192, BF), ("v0", 144, BF), ("va", 208, BF), ("vb", 208, BF),
-    ("t1", 256, F32), ("t2", 256, F32), ("scn", 256, F32), ("row", 512, F32), ("m", 4096, BF), ("mo", 256 * (16 - NS), BF),
+    ("j16", 256, BF), ("px", 256, F32), ("eye", 256, F32), ("ne", 256, BF), ("rm", 256, BF), ("r8", 512, BF), ("c12", 256, BF),
+    ("di", 512, BF), ("df", 512, BF), ("sg", 64, BF), ("v0", 144, BF), ("va", 208, BF), ("vb", 208, BF),
+    ("t1", 256, F32), ("t2", 256, F32), ("scn", 256, F32), ("row", 512, F32), ("m", 4096, BF), ("mo", 128 * (16 - NS), BF),
     ("acc", 16, F32), ("ec", 256, BF), ("es2", 256, BF), ("e32", 16, F32), ("ri", 112, I32), ("pt", 16, U16), ("pz", 16, U16), ("pm", 256, F32), ("sw", 512, F32),
     ("tr", 512, F32),
     ("sm0", 16, F32), ("sm1", 16, F32), ("oo0", 16, BF), ("oo1", 16, BF), ("hl0", 16, U16), ("hl1", 16, U16),
@@ -35,7 +35,7 @@ for _n, _w, _d in [
     SCRATCH[_n] = ("sbuf", [128, _w], _d)
 SCRATCH["ps"] = ("psum", [128, 4096], F32)
 POOL = {"v": 14, "s": 10, "t": 8, "g": 6}
-SEMAPHORES = [q + str(i) for q in POOL for i in range(POOL[q])] + ["lx", "lu", "lv", "lw", "lp", "loc", "sty", "sts"] + \
+SEMAPHORES = [q + str(i) for q in POOL for i in range(POOL[q])] + ["lx", "lu", "lv", "lw", "lp", "ld", "loc", "sty", "sts"] + \
     [n + str(t) for t in range(R) for n in ("an", "ap", "ab", "ao", "ah", "rq", "rs", "rb", "ro")]
 
 
@@ -133,10 +133,10 @@ def rank_program(g, core, T, topo):
 
     tot = {}
 
-    def dma(q, out, in_, sem, rd, wr):
+    def dma(q, out, in_, sem, rd, wr, how=None):
         rd, wr = rd.split(), wr.split()
         deps(q, rd, wr)
-        Q[q].dma_start(out, in_).then_inc(T.sem[sem], 16)
+        Q[q].dma_start(out, in_, **({"accum_op": how} if how else {})).then_inc(T.sem[sem], 16)
         tot[sem] = tot.get(sem, 0) + 16
         mark(event(sem, tot[sem], known[q], "d"), [], wr)
 
@@ -331,7 +331,6 @@ def rank_program(g, core, T, topo):
     cp(T.ubs[:], T.us[:].indirect(L(UP, 8)), "uq lu0", "ubs")
     ts(tmi[:, 0:16], XU, cl("q3"), 1.0, A.add, A.add, "xu pc", "y2")
     ts(tmi[:, 16:48], n23, cl("q7"), cl("h"), A.add, A.subtract, "n23 pc", "dx")
-    ms(T.va[:], 0.0, "vaL vaU vac"), ms(T.vb[:], 0.0, "vbL vbU vbc"), ms(T.zz[:], 0.0, "zL zU zc")
     quant(T.xq0[:], T.xs0[:], T.xt[:], "xt", "xq0")
     flat(AT, AT + 8, 1, one[:, 0:8], "q7", 8.0, "lat", "v")
     ts(li[:, YL:YL + 16], r82, cl("q7"), None, A.add, None, "r82 pc", "lyl")
@@ -350,46 +349,46 @@ def rank_program(g, core, T, topo):
     aff(x4, n23, -4.0, cl("4h+32"), "n23 4h+32", "x4")
     lt(ts, tmi[:, 56:64], tmp[:, 16:24], 0.25, None, A.mult, None, "x4", "mi2")
     lt(ts, y2, y2, 7, None, A.bitwise_and, None, "y2", "y2")
-    lt(ts, dx, dx, 7, None, A.bitwise_and, None, "dx", "dx")
     lt(ts, m0, mi, 1, None, A.bitwise_and, None, "mi1 mi2", "m0")
     lt(ts, m1, mi, 1, 1, A.logical_shift_right, A.bitwise_and, "mi1 mi2", "m1")
     lt(ts, m2, mi, 2, 1, A.logical_shift_right, A.bitwise_and, "mi1 mi2", "m2")
+    lt(ts, tmp[:, 128:136], tmi[:, 64:72], cl("b2"), None, A.not_equal, None, "m0 pc", "k0a")
+    lt(ts, tmp[:, 136:144], tmi[:, 72:80], cl("b1"), None, A.not_equal, None, "m0 pc", "k0b")
+    lt(ts, tmp[:, 144:152], tmi[:, 80:88], cl("h"), None, A.not_equal, None, "m1 pc", "k1a")
+    lt(ts, tmp[:, 152:160], tmi[:, 88:96], cl("b2"), None, A.not_equal, None, "m1 pc", "k1b")
+    lt(ts, sp, m1, 4.0, -2.0, A.mult, A.add, "m1", "sp")
+    lt(ts, w1, m2, 8.0, -4.0, A.mult, A.add, "m2", "w1")
+    lt(tt, kx, k0, k1, A.max, "k0a k0b k1a k1b", "kx")
+    lt(tt, sp, sp, k0, A.mult, "k0a k0b", "sp")
+    lt(aff, nk, kx, -1.0, 1.0, "kx", "nk")
+    lt(tt, w1, w1, kx, A.mult, "kx", "w1")
+    lt(tt, sp, sp, mi, A.subtract, "mi1 mi2", "sp")
+    lt(ts, dx, dx, 7, None, A.bitwise_and, None, "dx", "dx")
+    lt(tt, sp, sp, w1, A.add, "w1", "sp")
+    lt(aff, tmp[:, 128:136], tmp[:, 176:184], 16.0, cl("q+112"), "sp q+112", "k0a")
+    lt(aff, tmp[:, 156:160], tmp[:, 188:192], -8.0, cl("87-q7"), "sp 87-q7", "k1b")
+    lt(aff, tmp[:, 136:140], tmp[:, 184:188], 16.0, cl("2q7+112"), "sp 2q7+112", "k0b")
+    lt(aff, tmp[:, 140:144], tmp[:, 188:192], 16.0, cl("2q7+113"), "sp 2q7+113 k0b", "k0c")
+    lt(aff, tmp[:, 208:216], tmp[:, 192:200], cl("128(1-o)"), 0.0, "nk 128(1-o)", "w1")
+    lt(aff, tmp[:, 216:220], tmp[:, 200:204], 128.0, 0.0, "nk sp", "w2")
     lt(tt, tmp[:, 112:128], y2, bu, A.add, "y2 bu", "yz")
     lt(tt, x4, x4, dx, A.add, "dx", "x4")
     lt(ts, bv, dx, -1.0, cl("4q7+8"), A.mult, A.add, "dx 4q7+8", "bv")
     lt(ts, gz, dx, 4.0, None, A.is_gt, None, "dx", "gz")
     lt(tt, li[:, LO:LO + 16], XU, tmp[:, 112:128], A.min, "xu yz", "llo")
-    lt(tt, li[:, HI:HI + 16], XU, tmp[:, 112:128], A.max, "xu yz", "lhi")
     lt(tt, bv, bv, x4, A.subtract, "x4", "bv")
-    lt(ts, tmp[:, 128:136], tmi[:, 64:72], cl("b2"), None, A.not_equal, None, "m0 pc", "k0a")
-    lt(ts, tmp[:, 136:144], tmi[:, 72:80], cl("b1"), None, A.not_equal, None, "m0 pc", "k0b")
+    lt(tt, li[:, HI:HI + 16], XU, tmp[:, 112:128], A.max, "xu yz", "lhi")
     lt(tt, bv, bv, gz, A.mult, "gz", "bv")
-    lt(ts, tmp[:, 144:152], tmi[:, 80:88], cl("h"), None, A.not_equal, None, "m1 pc", "k1a")
-    lt(ts, tmp[:, 152:160], tmi[:, 88:96], cl("b2"), None, A.not_equal, None, "m1 pc", "k1b")
-    lt(tt, x4, x4, bv, A.add, "bv", "x4")
-    lt(ts, gz, dx, 0.0, cl("256+q7"), A.is_equal, A.mult, "dx 256+q7", "gz")
-    lt(ts, sp, m1, 4.0, -2.0, A.mult, A.add, "m1", "sp")
     lt(tt, x4, x4, m32, A.add, "m32", "x4")
-    lt(tt, kx, k0, k1, A.max, "k0a k0b k1a k1b", "kx")
-    lt(ts, w1, m2, 8.0, -4.0, A.mult, A.add, "m2", "w1")
-    lt(tt, sp, sp, k0, A.mult, "k0a k0b", "sp")
-    lt(tt, li[:, TI:TI + 32], x4, gz, A.max, "x4 gz", "lti")
-    lt(tt, w1, w1, kx, A.mult, "kx", "w1")
-    lt(tt, sp, sp, mi, A.subtract, "mi1 mi2", "sp")
-    lt(ts, nk, kx, -1.0, 1.0, A.mult, A.add, "kx", "nk")
-    lt(tt, sp, sp, w1, A.add, "w1", "sp")
-    lt(ts, tmp[:, 216:220], tmp[:, 200:204], 128.0, None, A.mult, None, "nk sp", "w2")
-    lt(ts, tmp[:, 128:136], tmp[:, 176:184], 16.0, cl("q+112"), A.mult, A.add, "sp q+112", "k0a")
-    lt(ts, tmp[:, 136:144], tmp[:, 184:192], 16.0, cl("2q7+112"), A.mult, A.add, "sp 2q7+112", "k0b")
-    lt(ts, tmp[:, 156:160], tmp[:, 188:192], -8.0, cl("87-q7"), A.mult, A.add, "sp 87-q7", "k1b")
-    lt(ts, tmp[:, 208:216], tmp[:, 192:200], cl("128(1-o)"), None, A.mult, None, "nk 128(1-o)", "w1")
+    lt(ts, gz, dx, 0.0, cl("256+q7"), A.is_equal, A.mult, "dx 256+q7", "gz")
+    lt(tt, x4, x4, bv, A.add, "bv", "x4")
     lt(tt, tmp[:, 128:136], tmp[:, 128:136], tmp[:, 192:200], A.subtract, "nk", "k0a")
     lt(tt, tmp[:, 156:160], tmp[:, 156:160], tmp[:, 172:176], A.mult, "kx", "k1b")
+    lt(tt, li[:, TI:TI + 32], x4, gz, A.max, "x4 gz", "lti")
     lt(tt, li[:, PV:PV + 12], tmp[:, 128:140], tmp[:, 208:220], A.max, "k0a k0b w1 w2", "lpv")
-    lt(tt, tmp[:, 156:160], tmp[:, 156:160], tmp[:, 140:144], A.add, "k0b", "k1b")
-    lt(ts, li[:, PU:PU + 4], tmp[:, 156:160], 1.0, None, A.add, None, "k1b", "lpu")
+    lt(tt, li[:, PU:PU + 4], tmp[:, 156:160], tmp[:, 140:144], A.add, "k0c k1b", "lpu")
     lt(cp, T.lu[:, AT:VA], li[:, AT:VA], "lat xl lyl llo lhi lti ltx lpv lpu", "lu")
-    slots = [of(lin, "s", "hb0", "q=3", -1.0, "hu"), of(lin, "s", "td", "u", 4.0, "q=3"), of(lin, "s", "32u", "u", 32.0, "hb0"),
+    slots = [of(lin, "s", "2q7+113", "q7", 2.0, 113.0), of(lin, "s", "hb0", "q=3", -1.0, "hu"), of(lin, "s", "td", "u", 4.0, "q=3"), of(lin, "s", "32u", "u", 32.0, "hb0"),
              of(flat, VA, VA + 4, 1, eight, "o", "q1", "lva1"), of(flat, VA + 4, VA + 8, 1, eight, "1-o", "q1", "lva2"),
              of(lin, "s", "hb1", "1-2b2", "h", "32u"),
              of(flat, VA + 8, VA + 16, 2, one[:, 0:4], "vb", 0.0, "lv0"), of(flat, VA + 9, VA + 16, 2, eight, "1-o/2", "vb", "lv1"),
@@ -402,22 +401,26 @@ def rank_program(g, core, T, topo):
 
     def tables():
         sel(T.fe[:], T.ones[:], [[-1, 528]], A.is_equal, 0.0, 3, "ones", "fe", cm=4)
-        sel(T.di[:], one[:], [[0, 4], [-1, 8], [1, 8]], A.not_equal, -1.0, 0, "one", "di")
-        sel(T.df[:], one[:], [[0, 2], [2, 8], [-1, 16]], A.is_ge, -1.0, 0, "one", "df")
-        sel(T.sg[:, 0:64], one[:, 0:64], [[0, 8], [1, 8]], A.is_equal, -1.0, -7, "one", "sgN")
+        for a in (0, 256):
+            sel(T.di[:, a:a + 256], one[:], [[0, 4], [-1, 8], [1, 8]], A.not_equal, -1.0, 0, "one", "di")
+        sel(T.sg[:], one[:, 0:64], [[0, 8], [1, 8]], A.is_equal, -1.0, -7, "one", "sg")
 
     def small():
-        for o, st, w, c, k in ((T.va[:, 128:144], 0, 16, 1, "vac"), (T.v0[:, 128:144], 0, 16, 1, "v0c"), (li[:, C8:C8 + 8], 1, 8, 0, "lc8"),
-                               (T.val[:, 384:400], 0, 16, 0, "valc"), (T.bb[:, 256:272], 1, 16, 0, "bcN"), (T.di[:, 0:256:8], 0, 32, 0, "di"),
-                               (T.sc[:, 15:16], 0, 1, 0, "sc0"), (T.dl[:, 64:145:80], 0, 2, -2, "dlc"), (T.zz[:, 144:160], 0, 16, 5, "zc"),
-                               (T.vb[:, 128:144], 0, 16, 1, "vbc")):
+        for o, st, w, c, k in ((T.va[:, 0:128], 0, 128, 0, "vaL"), (T.va[:, 128:144], 0, 16, 1, "vac"), (T.v0[:, 128:144], 0, 16, 1, "v0c"),
+                               (li[:, C8:C8 + 8], 1, 8, 0, "lc8"), (T.bb[:, 256:272], 1, 16, 0, "bcN"), (T.di[:, 0:512:8], 0, 64, 0, "di"),
+                               (T.sc[:, 15:16], 0, 1, 0, "sc0"), (T.zz[:, 16:144], 0, 128, 0, "zL zL0"), (T.zz[:, 144:160], 0, 16, 5, "zc"),
+                               (T.zz[:, 145:146], 0, 1, 1, "zc"), (T.dl[:, 64:145:80], 0, 2, -2, "dlc"), (T.vb[:, 0:128], 0, 128, 0, "vbL"), (T.vb[:, 128:144], 0, 16, 1, "vbc"),
+                               (T.bb[:, 800:816], 1, 16, 8, "bcF")):
             iota(o, [[st, w]], c, k)
-        sel(T.r8[:], one[:], [[0, 32], [1, 8]], A.not_equal, 0.0, 0, "one", "r8")
-        for o, st, w, c, k in ((T.bb[:, 800:816], 1, 16, 8, "bcF"), (T.df[:, 0:256:16], 0, 16, 0, "df"), (T.dl[:, 288:289], 0, 1, -2, "dlcF")):
+        for a in (0, 256):
+            sel(T.r8[:, a:a + 256], one[:], [[0, 32], [1, 8]], A.not_equal, 0.0, 0, "one", "r8")
+        for a in (0, 256):
+            sel(T.df[:, a:a + 256], one[:], [[0, 2], [2, 8], [-1, 16]], A.is_ge, -1.0, 0, "one", "df")
+        for o, st, w, c, k in ((T.df[:, 0:512:16], 0, 32, 0, "df"), (T.dl[:, 288:289], 0, 1, -2, "dlcF"), (T.val[:, 384:400], 0, 16, 0, "valc"),
+                               (T.va[:, 144:208], 0, 64, 0, "vaU"), (T.vb[:, 144:208], 0, 64, 0, "vbU"), (T.zz[:, 160:224], 0, 64, 0, "zU")):
             iota(o, [[st, w]], c, k)
-        sel(T.sg[:, 64:192], one[:, 0:128], [[0, 8], [1, 16]], A.is_equal, -1.0, -15, "one", "sgF")
         for o, st, w, c, k in ((T.bb[:, 528:544], 1, 16, 0, "bcU"), (T.dts[:], 0, 32, 0, "dts"), (T.sml[:], 0, 48, -1, "sml"),
-                               (T.zz[:, 145:146], 0, 1, 1, "zc"), (T.cum[:, 0:16], 0, 16, -1, "cum0"), (T.na[:, 131:384:4], 0, 64, 1, "nac"),
+                               (T.cum[:, 0:16], 0, 16, -1, "cum0"), (T.na[:, 131:384:4], 0, 64, 1, "nac"),
                                (T.c12[:], 0, 256, 0, "c12"), (T.c12[:, 0:256:16], 0, 16, -12, "c12")):
             iota(o, [[st, w]], c, k)
 
@@ -433,6 +436,9 @@ def rank_program(g, core, T, topo):
         send_x(t)
         if t == 0:
             tables()
+        else:
+            ms(T.va[:, 0:128], 0.0, "vaL"), ms(T.va[:, 144:208], 0.0, "vaU")
+            quant(T.vq[:], T.vs[:], T.vt[:], "vt", "vq")
         act(T.t2[:], ps(1, 0, 256), "ps1", "t2", f=F.Abs, scale=1.25 * 2.0 ** -24, bias=2.0 ** -120)
         tt(T.t1[:], ps(0, 0, 256), T.eye[:], A.mult, "ps0 eye", "t1")
         act(T.row[:, 0:256], ps(1, 0, 256), "ps1", "row")
@@ -452,7 +458,8 @@ def rank_program(g, core, T, topo):
         def count(c):
             w = T.m[:, 256 * c:256 * c + 256]
             if WHO[c] == "v":
-                scan(T.mo[:, 256 * (c - NS):256 * (c - NS) + 256], w, w, A.add, A.max, "m%d" % c, "mo%d" % c)
+                scan(T.mo[:, 128 * (c - NS):128 * (c - NS) + 128], T.m[:, 256 * c:256 * c + 128], T.m[:, 256 * c + 128:256 * c + 256],
+                     A.add, A.add, "m%d" % c, "mo%d" % c)
             else:
                 act(w, w, "", "m%d ar%d" % (c, c), f=F.Relu, scale=-32.0 if WHO[c] == "s" else 1.0, accum_out=acc[:, c:c + 1])
 
@@ -477,7 +484,7 @@ def rank_program(g, core, T, topo):
                 count(c - 1)
             run(equal[c - NS:c - NS + 1])
         tt(ri[:, 0:NS], acc[:, 0:NS], e32[:, 0:NS], A.add, "e32 " + " ".join("ar%d" % c for c in range(NS)), "xb")
-        tt(ri[:, NS:16], T.mo[:, 255:256 * (16 - NS):256], e32[:, NS:16], A.add, "e32 " + " ".join("mo%d" % c for c in range(NS, 16)), "xa")
+        tt(ri[:, NS:16], T.mo[:, 127:128 * (16 - NS):128], e32[:, NS:16], A.add, "e32 " + " ".join("mo%d" % c for c in range(NS, 16)), "xa")
         ts(ri[:, 16:32], ri[:, 0:16], 9, None, A.logical_shift_right, None, "xa xb", "hi")
         ts(ri[:, 32:48], ri[:, 0:16], 496, None, A.bitwise_and, None, "xa xb", "lo")
         ts(ri[:, 64:80], ri[:, 0:16], 480, None, A.bitwise_and, None, "xa xb", "r16")
@@ -496,9 +503,9 @@ def rank_program(g, core, T, topo):
         dts, val, da, dz = T.dts, T.val, T.da, T.dz
         of_so = [of(act, val[:, 0:128], so[:].indirect(L(VA, 8)), "lu2 " + sk, "val1"),
                  of(act, val[:, 128:384], so[:].indirect(L(VA + 8, 16)), "lu2 " + sk, "val2"),
-                 of(tt, da[:], val[:, 0:384], val[:, 1:385], A.subtract, "val1 val2 valc", "da"),
-                 of(cp, da[:, 15:128:16], val[:, 15:128:16], "val1 da", "da1"),
-                 of(cp, da[:, 159:384:32], val[:, 159:384:32], "val2 da", "da2")]
+                 of(aff, da[:], val[:, 1:385], -1.0, 0.0, "val1 val2 valc", "da"),
+                 of(iota, da[:, 15:128:16], [[0, 8]], 0, "da"), of(iota, da[:, 159:384:32], [[0, 8]], 0, "da"),
+                 of(dma, "g", da[:], val[:, 0:384], "ld", "val1 val2", "da", A.add)]
         of_to = [of(tt, dts[:, 0:15], to[:, 0:15], to[:, 1:16], A.subtract, tk, "dts"),
                  of(tt, dts[:, 16:23], to[:, 8:15], to[:, 9:16], A.subtract, tk, "dt1"),
                  of(ts, dts[:, 24:26], to[:, 8:16:4], -1.0, None, A.mult, None, tk, "dt2"),
@@ -506,7 +513,6 @@ def rank_program(g, core, T, topo):
                  of(ts, dts[:, 11:16:4], to[:, 11:16:4], to[:, 0:1], None, A.subtract, None, "dts " + tk, "dt4"),
                  of(act, dz[:, 0:256], dts[:].indirect(L(TB, 16)), "lu2 dts dt1 dt2 dt3 dt4", "dz dz2"),
                  of(act, dz[:, 256:384], dts[:, 16:32].indirect(L(Q7, 8)), "lu2 dts dt1 dt2 dt3 dt4", "dz3")]
-        of_own, of_far = (of_so, of_to) if side < 0 else (of_to, of_so)
 
         def out_of(q, sc, key, bank, dst, qs):
             fs = [lambda: [mm(bank + b, 256, *E(b), q[:], sc[:], "eq%d %s" % (b, key)) for b in range(4)]]
@@ -529,27 +535,23 @@ def rank_program(g, core, T, topo):
         if t == 0:
             small()
             run([of(quant, *E(b), T.fe[:, 3 - b:515 - b], "fe", "eq%d" % b) for b in range(4)])
-            soon, again = (from_prev("ssss"), once_more("ssss")) if way[-1][0] else ([], [])
-            run(slots[:-1] + soon[:5] + late[:10] + slots[-1:] + of_own[:2] + late[10:20] + soon[5:] + again + late[20:])
+            soon, again = (from_prev("ssss"), once_more("ssvv")) if way[-1][0] else ([], [])
+            run(slots[:-1] + soon[:5] + late[:26] + soon[5:] + again[:3] + late[26:] + slots[-1:])
             run(mine)
             act(T.v0[:, 0:128], T.va[:, 0:144].indirect(L(PV, 8)), "vaL vac lu", "v0L")
-            run(of_own[2:])
+            run(again[3:])
             aff(T.r0[:], T.v0[:].indirect(L(PN, 4)), -8.0, 9.0, "lu v0L v0c", "r0")
             during = from_next("ssss")
             if not soon:
                 after = from_prev("svsv") + once_more("svsv")
         else:
-            ms(T.va[:, 0:128], 0.0, "vaL"), ms(T.va[:, 144:208], 0.0, "vaU")
-            a, b = from_prev("ssss"), from_next("ssvv")
-            run(a[:5] + b[:3] + mine + of_own[:5] + a[5:] + of_own[5:] + b[3:])
-            during = once_more("ssss")
-            if not way[-side][0]:
-                during[0]()
-                during = [lambda: None] + during[1:]
+            a, b = from_prev("ssss"), from_next("ssss")
+            if way[-side][0]:
+                run(a[:5] + mine + a[5:] + once_more("svsv"))
+                during = b
             else:
-                run(during)
-                during = []
-            quant(T.vq[:], T.vs[:], T.vt[:], "vt", "vq")
+                run(a[:5] + b[:3] + mine + a[5:])
+                during = b[3:] + once_more("ssss")
 
         gg, gh, bb, bt, sc, kn, dl, db, yy, zz = T.gg, T.gh, T.bb, T.bt, T.sc, T.kn, T.dl, T.db, T.yy, T.zz
         SETS = {"N": 0, "U": 1, "F": 2}
@@ -574,25 +576,34 @@ def rank_program(g, core, T, topo):
             o = bt[:, 1025 + 512 * h:1536 + 512 * h:2] if k == "F" else bt[:, 512 * i + 256 * h:512 * i + 256 * h + 256]
             scaled(q, o, bb[:, 272 * i:272 * i + 272].indirect(L(TI + 16 * h, 16)), "lu bc%s b%s" % (k, k), "t%s%d" % (k, h))
 
-        def wins(k, h):
-            a, b = SUMS[k] + 256 * h, 512 * SETS[k] + 256 * h
+        def wins(k, h=0):
+            a, b = SUMS[k] + 512 * h, 512 * SETS[k] + 512 * h
             if k == "F":
-                scan(sc[:, a:a + 256], T.df[:], bt[:, b:b + 256], A.mult, A.add, "df tF%d tX%d" % (h // 2, h // 2), "wF%d" % h)
+                scan(sc[:, a:a + 512], T.df[:], bt[:, b:b + 512], A.mult, A.add, "df tF%d tX%d" % (h, h), "wF%d" % h)
             else:
-                scan(sc[:, a:a + 256], T.di[:], bt[:, b:b + 256], A.mult, A.add, "di t%s%d" % (k, h), "w%s%d" % (k, h))
+                scan(sc[:, a:a + 512], T.di[:], bt[:, b:b + 512], A.mult, A.add, "di t%s0 t%s1" % (k, k), "w" + k)
 
         def step(k):
             a, b = 80 * SETS[k], SUMS[k]
-            tt(dl[:, a:a + 64], sc[:, b - 1:b + 504:8], sc[:, b + 7:b + 512:8], A.subtract, "sc0 wF3 w%s0 w%s1" % (k, k), "dl" + k)
+            tt(dl[:, a:a + 64], sc[:, b - 1:b + 504:8], sc[:, b + 7:b + 512:8], A.subtract, "sc0 wF1 w" + k, "dl" + k)
 
         def anew(k):
             a = 80 * SETS[k]
             ms(dl[:, a:a + 128:16] if k == "F" else dl[:, a:a + 64:8], -2.0, "dl" + k)
 
         def back(k):
-            i = SETS[k]
-            w, a = (128, 64) if k == "F" else (64, 0)
-            tt(db[:, 64 * i:64 * i + w], dl[:, 80 * i + 1:80 * i + w + 1], T.sg[:, a:a + w], A.mult, "dlc dlcF sgN sgF dlF2 dl" + k, "db" + k)
+            i, w = SETS[k], 128 if k == "F" else 64
+            o, d = db[:, 64 * i:64 * i + w], dl[:, 80 * i + 1:80 * i + w + 1]
+            if k == "N":
+                tt(o, d, T.sg[:], A.mult, "dlc sg dlN", "dbN")
+            else:
+                aff(o, d, -1.0, 0.0, "dlc dlcF dlF2 dl" + k, "db" + k)
+
+        def ends(k):
+            if k == "F":
+                ms(db[:, 143:256:16], -2.0, "dbF")
+            else:
+                iota(db[:, 71:128:8], [[0, 8]], -2, "dbU")
 
         def far_of(h):
             act(gh[:, 768 + 256 * h:1024 + 256 * h], T.dd[:, 64 + 32 * h:96 + 32 * h].indirect(L(YL, 16)), "lu ddF", "ghX%d" % h, f=F.Abs)
@@ -601,16 +612,15 @@ def rank_program(g, core, T, topo):
             tt(bb[:, 816 + 256 * h:1072 + 256 * h], gg[:, 32 * h:32 * h + 32].indirect(L(XL, 16)), gh[:, 768 + 256 * h:1024 + 256 * h],
                A.is_lt if h else A.is_le, "lu ggN ghX%d" % h, "bX%d" % h)
 
-        def rows(h):
-            a = SUMS["X"] + 256 * h
-            scan(sc[:, a:a + 256], T.r8[:], bb[:, 816 + 256 * h:1072 + 256 * h], A.mult, A.add, "r8 bX%d" % h, "wX%d" % h)
+        def rows():
+            scan(sc[:, SUMS["X"]:SUMS["X"] + 512], T.r8[:], bb[:, 816:1328], A.mult, A.add, "r8 bX0 bX1", "wX")
 
         def turn_x(h):
             scaled("s", bt[:, 1024 + 512 * h:1536 + 512 * h:2], bb[:, 816 + 256 * h:1072 + 256 * h].indirect(L(TX, 16)), "lu bX%d" % h, "tX%d" % h)
 
-        near = [of(scaled, "v", kn[:, 64:128], sc[:, SUMS["X"] + 7:SUMS["X"] + 512:8], "wX0 wX1", "x32"),
-                of(tt, kn[:, 0:64], sc[:, 23:528:8], kn[:, 64:128], A.add, "wN0 wN1 x32", "kn")]
-        WF = "kn wN1 wF0 wF1 wF2 wF3"
+        near = [of(scaled, "s", kn[:, 64:128], sc[:, SUMS["X"] + 7:SUMS["X"] + 512:8], "wX", "x32"),
+                of(tt, kn[:, 0:64], sc[:, 23:528:8], kn[:, 64:128], A.add, "wN x32", "kn")]
+        WF = "kn wN wF0 wF1"
         whole = [of(tt, dl[:, 160:288:2], sc[:, 527:1536:16], kn[:, 0:64], A.subtract, WF, "dlF"),
                  of(tt, dl[:, 161:288:2], kn[:, 0:64], sc[:, 543:1552:16], A.subtract, WF, "dlF2"), of(anew, "F")]
 
@@ -646,7 +656,7 @@ def rank_program(g, core, T, topo):
             dst, dn_ = state(k + 1)
             lst, w, a, b, st, win = MOVE[p]
             r, rk = (T.r0[:], "r0") if k == 0 else (T.rr[:, a:a + 16 * w], "rr" + "LU"[p == "U"])
-            tt(dst[:, a:b:st], zz[:, 16:16 + win].indirect(L(lst, w)), r, A.is_gt, rk + " lu zL zc" + " zU" * (p == "U"), dn_ + "LU"[p == "U"])
+            tt(dst[:, a:b:st], zz[:, 16:16 + win].indirect(L(lst, w)), r, A.is_gt, rk + " lu zL zL0 zc" + " zU" * (p == "U"), dn_ + "LU"[p == "U"])
 
         dist("N"), high("N")
         ts(T.dd[:, 192:256], T.dd[:, 0:64], -1.0, None, A.mult, None, "ddN", "nd")
@@ -654,21 +664,18 @@ def rank_program(g, core, T, topo):
         tt(gg[:, 0:64], T.dd[:, 0:64], T.dd[:, 192:256], A.max, "ddN nd", "ggN")
         far_of(0), beat("N"), turn("N", 0), turn("N", 1, "v")
         act(gg[:, 64:192], T.dd[:, 64:192], "ddF", "ggF", f=F.Abs)
-        high("F"), cross(0), wins("N", 1), wins("N", 0), far_of(1), rows(0), step("N"), turn_x(0), anew("N")
-        FORTH = {0: [of(back, "N")], 2: [of(wins, "F", 0)], 3: near[1:], 4: [of(back, "F")], 7: [of(wins, "U", 1)]}
-        BACK = {0: [of(beat, "F")], 1: [of(cross, 1)], 2: [of(wins, "F", 1)], 4: [of(beat, "U")], 6: [of(wins, "U", 0)], 7: [of(step, "U")]}
-        MOVED = {1: [of(rows, 1), of(turn, "F", 0), of(turn_x, 1)], 2: near[:1] + [of(turn, "F", 1)],
-                 3: [of(wins, "F", 2), of(wins, "F", 3), of(high, "U")] + whole,
-                 5: [of(turn, "U", 0)], 6: [of(turn, "U", 1)], 7: [of(anew, "U"), of(back, "U")]}
-        if during:
-            MOVED[4] = during[0:2]
-            MOVED[7] += during[2:3]
-            MOVED[8], MOVED[9] = during[3:4], during[4:5]
-        if t == 0 and not after:
-            MOVED[8] += of_far[0:3]
-            MOVED[9] += of_far[3:5]
-            MOVED[10] = of_far[5:7]
-            of_far = []
+        high("F"), cross(0), wins("N"), far_of(1), step("N"), turn_x(0), beat("F")
+        ts(zz[:, 18:144:4], dl[:, 1:64:2], 1.0, None, A.add, None, "dlN", "zL")
+        ts(zz[:, 16:144:4], dl[:, 1:64:2], -1.0, 1.0, A.mult, A.add, "dlN", "zL0")
+        anew("N")
+        FORTH = {2: [of(wins, "F", 0)], 3: near[1:], 4: [of(beat, "U"), of(ends, "F")], 5: of_to[1:2], 6: of_to[4:5],
+                 7: [of(anew, "U"), of(back, "U"), of(ends, "U")]}
+        BACK = {1: [of(cross, 1)], 4: of_to[0:1], 5: of_to[2:3], 6: of_so[2:] + [of(wins, "U")]}
+        MOVED = {0: [of(back, "N"), of_so[0], of(turn, "F", 0)], 1: [rows, of(turn_x, 1)], 2: near[:1] + [of(turn, "F", 1)],
+                 3: [of(wins, "F", 1), of(high, "U"), of_so[1]] + whole + [of(back, "F")],
+                 4: [of(turn, "U", 0)], 5: [of_to[3], of(turn, "U", 1)], 6: [of(step, "U")], 8: of_to[5:6], 9: of_to[6:7],
+                 10: during[:4]}
+        during = during[4:]
         for k in range(12):
             p = "N" if k < 4 else "F"
             to_ = "N" if k < 3 else "F"
@@ -678,13 +685,15 @@ def rank_program(g, core, T, topo):
                 stood(k, "U")
             if k == 11:
                 forth(k, "U")
-            forth(k, p)
+            if k:
+                forth(k, p)
             if 7 < k < 11:
                 forth(k, "U")
             if k == 11:
                 ts(T.sml[:, 0:8], yy[:, 135:192:8], 0.5, None, A.is_lt, None, "yU sml", "fr")
             run(FORTH.get(k, []))
-            backw(p)
+            if k:
+                backw(p)
             if k > 7:
                 backw("U")
             run(BACK.get(k, []))
@@ -710,8 +719,8 @@ def rank_program(g, core, T, topo):
                 left()
             ts(na[:, 129:384:4], zz[:, 160:224], 1.0, None, A.not_equal, None, "zU", "na2")
             tt(na[:, 128:384:2], cum[:].indirect(L(CU, 8)), T.fb[:], A.is_ge, "cum cum0 fb lu2", "na3")
-            scan(ss[:, 0:128], na[:, 0:128], da[:, 0:128], A.mult, A.add, "na1 da da1", "ss1")
-            scan(ss[:, 128:384], na[:, 128:384], da[:, 128:384], A.mult, A.add, "na2 na3 nac da da2", "ss2")
+            scan(ss[:, 0:128], na[:, 0:128], da[:, 0:128], A.mult, A.add, "na1 da", "ss1")
+            scan(ss[:, 128:384], na[:, 128:384], da[:, 128:384], A.mult, A.add, "na2 na3 nac da", "ss2")
             cp(out[:, 0:8], ss[:, 15:128:16], "ss1", key)
             cp(out[:, 8:16], ss[:, 159:384:32], "ss2", key + "b")
 
@@ -731,15 +740,8 @@ def rank_program(g, core, T, topo):
             scan(ss[:, 512:768], nb[:], dz[:, 0:256], A.mult, A.add, "nb dz dz2", "ss4")
             cp(out[:], ss[:, 527:768:16], "ss4", key + " " + key + "b")
 
-        if side < 0:
-            free_turn(), free_before(), seats(hl, "hl" + s, True)
-        else:
-            free_before(), run(of_far[:2]), suitors(hl, "hl" + s, True), free_turn()
-            of_far = of_far[2:]
-        send(-side, hl[:], "hl%s hl%sb" % (s, s), hn[:], "ah" + s, "rb" + s)
         (d1, n1), (d2, n2) = ((T.dn, "dn"), (T.dp, "dp"))[::-side]
         own, far = (d1, n1, T.al, "al alb"), (d2, n2, hn, "hn" + s)
-        early, late_ = (far, own) if way[side][0] else (own, far)
 
         def part(b, how, q, o, key):
             w = how[0][:, 256 * b:256 * b + 256].indirect(how[2][:])
@@ -748,26 +750,37 @@ def rank_program(g, core, T, topo):
         def blk(buf, b):
             return buf[:, 256 * b:256 * b + 256]
 
-        run(after[:1] + of_far)
-        if early is far:
-            for b in range(4):
-                part(b, early, "s", blk(T.vg, b), "vg%d" % b)
-        (suitors if side < 0 else seats)(T.al, "al", False)
+        def column(b, q):
+            (act if q == "s" else cp)(blk(T.vc, b - 2), blk(T.vg, b).indirect(T.pz[:]), "vg%d pz" % b, "vc%d" % b)
+
+        selfish = t < R - 1 and not way[marks_side(t + 1)][0]
+        if selfish:
+            free_before(), free_turn(), run(during), suitors(T.al, "al", True)
+            part(2, own, "s", blk(T.vg, 2), "vg2"), part(3, own, "s", blk(T.vg, 3), "vg3"), column(3, "s"), part(1, own, "s", blk(T.vg, 1), "vg1")
+            seats(hl, "hl" + s, False)
+        elif side < 0:
+            free_turn(), free_before(), run(during), seats(hl, "hl" + s, True)
+        else:
+            free_before(), run(during), suitors(hl, "hl" + s, True), free_turn()
+        send(-side, hl[:], "hl%s hl%sb" % (s, s), hn[:], "ah" + s, "rb" + s)
+        run(after[:1])
+        if not selfish:
+            (suitors if side < 0 else seats)(T.al, "al", False)
         run(after[1:])
         for h in range(2):
             for b in range(4):
                 mm(4 * h + b, 128, *E(b), xq[:, 128 * h:128 * h + 128], xs[:, 128 * h:128 * h + 128], "eq%d" % b + XK, True, False)
 
         def larger(b):
-            tt(blk(T.zp, b), blk(late_[0], b).indirect(late_[2][:]), blk(T.vg, b), A.max, "%s%d vg%d %s" % (late_[1], b, b, late_[3]), "zp%d" % b)
+            tt(blk(T.zp, b), blk(far[0], b).indirect(far[2][:]), blk(T.vg, b), A.max, "%s%d vg%d %s" % (far[1], b, b, far[3]), "zp%d" % b)
 
-        def home(b, h, q, other=False):
+        def home(b, h):
             o, w, key = T.zt[:, 512 * h + b:512 * h + 512:4], blk(T.zp, b).indirect(T.pz[:, 8 * h:8 * h + 8]), "zt%d%d" % (b, h)
-            if other:
+            if b > 1:
                 a = 256 * (b - 2) + 128 * h
                 tt(o, w, T.vc[:, a:a + 128], A.max, "pz zp%d vc%d" % (b, b), key)
             else:
-                (act if q == "s" else cp)(o, w, "pz zp%d" % b, key)
+                act(o, w, "pz zp%d" % b, key)
 
         def product(h):
             a = 128 * h
@@ -776,43 +789,34 @@ def rank_program(g, core, T, topo):
                 mm(4 * h + b, 128, T.wq[:, 128 * b:128 * b + 128], T.wsc[:, 128 * b:128 * b + 128], T.zq[:, a:a + 128], T.zs[:, a:a + 128],
                    "wq zq%d" % h, False, True)
 
-        if early is far:
-            for b in range(4):
-                larger(b)
-            home(0, 0, "s"), home(1, 0, "s"), home(2, 0, "v"), home(0, 1, "s"), home(3, 0, "v"), home(1, 1, "s"), product(0)
-            home(2, 1, "s"), home(3, 1, "v"), product(1)
-        else:
-            part(2, early, "v", blk(T.vg, 2), "vg2"), part(3, early, "s", blk(T.vg, 3), "vg3")
-            part(0, early, "v", blk(T.vg, 0), "vg0"), part(1, early, "s", blk(T.vg, 1), "vg1")
-            cp(blk(T.vc, 0), blk(T.vg, 2).indirect(T.pz[:]), "vg2 pz", "vc2")
-            act(blk(T.vc, 1), blk(T.vg, 3).indirect(T.pz[:]), "vg3 pz", "vc3")
-            larger(0), part(2, late_, "s", blk(T.zp, 2), "zp2"), larger(1), part(3, late_, "s", blk(T.zp, 3), "zp3")
-            for h in range(2):
-                home(0, h, "s"), home(2, h, "v", True), home(1, h, "s"), home(3, h, "v", True), product(h)
+        if not selfish:
+            part(2, own, "v", blk(T.vg, 2), "vg2"), part(3, own, "s", blk(T.vg, 3), "vg3"), part(1, own, "s", blk(T.vg, 1), "vg1")
+            column(3, "s")
+        part(0, own, "v", blk(T.vg, 0), "vg0"), column(2, "v")
+        larger(0), part(2, far, "s", blk(T.zp, 2), "zp2"), larger(1), part(3, far, "s", blk(T.zp, 3), "zp3")
+        home(0, 0), home(2, 0), home(1, 0), home(3, 0), home(2, 1), product(0), home(0, 1), home(1, 1), home(3, 1), product(1)
         s2 = str(t + 1)
         for h in range(2):
             a = 128 * h
             for b in range(4):
-                scaled(("svsv", "svvv")[h][b], T.xn[:, 4 * a + b:4 * a + 512:4], ps(4 * h + b, 0, 128), "ps%d" % (4 * h + b), "xn%d%d" % (h, b))
+                scaled("svsv"[b], T.xn[:, 4 * a + b:4 * a + 512:4], ps(4 * h + b, 0, 128), "ps%d" % (4 * h + b), "xn%d%d" % (h, b))
             quant(T["xq" + s2][:, a:a + 128], T["xs" + s2][:, a:a + 128], T.xn[:, 4 * a:4 * a + 512],
                   " ".join("xn%d%d" % (h, b) for b in range(4)), ("xq", "xr")[h] + s2)
 
     s = str(R)
     xq, xs = T["xq" + s], T["xs" + s]
     w, wk = (T.al, "al alb") if side < 0 else (hn, "hn%d" % (R - 1))
-    act(T.ab[:], T.px[:].indirect(w[:]), "px " + wk, "ab")
     for h in range(2):
         a, key = 128 * h, ("xq", "xr")[h] + s
         mm(h, 128, T.vq[:], T.vs[:], xq[:, a:a + 128], xs[:, a:a + 128], "vq " + key)
         dma("y", T.oc[:, 4 * a:4 * a + 512], xq[:, a:a + 128].bitcast(dt.uint8), "sty", key, "")
-        for k in range(4 * h):
-            dma("y", T.osc[4 * k:4 * k + 4, :], xs[32 * k:32 * k + 4, :], "sty", "xq%s xr%s" % (s, s), "")
-    for h in range(2):
-        a = 128 * h
-        cp(T.yo[:, a:a + 128], ps(h, 0, 128), "ps%d" % h, "yo%d" % h)
+        (cp if h else act)(T.yo[:, a:a + 128], ps(h, 0, 128), "ps%d" % h, "yo%d" % h)
     dma("y", T.y[:], T.yo[:], "sty", "yo0 yo1", "")
-    act(T.wj[:], T.ab[:].indirect(T.pz[:]), "ab pz", "wj")
-    dma("s", T.ol[:], T.wj[0:128:16, :], "sts", "wj", "")
+    act(T.ab[:], T.px[:].indirect(w[:]), "px " + wk, "ab")
+    cp(T.wj[:], T.ab[:].indirect(T.pz[:]), "ab pz", "wj")
+    for k in range(4):
+        dma("s", T.osc[4 * k:4 * k + 4, :], xs[32 * k:32 * k + 4, :], "sts", "xq%s xr%s" % (s, s), "")
+    dma("y", T.ol[:], T.wj[0:128:16, :], "sty", "wj", "")
     for q in POOL:
         for e in cnt[q][-POOL[q]:]:
             need("g", e)

from concourse.bass import DstId, RemoteDMATransfer
from concourse.mybir import dt, AluOpType as A, ActivationFunctionType as F

R, C = 2, 256
X4, U8, BF, F32, I32, U16 = "float8_e4m3fn_x4", "uint8", "bfloat16", "float32", "int32", "uint16"
UP, SEL, AT, XL, YL, LO, HI, TI, TX, PV, PN, PU, VA, CU, C8, Q7, UE, HB, TB, NL = \
    0, 8, 12, 20, 36, 52, 68, 84, 116, 132, 140, 144, 148, 172, 180, 188, 196, 204, 220, 236
WHO = "sssssbbvvvvvvvvv"
NS = WHO.index("v")
SCRATCH = {}
for _n, _w, _d in [
    ("xt", 1024, BF), ("ut", 512, BF), ("vt", 512, BF), ("uq", 128, X4), ("us", 128, U8), ("ub", 128, X4), ("ubs", 128, U8),
    ("vq", 128, X4), ("vs", 128, U8), ("wq", 512, X4), ("wsc", 512, U8), ("eq", 512, X4), ("es", 512, U8),
    ("ones", 528, BF), ("one", 256, BF), ("fe", 528, BF),
    ("xq0", 256, X4), ("xs0", 256, U8), ("xq1", 256, X4), ("xs1", 256, U8), ("xq2", 256, X4), ("xs2", 256, U8),
    ("nq0", 256, X4), ("ns0", 256, U8), ("nq1", 256, X4), ("ns1", 256, U8),
    ("pq0", 256, X4), ("pr0", 256, U8), ("pq1", 256, X4), ("pr1", 256, U8),
    ("rq0", 256, X4), ("rs0", 256, U8), ("rq1", 256, X4), ("rs1", 256, U8),
    ("gt", 1024, BF), ("gq", 256, X4), ("gs", 256, U8), ("zt", 1024, BF), ("zq", 256, X4), ("zs", 256, U8), ("xn", 1024, BF),
    ("dn", 1024, BF), ("dp", 1024, BF), ("vg", 1024, BF), ("zp", 1024, BF), ("vc", 512, BF),
    ("li", NL + 4, F32), ("lu", NL + 4, U16), ("pi", 16, I32), ("pc", 64, F32), ("rw", 128, F32), ("tmp", 224, F32), ("tmi", 128, I32),
    ("j16", 256, BF), ("px", 256, F32), ("eye", 256, F32), ("ne", 256, BF), ("rm", 256, BF), ("r8", 512, BF), ("c12", 256, BF),
    ("di", 512, BF), ("df", 512, BF), ("sg", 64, BF), ("v0", 144, BF), ("va", 208, BF), ("vb", 208, BF),
    ("t1", 256, F32), ("t2", 256, F32), ("scn", 256, F32), ("row", 512, F32), ("m", 4096, BF), ("mo", 128 * (16 - NS), BF),
    ("acc", 16, F32), ("ec", 256, BF), ("es2", 256, BF), ("e32", 16, F32), ("ri", 112, I32), ("pt", 16, U16), ("pz", 16, U16), ("pm", 256, F32), ("sw", 512, F32),
    ("tr", 512, F32),
    ("sm0", 16, F32), ("sm1", 16, F32), ("oo0", 16, BF), ("oo1", 16, BF), ("hl0", 16, U16), ("hl1", 16, U16),
    ("bn0", 16, F32), ("bn1", 16, F32), ("on0", 16, BF), ("on1", 16, BF), ("hn0", 16, U16), ("hn1", 16, U16),
    ("at", 192, F32), ("dd", 256, F32), ("gg", 192, F32), ("gh", 1280, F32), ("bb", 1328, BF), ("bt", 2048, BF), ("sc", 2576, BF),
    ("kn", 128, BF), ("dl", 304, BF), ("db", 256, BF), ("yy", 192, BF), ("zz", 224, BF), ("r0", 64, BF), ("rr", 208, BF),
    ("na", 384, BF), ("nb", 256, BF), ("val", 400, BF), ("da", 384, BF), ("dts", 32, BF), ("dz", 384, BF), ("cum", 272, BF),
    ("sml", 48, BF), ("fb", 128, BF), ("c2", 128, BF), ("n2", 128, BF), ("ss", 768, BF), ("al", 16, U16),
    ("ab", 256, BF), ("wj", 256, F32), ("yo", 256, F32),
]:
    SCRATCH[_n] = ("sbuf", [128, _w], _d)
SCRATCH["ps"] = ("psum", [128, 4096], F32)
POOL = {"v": 14, "s": 10, "t": 8, "g": 6}
SEMAPHORES = [q + str(i) for q in POOL for i in range(POOL[q])] + ["lx", "lu", "lv", "lw", "lp", "ld", "loc", "sty", "sts"] + \
    [n + str(t) for t in range(R) for n in ("an", "ap", "ab", "ao", "ah", "rq", "rs", "rb", "ro")]


def relays_of(c, d, T, topo):
    ok = [e for e in topo.cores_of(c) if T.rank_of(e) is None and topo.may_write(e, d)]
    return sorted(ok, key=lambda e: topo.die(e) != topo.die(c))[:2]


def bits(es):
    return sum(1 << e for e in es)


def marks_side(t):
    return 1 if t % 2 else -1


def landing(T, side, s):
    return (T["pq" + s], T["pr" + s], "ap" + s) if side == 1 else (T["nq" + s], T["ns" + s], "an" + s)


def hand_on(g, core, T, topo):
    n = len(T.cores)
    for r in range(n):
        for side in (1, -1):
            c, d = T.cores[r], T.cores[(r + side) % n]
            if topo.may_write(c, d) or core not in relays_of(c, d, T, topo):
                continue
            rid, pid = topo.addr(d, core)
            mask, k = topo.mask(core, d), len(topo.engines(core, d))
            sent = 0
            for t in range(R):
                s = str(t)
                q, sc, far = landing(T, side, s)
                if core == relays_of(c, d, T, topo)[0]:
                    msgs = [("rq", q[:].bitcast(dt.uint8), T["rq" + s][:].bitcast(dt.uint8), far)]
                else:
                    msgs = [("rs", sc[:], T["rs" + s][:], far)]
                    if side != marks_side(t):
                        msgs += [("rb", T["hn" + s][:], T["hn" + s][:], "ah" + s)]
                    else:
                        msgs += [("rb", T["bn" + s][:], T["bn" + s][:], "ab" + s), ("ro", T["on" + s][:], T["on" + s][:], "ao" + s)]
                for w, o, i, far in msgs:
                    g.wait_ge(T.sem[w + s], 8 if w in ("rq", "rs") else len(topo.engines(c, core)))
                    g.remote_dma(o, i, T.sem[far], T.sem.loc, pid, rid, mask)
                    sent += k
            g.wait_ge(T.sem.loc, sent)


def rank_program(g, core, T, topo):
    rank = T.rank_of(core)
    if rank is None:
        return hand_on(g, core, T, topo)
    n = len(T.cores)
    V, S, P, Y = g.vector, g.scalar, g.tensor, g.sync
    Q = {"v": V, "s": S, "t": P, "g": g, "y": Y}
    ev, known, cnt, last, readers = [], {q: 0 for q in Q}, {q: [] for q in POOL}, {}, {}

    def need(q, e):
        if not known[q] >> e & 1:
            Q[q].wait_ge(T.sem[ev[e][0]], ev[e][1])
            known[q] |= ev[e][2]

    def event(sem, val, kn, q):
        ev.append((sem, val, kn | 1 << len(ev), q))
        return len(ev) - 1

    def deps(q, rd, wr):
        d = [last[k] for k in rd + wr if k in last]
        for k in wr:
            d += readers.get(k, [])
        for k in rd:
            if k[:2] == "ps":
                d += [e for e in readers.get(k, []) if ev[e][3] != q]
        for e in sorted(set(d), reverse=True):
            if not (q == "t" and ev[e][3] == "t"):
                need(q, e)

    def mark(e, rd, wr):
        for k in rd:
            readers.setdefault(k, []).append(e)
        for k in wr:
            last[k] = e
            readers[k] = []

    def op(q, fn, rd, wr):
        rd, wr = rd.split(), wr.split()
        deps(q, rd, wr)
        i, k = len(cnt[q]), POOL[q]
        if i >= k:
            need(q, cnt[q][i - k])
        fn().then_inc(T.sem[q + str(i % k)], 1)
        e = event(q + str(i % k), i // k + 1, known[q], q)
        cnt[q].append(e)
        mark(e, rd, wr)

    tot = {}

    def dma(q, out, in_, sem, rd, wr, how=None):
        rd, wr = rd.split(), wr.split()
        deps(q, rd, wr)
        Q[q].dma_start(out, in_, **({"accum_op": how} if how else {})).then_inc(T.sem[sem], 16)
        tot[sem] = tot.get(sem, 0) + 16
        mark(event(sem, tot[sem], known[q], "d"), [], wr)

    def arrives(key, sem, val):
        last[key] = event(sem, val, 0, "r")

    def ts(o, i, s1, s2, o0, o1, rd, wr):
        if s2 is None:
            op("v", lambda: V.tensor_scalar(o, i, s1, None, o0), rd, wr)
        else:
            op("v", lambda: V.tensor_scalar(o, i, s1, s2, o0, o1), rd, wr)

    def tt(o, a, b, f, rd, wr):
        op("v", lambda: V.tensor_tensor(o, a, b, f), rd, wr)

    def cp(o, i, rd, wr):
        op("v", lambda: V.tensor_copy(o, i), rd, wr)

    def ms(o, c, wr):
        op("v", lambda: V.memset(o, c), "", wr)

    def scan(o, a, b, o0, o1, rd, wr):
        op("v", lambda: V.tensor_tensor_scan(o, a, b, 0.0, o0, o1), rd, wr)

    def act(o, i, rd, wr, f=F.Copy, **kw):
        op("s", lambda: S.activation(o, i, f, **kw), rd, wr)

    def aff(o, i, scale, bias, rd, wr):
        act(o, i, rd, wr, f=F.Identity, scale=scale, bias=bias)

    def fill(o, w, c, wr):
        act(o, T.ones[:, 0:w], "ones", wr, scale=c / 32.0)

    def iota(o, pat, base, wr):
        op("g", lambda: g.iota(o, pat, base, 0, allow_small_or_imprecise_dtypes=True), "", wr)

    def sel(o, i, pat, cmp, other, base, rd, wr, cm=0):
        op("g", lambda: g.affine_select(o, i, pat, cmp, other, base, cm), rd, wr)

    def quant(q, s, i, rd, wr):
        op("v", lambda: V.quantize_mx(q, s, i), rd, wr)

    def mm(bank, w, l, ls, r, rs, rd, start=True, stop=True):
        op("t", lambda: P.matmul_mx(T.ps[:, 512 * bank:512 * bank + w], l, ls, r, rs, start, stop), rd, "ps%d" % bank)

    def scaled(q, o, i, rd, wr):
        if q == "s":
            act(o, i, rd, wr, scale=0.03125)
        else:
            ts(o, i, 0.03125, None, A.mult, None, rd, wr)

    def of(f, *a):
        return lambda: f(*a)

    def run(fs):
        for f in fs:
            f()

    def L(a, w):
        return T.lu[:, a:a + w]

    def ps(b, a, w):
        return T.ps[:, 512 * b + a:512 * b + a + w]

    def E(b):
        return T.eq[:, 128 * b:128 * b + 128], T.es[:, 128 * b:128 * b + 128]

    way = {}
    for side in (1, -1):
        d = T.cores[(rank + side) % n]
        direct = topo.may_write(core, d)
        way[side] = (direct, [d, d] if direct else relays_of(core, d, T, topo))
    sent = [0]

    def send_x(t):
        s = str(t)
        deps("g", ["xq" + s, "xr" + s], [])
        for k, src, rel in ((1, "xs", "rs"), (0, "xq", "rq")):
            tr = []
            for side in (1, -1):
                direct, to = way[side]
                es = topo.engines(core, to[k])
                rid, pid = topo.addr(to[k], core)
                far = landing(T, side, s)
                i, o = T[src + s][:], (far[k] if direct else T[rel + s])[:]
                if k == 0:
                    i, o = i.bitcast(dt.uint8), o.bitcast(dt.uint8)
                tr.append(RemoteDMATransfer(dst_ids=[DstId(rid=rid, pnc=pid)], dma_engine_mask=bits(es[:8] if direct else es[-8:]),
                                            remote_sem=T.sem[far[2] if direct else rel + s], src=i, dst=o))
            g.remote_dma_fused(tr, local_sem=T.sem.loc)
            sent[0] += 16

    def send(side, src, key, far, sem, rel):
        direct, to = way[side]
        rid, pid = topo.addr(to[1], core)
        deps("g", key.split(), [])
        g.remote_dma(far, src, T.sem[sem if direct else rel], T.sem.loc, pid, rid, topo.mask(core, to[1]))
        sent[0] += len(topo.engines(core, to[1]))

    def brought(side):
        c = T.cores[(rank + side) % n]
        return len(topo.engines(c if topo.may_write(c, core) else relays_of(c, core, T, topo)[1], core))

    for t in range(R):
        s = str(t)
        arrives("nq" + s, "an" + s, 16)
        arrives("pq" + s, "ap" + s, 16)
        arrives("bn" + s, "ab" + s, brought(-marks_side(t)))
        arrives("on" + s, "ao" + s, brought(-marks_side(t)))
        arrives("hn" + s, "ah" + s, brought(marks_side(t)))

    dma("y", T.xt[:], T.x[:], "lx", "", "xt")
    dma("s", T.ut[:], T.u[:], "lu", "", "ut")
    dma("y", T.wq[:].bitcast(dt.uint8), T.wc[:], "lw", "xt", "")
    dma("y", T.wsc[:], T.ws[:], "lw", "", "wq")
    dma("y", T.vt[:], T.v[:], "lv", "", "vt")

    li, rw, tmp, tmi, pc, pi, one = T.li, T.rw, T.tmp, T.tmi, T.pc, T.pi, T.one
    c16, n23, m32, bu, r82, rx = rw[:, 0:16], rw[:, 16:48], rw[:, 48:80], rw[:, 80:96], rw[:, 96:112], rw[:, 112:128]
    eight = rw[:, 100:104]
    op("g", lambda: g.iota(pi[:, 0:1], [[0, 1]], 0, 1), "", "p")
    iota(li[:, UP:UP + 8], [[16, 8]], 0, "lup")
    iota(T.j16[:], [[0, 16], [1, 16]], 0, "j16")
    iota(c16, [[1, 16]], 0, "c16")
    op("g", lambda: g.iota(tmi[:, 48:56], [[1, 8]], 0, 0), "", "mi1")
    iota(r82, [[8, 4], [0, 4]], 0, "r82")
    iota(n23, [[0, 8], [-2, 4]], 8, "n23")
    iota(rx, [[64, 4], [2, 4]], 0, "rx")
    iota(bu, [[8, 8], [0, 2]], 0, "bu")
    iota(T.px[:], [[1, 256]], 0, "px")
    iota(m32, [[32, 8], [0, 4]], -1, "m32")
    sh = {"q": (0, 15), "e": (0, 16), "h": (3, 1), "q7": (0, 7), "q3": (0, 3), "q2": (2, 3), "q1": (1, 7), "o": (0, 1), "b1": (1, 1), "b2": (2, 1)}
    col = {}

    def cl(k):
        return col.setdefault(k, pc[:, len(col):len(col) + 1])

    def arg(x):
        return cl(x) if x in col else x

    def lin(q, k, a, s1, s2, o0=A.mult, o1=A.add):
        rd = "pq pc %s %s %s" % (a, s1, s2)
        if q == "s":
            aff(cl(k), cl(a), arg(s1), arg(s2), rd, k)
        else:
            ts(cl(k), cl(a), arg(s1), arg(s2), o0, o1, rd, k)

    def flat(a, b, step, row, s1, s2, wr, q="s"):
        rd = "one r82 c16 n23 xl pq pc %s %s" % (s1, s2)
        if q == "s":
            aff(li[:, a:b:step], row, arg(s1), arg(s2), rd, wr)
        else:
            ts(li[:, a:b:step], row, arg(s1), arg(s2), A.mult, A.add, rd, wr)

    def digits(a, b, wr):
        for i, k in list(enumerate(sh))[a:b]:
            ts(pi[:, i + 1:i + 2], pi[:, 0:1], sh[k][0], sh[k][1], A.logical_shift_right, A.bitwise_and, "p", "pi" + k)
            cl(k)
        cp(pc[:, a:b], pi[:, a + 1:b + 1], " ".join("pi" + k for k in list(sh)[a:b]), wr)

    ms(T.ones[:], 32.0, "ones")
    fill(T.rm[:], 256, 1.0, "rm")
    fill(one[:], 256, 1.0, "one")
    fill(T.rm[:, 0:256:16], 16, 0.0, "rm")
    digits(0, 2, "pq")
    cp(L(UP, 8), li[:, UP:UP + 8], "lup", "lu0")
    digits(2, 10, "pc")
    ts(T.eye[:], T.j16[:], cl("q"), None, A.is_equal, None, "j16 pq", "eye")
    ms(li[:, SEL:SEL + 4], 0.0, "ls")
    lin("v", "u", "q2", 1.0, 1.0, A.is_equal, A.mult)
    lin("v", "q=3", "q", 3.0, 1.0, A.is_equal, A.mult)
    lin("v", "w129", "q2", 0.0, 129.0, A.is_equal, A.mult)
    lin("v", "vd", "q2", "q1", "o", A.subtract, A.mult)
    fill(T.sw[:], 512, 0.0, "sw")
    for k, a, b, c in (("8q7", "q7", 8.0, 0.0), ("4h+32", "h", 4.0, 32.0), ("4q7+8", "q7", 4.0, 8.0), ("256+q7", "q7", 1.0, 256.0),
                       ("1-o", "o", -1.0, 1.0), ("2q7+112", "q7", 2.0, 112.0), ("87-q7", "q7", -1.0, 87.0), ("1-o/2", "o", -0.5, 1.0),
                       ("q+112", "q", 1.0, 112.0), ("128(1-o)", "o", -128.0, 128.0),
                       ("1+o/2", "o", 0.5, 1.0), ("16q+15", "q", 16.0, 15.0), ("16q7+b2", "q7", 16.0, "b2"), ("8q+112", "q", 8.0, 112.0),
                       ("1-2b2", "b2", -2.0, 1.0), ("q+4", "q", 1.0, 4.0), ("ha", "h", 2.0, "u"), ("24q3", "q=3", 24.0, 0.0),
                       ("hb", "16q7+b2", "h", "w129"), ("tu", "q+4", "u", "24q3"), ("hu", "8q+112", "u", "hb"), ("tb0", "q7", "h", "tu")):
        lin("s", k, a, b, c)
    XLo, XU = li[:, XL:XL + 16], tmp[:, 0:16]
    ts(li[:, SEL + 2:SEL + 3], cl("q"), 32.0, cl("e"), A.mult, A.add, "pq ls", "ls2")
    ts(T.ne[:], T.j16[:], cl("q"), None, A.not_equal, None, "j16 pq", "ne")
    ts(li[:, SEL:SEL + 1], li[:, SEL + 2:SEL + 3], 1.0, None, A.add, None, "ls2", "ls0")
    ts(XLo, c16, 2.0, cl("h"), A.mult, A.add, "c16 pc", "xl")
    ts(XU, c16, 4.0, cl("q2"), A.mult, A.add, "c16 pc", "xu")
    cp(T.lu[:, SEL:AT], li[:, SEL:AT], "ls0 ls2", "lu1")
    quant(T.uq[:], T.us[:], T.ut[:], "ut", "uq")
    lin("v", "e-32", "e", 1.0, -32.0)
    cp(T.ub[:].bitcast(dt.uint32), T.uq[:].bitcast(dt.uint32).indirect(L(UP, 8)), "uq lu0", "ub")
    cp(T.ubs[:], T.us[:].indirect(L(UP, 8)), "uq lu0", "ubs")
    ts(tmi[:, 0:16], XU, cl("q3"), 1.0, A.add, A.add, "xu pc", "y2")
    ts(tmi[:, 16:48], n23, cl("q7"), cl("h"), A.add, A.subtract, "n23 pc", "dx")
    quant(T.xq0[:], T.xs0[:], T.xt[:], "xt", "xq0")
    flat(AT, AT + 8, 1, one[:, 0:8], "q7", 8.0, "lat", "v")
    ts(li[:, YL:YL + 16], r82, cl("q7"), None, A.add, None, "r82 pc", "lyl")
    flat(AT + 2, AT + 6, 1, one[:, 0:4], "q7", 0.0, "lat", "v")
    ts(li[:, TX:TX + 16], rx, cl("h"), cl("8q7"), A.add, A.add, "rx pc 8q7", "ltx")
    lin("v", "vb", "vd", 1.0, "q1")

    late = []

    def lt(f, *a):
        late.append(of(f, *a))

    y2, dx, x4, bv, gz = tmi[:, 0:16], tmi[:, 16:48], tmp[:, 16:48], tmp[:, 48:80], tmp[:, 80:112]
    mi, m0, m1, m2 = tmi[:, 48:64], tmi[:, 64:80], tmi[:, 80:96], tmi[:, 96:112]
    k0, k1, kx, sp, nk, w1 = [tmp[:, 128 + 16 * i:144 + 16 * i] for i in range(6)]
    aff(x4, n23, -4.0, cl("4h+32"), "n23 4h+32", "x4")
    lt(ts, tmi[:, 56:64], tmp[:, 16:24], 0.25, None, A.mult, None, "x4", "mi2")
    lt(ts, y2, y2, 7, None, A.bitwise_and, None, "y2", "y2")
    lt(ts, m0, mi, 1, None, A.bitwise_and, None, "mi1 mi2", "m0")
    lt(ts, m1, mi, 1, 1, A.logical_shift_right, A.bitwise_and, "mi1 mi2", "m1")
    lt(ts, m2, mi, 2, 1, A.logical_shift_right, A.bitwise_and, "mi1 mi2", "m2")
    lt(ts, tmp[:, 128:136], tmi[:, 64:72], cl("b2"), None, A.not_equal, None, "m0 pc", "k0a")
    lt(ts, tmp[:, 136:144], tmi[:, 72:80], cl("b1"), None, A.not_equal, None, "m0 pc", "k0b")
    lt(ts, tmp[:, 144:152], tmi[:, 80:88], cl("h"), None, A.not_equal, None, "m1 pc", "k1a")
    lt(ts, tmp[:, 152:160], tmi[:, 88:96], cl("b2"), None, A.not_equal, None, "m1 pc", "k1b")
    lt(ts, sp, m1, 4.0, -2.0, A.mult, A.add, "m1", "sp")
    lt(ts, w1, m2, 8.0, -4.0, A.mult, A.add, "m2", "w1")
    lt(tt, kx, k0, k1, A.max, "k0a k0b k1a k1b", "kx")
    lt(tt, sp, sp, k0, A.mult, "k0a k0b", "sp")
    lt(aff, nk, kx, -1.0, 1.0, "kx", "nk")
    lt(tt, w1, w1, kx, A.mult, "kx", "w1")
    lt(tt, sp, sp, mi, A.subtract, "mi1 mi2", "sp")
    lt(ts, dx, dx, 7, None, A.bitwise_and, None, "dx", "dx")
    lt(tt, sp, sp, w1, A.add, "w1", "sp")
    lt(aff, tmp[:, 128:136], tmp[:, 176:184], 16.0, cl("q+112"), "sp q+112", "k0a")
    lt(aff, tmp[:, 156:160], tmp[:, 188:192], -8.0, cl("87-q7"), "sp 87-q7", "k1b")
    lt(aff, tmp[:, 136:140], tmp[:, 184:188], 16.0, cl("2q7+112"), "sp 2q7+112", "k0b")
    lt(aff, tmp[:, 140:144], tmp[:, 188:192], 16.0, cl("2q7+113"), "sp 2q7+113 k0b", "k0c")
    lt(aff, tmp[:, 208:216], tmp[:, 192:200], cl("128(1-o)"), 0.0, "nk 128(1-o)", "w1")
    lt(aff, tmp[:, 216:220], tmp[:, 200:204], 128.0, 0.0, "nk sp", "w2")
    lt(tt, tmp[:, 112:128], y2, bu, A.add, "y2 bu", "yz")
    lt(tt, x4, x4, dx, A.add, "dx", "x4")
    lt(ts, bv, dx, -1.0, cl("4q7+8"), A.mult, A.add, "dx 4q7+8", "bv")
    lt(ts, gz, dx, 4.0, None, A.is_gt, None, "dx", "gz")
    lt(tt, li[:, LO:LO + 16], XU, tmp[:, 112:128], A.min, "xu yz", "llo")
    lt(tt, bv, bv, x4, A.subtract, "x4", "bv")
    lt(tt, li[:, HI:HI + 16], XU, tmp[:, 112:128], A.max, "xu yz", "lhi")
    lt(tt, bv, bv, gz, A.mult, "gz", "bv")
    lt(tt, x4, x4, m32, A.add, "m32", "x4")
    lt(ts, gz, dx, 0.0, cl("256+q7"), A.is_equal, A.mult, "dx 256+q7", "gz")
    lt(tt, x4, x4, bv, A.add, "bv", "x4")
    lt(tt, tmp[:, 128:136], tmp[:, 128:136], tmp[:, 192:200], A.subtract, "nk", "k0a")
    lt(tt, tmp[:, 156:160], tmp[:, 156:160], tmp[:, 172:176], A.mult, "kx", "k1b")
    lt(tt, li[:, TI:TI + 32], x4, gz, A.max, "x4 gz", "lti")
    lt(tt, li[:, PV:PV + 12], tmp[:, 128:140], tmp[:, 208:220], A.max, "k0a k0b w1 w2", "lpv")
    lt(tt, li[:, PU:PU + 4], tmp[:, 156:160], tmp[:, 140:144], A.add, "k0c k1b", "lpu")
    lt(cp, T.lu[:, AT:VA], li[:, AT:VA], "lat xl lyl llo lhi lti ltx lpv lpu", "lu")
    slots = [of(lin, "s", "2q7+113", "q7", 2.0, 113.0), of(lin, "s", "hb0", "q=3", -1.0, "hu"), of(lin, "s", "td", "u", 4.0, "q=3"), of(lin, "s", "32u", "u", 32.0, "hb0"),
             of(flat, VA, VA + 4, 1, eight, "o", "q1", "lva1"), of(flat, VA + 4, VA + 8, 1, eight, "1-o", "q1", "lva2"),
             of(lin, "s", "hb1", "1-2b2", "h", "32u"),
             of(flat, VA + 8, VA + 16, 2, one[:, 0:4], "vb", 0.0, "lv0"), of(flat, VA + 9, VA + 16, 2, eight, "1-o/2", "vb", "lv1"),
             of(flat, VA + 16, VA + 24, 2, eight, "o", "vb", "lv2"), of(flat, VA + 17, VA + 24, 2, eight, "1+o/2", "vb", "lv3"),
             of(flat, CU, CU + 8, 1, one[:, 0:8], "16q+15", 0.0, "lcu"), of(flat, Q7, Q7 + 8, 1, one[:, 0:8], "q7", 0.0, "lq7"),
             of(flat, UE, UE + 8, 1, li[:, XL:XL + 8], 16.0, 31.0, "lue"),
             of(flat, TB, TB + 8, 1, one[:, 0:8], "tb0", 0.0, "ltb0"), of(flat, TB + 8, TB + 16, 1, one[:, 0:8], "tb0", "td", "ltb1"),
             of(flat, HB, HB + 8, 1, rw[:, 0:8], "ha", "hb0", "lhb0"), of(flat, HB + 8, HB + 16, 1, rw[:, 0:8], "ha", "hb1", "lhb1"),
             of(cp, T.lu[:, VA:NL], li[:, VA:NL], "lva1 lva2 lv0 lv1 lv2 lv3 lcu lc8 lq7 lue lhb0 lhb1 ltb0 ltb1", "lu2")]

    def tables():
        sel(T.fe[:], T.ones[:], [[-1, 528]], A.is_equal, 0.0, 3, "ones", "fe", cm=4)
        for a in (0, 256):
            sel(T.di[:, a:a + 256], one[:], [[0, 4], [-1, 8], [1, 8]], A.not_equal, -1.0, 0, "one", "di")
        sel(T.sg[:], one[:, 0:64], [[0, 8], [1, 8]], A.is_equal, -1.0, -7, "one", "sg")

    def small():
        for o, st, w, c, k in ((T.va[:, 0:128], 0, 128, 0, "vaL"), (T.va[:, 128:144], 0, 16, 1, "vac"), (T.v0[:, 128:144], 0, 16, 1, "v0c"),
                               (li[:, C8:C8 + 8], 1, 8, 0, "lc8"), (T.bb[:, 256:272], 1, 16, 0, "bcN"), (T.di[:, 0:512:8], 0, 64, 0, "di"),
                               (T.sc[:, 15:16], 0, 1, 0, "sc0"), (T.zz[:, 16:144], 0, 128, 0, "zL zL0"), (T.zz[:, 144:160], 0, 16, 5, "zc"),
                               (T.zz[:, 145:146], 0, 1, 1, "zc"), (T.dl[:, 64:145:80], 0, 2, -2, "dlc"), (T.vb[:, 0:128], 0, 128, 0, "vbL"), (T.vb[:, 128:144], 0, 16, 1, "vbc"),
                               (T.bb[:, 800:816], 1, 16, 8, "bcF")):
            iota(o, [[st, w]], c, k)
        for a in (0, 256):
            sel(T.r8[:, a:a + 256], one[:], [[0, 32], [1, 8]], A.not_equal, 0.0, 0, "one", "r8")
        for a in (0, 256):
            sel(T.df[:, a:a + 256], one[:], [[0, 2], [2, 8], [-1, 16]], A.is_ge, -1.0, 0, "one", "df")
        for o, st, w, c, k in ((T.df[:, 0:512:16], 0, 32, 0, "df"), (T.dl[:, 288:289], 0, 1, -2, "dlcF"), (T.val[:, 384:400], 0, 16, 0, "valc"),
                               (T.va[:, 144:208], 0, 64, 0, "vaU"), (T.vb[:, 144:208], 0, 64, 0, "vbU"), (T.zz[:, 160:224], 0, 64, 0, "zU")):
            iota(o, [[st, w]], c, k)
        for o, st, w, c, k in ((T.bb[:, 528:544], 1, 16, 0, "bcU"), (T.dts[:], 0, 32, 0, "dts"), (T.sml[:], 0, 48, -1, "sml"),
                               (T.cum[:, 0:16], 0, 16, -1, "cum0"), (T.na[:, 131:384:4], 0, 64, 1, "nac"),
                               (T.c12[:], 0, 256, 0, "c12"), (T.c12[:, 0:256:16], 0, 16, -12, "c12")):
            iota(o, [[st, w]], c, k)

    for t in range(R):
        s = str(t)
        xq, xs = T["xq" + s], T["xs" + s]
        sm, oo, hl, bn, on, hn = [T[k + s] for k in ("sm", "oo", "hl", "bn", "on", "hn")]
        side = marks_side(t)
        XK = " xq%s xr%s" % (s, s)
        mm(0, 256, T.ub[:], T.ubs[:], xq[:], xs[:], "ub ubs" + XK)
        mm(1, 256, T.ub[:], T.ubs[:], xq[:], xs[:], "ub ubs" + XK)
        mm(2, 256, T.uq[:], T.us[:], xq[:], xs[:], "uq" + XK)
        send_x(t)
        if t == 0:
            tables()
        else:
            ms(T.va[:, 0:128], 0.0, "vaL"), ms(T.va[:, 144:208], 0.0, "vaU")
            quant(T.vq[:], T.vs[:], T.vt[:], "vt", "vq")
        act(T.t2[:], ps(1, 0, 256), "ps1", "t2", f=F.Abs, scale=1.25 * 2.0 ** -24, bias=2.0 ** -120)
        tt(T.t1[:], ps(0, 0, 256), T.eye[:], A.mult, "ps0 eye", "t1")
        act(T.row[:, 0:256], ps(1, 0, 256), "ps1", "row")
        scan(T.scn[:, ::-1], T.rm[:], T.t1[:, ::-1], A.mult, A.add, "rm t1", "scn")
        tt(T.row[:, 256:512], ps(0, 0, 256), T.t2[:], A.add, "ps0 t2", "up")
        act(T.pm[:], ps(2, 0, 256), "ps2", "pm")
        dma("y", T.px[1:128:16, :], T.pm[1:128:16, :], "lp", "pm", "px")
        ri, e32, acc = T.ri, T.e32, T.acc

        def ahead(c):
            o, w, sc = T.m[:, 256 * c:256 * c + 256], T.row[:, 16 * c:16 * c + 256], T.scn[:, 16 * c:16 * c + 1]
            if WHO[c] == "s":
                act(o, w, "row up scn", "m%d" % c, f=F.Sign, scale=-1.0, bias=sc)
            else:
                ts(o, w, sc, 32.0, A.is_gt, A.mult, "row up scn", "m%d" % c)

        def count(c):
            w = T.m[:, 256 * c:256 * c + 256]
            if WHO[c] == "v":
                scan(T.mo[:, 128 * (c - NS):128 * (c - NS) + 128], T.m[:, 256 * c:256 * c + 128], T.m[:, 256 * c + 128:256 * c + 256],
                     A.add, A.add, "m%d" % c, "mo%d" % c)
            else:
                act(w, w, "", "m%d ar%d" % (c, c), f=F.Relu, scale=-32.0 if WHO[c] == "s" else 1.0, accum_out=acc[:, c:c + 1])

        alone, both = [c for c in range(NS) if WHO[c] == "s"], [c for c in range(NS) if WHO[c] == "b"]
        tt(T.ec[:], ps(0, 0, 256), T.scn[:], A.is_equal, "ps0 scn", "ec")
        for c in both:
            ahead(c)
        for i, c in enumerate(alone):
            ahead(c)
            if i:
                count(alone[i - 1])
            if i == len(alone) - 1:
                for b in both:
                    count(b)
        count(alone[-1])
        equal = [of(scan, T.es2[:, ::-1], T.ne[:, ::-1], T.ec[:, ::-1], A.mult, A.add, "ne ec", "es2"),
                 of(ts, e32[:, 0:16], T.es2[:, 0:256:16], 32.0, cl("e-32"), A.mult, A.add, "es2 e-32", "e32")]
        for c in range(NS, 17):
            if c < 16:
                ahead(c)
            if c > NS:
                count(c - 1)
            run(equal[c - NS:c - NS + 1])
        tt(ri[:, 0:NS], acc[:, 0:NS], e32[:, 0:NS], A.add, "e32 " + " ".join("ar%d" % c for c in range(NS)), "xb")
        tt(ri[:, NS:16], T.mo[:, 127:128 * (16 - NS):128], e32[:, NS:16], A.add, "e32 " + " ".join("mo%d" % c for c in range(NS, 16)), "xa")
        ts(ri[:, 16:32], ri[:, 0:16], 9, None, A.logical_shift_right, None, "xa xb", "hi")
        ts(ri[:, 32:48], ri[:, 0:16], 496, None, A.bitwise_and, None, "xa xb", "lo")
        ts(ri[:, 64:80], ri[:, 0:16], 480, None, A.bitwise_and, None, "xa xb", "r16")
        tt(ri[:, 48:64], ri[:, 32:48], ri[:, 16:32], A.add, "hi lo", "pti")
        ts(ri[:, 80:96], ri[:, 64:80], 0.5, None, A.mult, None, "r16", "r17")
        cp(T.pt[:], ri[:, 48:64], "pti", "pt")
        tt(ri[:, 96:112], ri[:, 80:96], ri[:, 16:32], A.add, "r17 hi", "r18")
        cp(T.sw[:].indirect(T.pt[:]), T.px[:], "px pt", "sw")
        cp(T.pz[:], ri[:, 96:112], "r18", "pz")
        op("v", lambda: V.transpose(T.tr[:], T.sw[:]), "sw", "tr")
        cp(sm[:], T.tr[:].indirect(L(SEL, 1)), "tr lu1", "sm" + s)
        send(side, sm[:], "sm" + s, bn[:], "ab" + s, "rb" + s)
        cp(oo[:], T.tr[:].indirect(L(SEL + 2, 1)), "tr lu1", "oo" + s)
        send(side, oo[:], "oo" + s, on[:], "ao" + s, "ro" + s)
        (so, sk), (to, tk) = ((oo, "oo" + s), (on, "on" + s))[::-side]
        dts, val, da, dz = T.dts, T.val, T.da, T.dz
        of_so = [of(act, val[:, 0:128], so[:].indirect(L(VA, 8)), "lu2 " + sk, "val1"),
                 of(act, val[:, 128:384], so[:].indirect(L(VA + 8, 16)), "lu2 " + sk, "val2"),
                 of(aff, da[:], val[:, 1:385], -1.0, 0.0, "val1 val2 valc", "da"),
                 of(iota, da[:, 15:128:16], [[0, 8]], 0, "da"), of(iota, da[:, 159:384:32], [[0, 8]], 0, "da"),
                 of(dma, "g", da[:], val[:, 0:384], "ld", "val1 val2", "da", A.add)]
        of_to = [of(tt, dts[:, 0:15], to[:, 0:15], to[:, 1:16], A.subtract, tk, "dts"),
                 of(tt, dts[:, 16:23], to[:, 8:15], to[:, 9:16], A.subtract, tk, "dt1"),
                 of(ts, dts[:, 24:26], to[:, 8:16:4], -1.0, None, A.mult, None, tk, "dt2"),
                 of(cp, dts[:, 7:24:16], to[:, 7:16:8], "dts " + tk, "dt3"),
                 of(ts, dts[:, 11:16:4], to[:, 11:16:4], to[:, 0:1], None, A.subtract, None, "dts " + tk, "dt4"),
                 of(act, dz[:, 0:256], dts[:].indirect(L(TB, 16)), "lu2 dts dt1 dt2 dt3 dt4", "dz dz2"),
                 of(act, dz[:, 256:384], dts[:, 16:32].indirect(L(Q7, 8)), "lu2 dts dt1 dt2 dt3 dt4", "dz3")]

        def out_of(q, sc, key, bank, dst, qs):
            fs = [lambda: [mm(bank + b, 256, *E(b), q[:], sc[:], "eq%d %s" % (b, key)) for b in range(4)]]
            return fs + [of(scaled, qs[b], dst(b)[0], ps(bank + b, 0, 256), "ps%d" % (bank + b), dst(b)[1]) for b in range(4)]

        def from_next(qs):
            return out_of(T["nq" + s], T["ns" + s], "nq" + s, 4, lambda b: (T.dn[:, 256 * b:256 * b + 256], "dn%d" % b), qs)

        def from_prev(qs):
            return out_of(T["pq" + s], T["pr" + s], "pq" + s, 0, lambda b: (T.gt[:, b:1024:4], "gt%d" % b), qs) + \
                [of(quant, T.gq[:], T.gs[:], T.gt[:], "gt0 gt1 gt2 gt3", "gq")]

        def once_more(qs):
            return out_of(T.gq, T.gs, "gq", 0, lambda b: (T.dp[:, 256 * b:256 * b + 256], "dp%d" % b), qs)

        whom = {-1: (L(AT + 4, 4), L(AT, 8)), 1: (L(XL, 4), L(XL, 8))}
        mine = [of(act, T.at[:, 0:64], sm[:].indirect(whom[side][0]), "lu sm" + s, "atN"),
                of(act, T.at[:, 64:192], sm[:].indirect(whom[side][1]), "lu sm" + s, "atF")]
        after = []
        if t == 0:
            small()
            run([of(quant, *E(b), T.fe[:, 3 - b:515 - b], "fe", "eq%d" % b) for b in range(4)])
            soon, again = (from_prev("ssss"), once_more("ssvv")) if way[-1][0] else ([], [])
            run(slots[:-1] + soon[:5] + late[:26] + soon[5:] + again[:3] + late[26:] + slots[-1:])
            run(mine)
            act(T.v0[:, 0:128], T.va[:, 0:144].indirect(L(PV, 8)), "vaL vac lu", "v0L")
            run(again[3:])
            aff(T.r0[:], T.v0[:].indirect(L(PN, 4)), -8.0, 9.0, "lu v0L v0c", "r0")
            during = from_next("ssss")
            if not soon:
                after = from_prev("svsv") + once_more("svsv")
        else:
            a, b = from_prev("ssss"), from_next("ssss")
            if way[-side][0]:
                run(a[:5] + mine + a[5:] + once_more("svsv"))
                during = b
            else:
                run(a[:5] + b[:3] + mine + a[5:])
                during = b[3:] + once_more("ssss")

        gg, gh, bb, bt, sc, kn, dl, db, yy, zz = T.gg, T.gh, T.bb, T.bt, T.sc, T.kn, T.dl, T.db, T.yy, T.zz
        SETS = {"N": 0, "U": 1, "F": 2}
        CELL = {"N": 0, "F": 64, "U": 128}
        SUMS = {"N": 16, "F": 528, "U": 1552, "X": 2064}

        def dist(k):
            a, b = (0, 64) if k == "N" else (64, 192)
            tt(T.dd[:, a:b], bn[:].indirect(whom[-side][k != "N"]), T.at[:, a:b], A.subtract, "lu at%s bn%s" % (k, s), "dd" + k)

        def high(k):
            i, a = SETS[k], CELL[k]
            act(gh[:, 256 * i:256 * i + 256], T.dd[:, a:a + 64].indirect(L(HI, 16)), "lu dd" + "NF"[k != "N"], "gh" + k, f=F.Abs)

        def beat(k):
            i, a = SETS[k], CELL[k]
            tt(bb[:, 272 * i:272 * i + 256], gg[:, a:a + 64].indirect(L(LO, 16)), gh[:, 256 * i:256 * i + 256], A.is_le,
               "lu gh%s gg%s" % (k, "NF"[k != "N"]), "b" + k)

        def turn(k, h, q="s"):
            i = SETS[k]
            o = bt[:, 1025 + 512 * h:1536 + 512 * h:2] if k == "F" else bt[:, 512 * i + 256 * h:512 * i + 256 * h + 256]
            scaled(q, o, bb[:, 272 * i:272 * i + 272].indirect(L(TI + 16 * h, 16)), "lu bc%s b%s" % (k, k), "t%s%d" % (k, h))

        def wins(k, h=0):
            a, b = SUMS[k] + 512 * h, 512 * SETS[k] + 512 * h
            if k == "F":
                scan(sc[:, a:a + 512], T.df[:], bt[:, b:b + 512], A.mult, A.add, "df tF%d tX%d" % (h, h), "wF%d" % h)
            else:
                scan(sc[:, a:a + 512], T.di[:], bt[:, b:b + 512], A.mult, A.add, "di t%s0 t%s1" % (k, k), "w" + k)

        def step(k):
            a, b = 80 * SETS[k], SUMS[k]
            tt(dl[:, a:a + 64], sc[:, b - 1:b + 504:8], sc[:, b + 7:b + 512:8], A.subtract, "sc0 wF1 w" + k, "dl" + k)

        def anew(k):
            a = 80 * SETS[k]
            ms(dl[:, a:a + 128:16] if k == "F" else dl[:, a:a + 64:8], -2.0, "dl" + k)

        def back(k):
            i, w = SETS[k], 128 if k == "F" else 64
            o, d = db[:, 64 * i:64 * i + w], dl[:, 80 * i + 1:80 * i + w + 1]
            if k == "N":
                tt(o, d, T.sg[:], A.mult, "dlc sg dlN", "dbN")
            else:
                aff(o, d, -1.0, 0.0, "dlc dlcF dlF2 dl" + k, "db" + k)

        def ends(k):
            if k == "F":
                ms(db[:, 143:256:16], -2.0, "dbF")
            else:
                iota(db[:, 71:128:8], [[0, 8]], -2, "dbU")

        def far_of(h):
            act(gh[:, 768 + 256 * h:1024 + 256 * h], T.dd[:, 64 + 32 * h:96 + 32 * h].indirect(L(YL, 16)), "lu ddF", "ghX%d" % h, f=F.Abs)

        def cross(h):
            tt(bb[:, 816 + 256 * h:1072 + 256 * h], gg[:, 32 * h:32 * h + 32].indirect(L(XL, 16)), gh[:, 768 + 256 * h:1024 + 256 * h],
               A.is_lt if h else A.is_le, "lu ggN ghX%d" % h, "bX%d" % h)

        def rows():
            scan(sc[:, SUMS["X"]:SUMS["X"] + 512], T.r8[:], bb[:, 816:1328], A.mult, A.add, "r8 bX0 bX1", "wX")

        def turn_x(h):
            scaled("s", bt[:, 1024 + 512 * h:1536 + 512 * h:2], bb[:, 816 + 256 * h:1072 + 256 * h].indirect(L(TX, 16)), "lu bX%d" % h, "tX%d" % h)

        near = [of(scaled, "s", kn[:, 64:128], sc[:, SUMS["X"] + 7:SUMS["X"] + 512:8], "wX", "x32"),
                of(tt, kn[:, 0:64], sc[:, 23:528:8], kn[:, 64:128], A.add, "wN x32", "kn")]
        WF = "kn wN wF0 wF1"
        whole = [of(tt, dl[:, 160:288:2], sc[:, 527:1536:16], kn[:, 0:64], A.subtract, WF, "dlF"),
                 of(tt, dl[:, 161:288:2], kn[:, 0:64], sc[:, 543:1552:16], A.subtract, WF, "dlF2"), of(anew, "F")]

        def state(k):
            return (T.v0, "v0") if k == 0 else (T.va, "va") if k % 2 else (T.vb, "vb")

        def forth(k, p):
            src, sn = state(k)
            if p == "N":
                scan(yy[:, 0:64], dl[:, 0:64], src[:, 0:128:2], A.add, A.max, "dlN %sL" % sn, "yL")
            elif p == "F":
                scan(yy[:, 0:128], dl[:, 160:288], src[:, 0:128], A.add, A.max, "dlF dlF2 %sL" % sn, "yL")
            else:
                scan(yy[:, 128:192], dl[:, 80:144], src[:, 144:208], A.add, A.max, "dlU %sU" % sn, "yU")

        def backw(p):
            if p == "N":
                scan(zz[:, 142:15:-2], db[:, 63::-1], yy[:, 63::-1], A.add, A.max, "dbN yL", "zL")
            elif p == "F":
                scan(zz[:, 143:15:-1], db[:, 255:127:-1], yy[:, 127::-1], A.add, A.max, "dbF yL", "zL")
            else:
                scan(zz[:, 223:159:-1], db[:, 127:63:-1], yy[:, 191:127:-1], A.add, A.max, "dbU yU", "zU")

        MOVE = {"N": (PN, 4, 0, 128, 2, 144), "F": (PV, 8, 0, 128, 1, 144), "U": (PU, 4, 144, 208, 1, 208)}

        def stood(k, p):
            src, sn = state(k)
            lst, w, a, b, st, win = MOVE[p]
            aff(T.rr[:, a:a + 16 * w], src[:, 0:win].indirect(L(lst, w)), -8.0, 9.0, "lu %sL %sc" % (sn, sn) + (" %sU" % sn) * (p == "U"),
                "rr" + "LU"[p == "U"])

        def move(k, p):
            dst, dn_ = state(k + 1)
            lst, w, a, b, st, win = MOVE[p]
            r, rk = (T.r0[:], "r0") if k == 0 else (T.rr[:, a:a + 16 * w], "rr" + "LU"[p == "U"])
            tt(dst[:, a:b:st], zz[:, 16:16 + win].indirect(L(lst, w)), r, A.is_gt, rk + " lu zL zL0 zc" + " zU" * (p == "U"), dn_ + "LU"[p == "U"])

        dist("N"), high("N")
        ts(T.dd[:, 192:256], T.dd[:, 0:64], -1.0, None, A.mult, None, "ddN", "nd")
        dist("F")
        tt(gg[:, 0:64], T.dd[:, 0:64], T.dd[:, 192:256], A.max, "ddN nd", "ggN")
        far_of(0), beat("N"), turn("N", 0), turn("N", 1, "v")
        act(gg[:, 64:192], T.dd[:, 64:192], "ddF", "ggF", f=F.Abs)
        high("F"), cross(0), wins("N"), far_of(1), step("N"), turn_x(0), beat("F")
        ts(zz[:, 18:144:4], dl[:, 1:64:2], 1.0, None, A.add, None, "dlN", "zL")
        ts(zz[:, 16:144:4], dl[:, 1:64:2], -1.0, 1.0, A.mult, A.add, "dlN", "zL0")
        anew("N")
        FORTH = {2: [of(wins, "F", 0)], 3: near[1:], 4: [of(beat, "U"), of(ends, "F")], 5: of_to[1:2], 6: of_to[4:5],
                 7: [of(anew, "U"), of(back, "U"), of(ends, "U")]}
        BACK = {1: [of(cross, 1)], 4: of_to[0:1], 5: of_to[2:3], 6: of_so[2:] + [of(wins, "U")]}
        MOVED = {0: [of(back, "N"), of_so[0], of(turn, "F", 0)], 1: [rows, of(turn_x, 1)], 2: near[:1] + [of(turn, "F", 1)],
                 3: [of(wins, "F", 1), of(high, "U"), of_so[1]] + whole + [of(back, "F")],
                 4: [of(turn, "U", 0)], 5: [of_to[3], of(turn, "U", 1)], 6: [of(step, "U")], 8: of_to[5:6], 9: of_to[6:7],
                 10: during[:4]}
        during = during[4:]
        for k in range(12):
            p = "N" if k < 4 else "F"
            to_ = "N" if k < 3 else "F"
            if 0 < k < 11:
                stood(k, to_)
            if 7 <= k < 11:
                stood(k, "U")
            if k == 11:
                forth(k, "U")
            if k:
                forth(k, p)
            if 7 < k < 11:
                forth(k, "U")
            if k == 11:
                ts(T.sml[:, 0:8], yy[:, 135:192:8], 0.5, None, A.is_lt, None, "yU sml", "fr")
            run(FORTH.get(k, []))
            if k:
                backw(p)
            if k > 7:
                backw("U")
            run(BACK.get(k, []))
            if k < 11:
                move(k, to_)
            if 7 <= k < 11:
                move(k, "U")
            run(MOVED.get(k, []))
        sml, cum, na, nb, ss = T.sml, T.cum, T.na, T.nb, T.ss
        scan(sml[:, 17:25], sml[:, 0:8], sml[:, 0:8], A.add, A.max, "fr", "cn")

        def held():
            ts(nb[:], zz[:, 16:224].indirect(L(HB, 16)), 1.0, None, A.not_equal, None, "zL zU zc lu2", "nb")

        def left():
            scan(cum[:, 16:272], T.c12[:], nb[:], A.add, A.add, "c12 nb", "cum")

        def seats(out, key, first):
            if first:
                held()
            ts(na[:, 0:128], zz[:, 16:144], 1.0, None, A.not_equal, None, "zL", "na1")
            if first:
                left()
            ts(na[:, 129:384:4], zz[:, 160:224], 1.0, None, A.not_equal, None, "zU", "na2")
            tt(na[:, 128:384:2], cum[:].indirect(L(CU, 8)), T.fb[:], A.is_ge, "cum cum0 fb lu2", "na3")
            scan(ss[:, 0:128], na[:, 0:128], da[:, 0:128], A.mult, A.add, "na1 da", "ss1")
            scan(ss[:, 128:384], na[:, 128:384], da[:, 128:384], A.mult, A.add, "na2 na3 nac da", "ss2")
            cp(out[:, 0:8], ss[:, 15:128:16], "ss1", key)
            cp(out[:, 8:16], ss[:, 159:384:32], "ss2", key + "b")

        def free_before():
            act(T.c2[:], sml[:, 16:32].indirect(L(Q7, 8)), "cn lu2", "c2")

        def free_turn():
            tt(sml[:, 32:40], sml[:, 17:25], sml[:, 0:8], A.mult, "cn fr", "fn")
            act(T.fb[:], sml[:, 32:48].indirect(L(C8, 8)), "fn lu2", "fb")

        def suitors(out, key, first):
            if first:
                held(), left()
            tt(T.n2[:], cum[:].indirect(L(UE, 8)), T.c2[:], A.is_le, "cum cum0 c2 lu2", "n2")
            scan(ss[:, 384:512], T.n2[:], dz[:, 256:384], A.mult, A.add, "n2 dz3", "ss3")
            cp(dz[:, 2:256:16], ss[:, 391:512:8], "ss3", "dz2")
            scan(ss[:, 512:768], nb[:], dz[:, 0:256], A.mult, A.add, "nb dz dz2", "ss4")
            cp(out[:], ss[:, 527:768:16], "ss4", key + " " + key + "b")

        (d1, n1), (d2, n2) = ((T.dn, "dn"), (T.dp, "dp"))[::-side]
        own, far = (d1, n1, T.al, "al alb"), (d2, n2, hn, "hn" + s)

        def part(b, how, q, o, key):
            w = how[0][:, 256 * b:256 * b + 256].indirect(how[2][:])
            (act if q == "s" else cp)(o, w, "%s %s%d" % (how[3], how[1], b), key)

        def blk(buf, b):
            return buf[:, 256 * b:256 * b + 256]

        def column(b, q):
            (act if q == "s" else cp)(blk(T.vc, b - 2), blk(T.vg, b).indirect(T.pz[:]), "vg%d pz" % b, "vc%d" % b)

        selfish = t < R - 1 and not way[marks_side(t + 1)][0]
        if selfish:
            free_before(), free_turn(), run(during), suitors(T.al, "al", True)
            part(2, own, "s", blk(T.vg, 2), "vg2"), part(3, own, "s", blk(T.vg, 3), "vg3"), column(3, "s"), part(1, own, "s", blk(T.vg, 1), "vg1")
            seats(hl, "hl" + s, False)
        elif side < 0:
            free_turn(), free_before(), run(during), seats(hl, "hl" + s, True)
        else:
            free_before(), run(during), suitors(hl, "hl" + s, True), free_turn()
        send(-side, hl[:], "hl%s hl%sb" % (s, s), hn[:], "ah" + s, "rb" + s)
        run(after[:1])
        if not selfish:
            (suitors if side < 0 else seats)(T.al, "al", False)
        run(after[1:])
        for h in range(2):
            for b in range(4):
                mm(4 * h + b, 128, *E(b), xq[:, 128 * h:128 * h + 128], xs[:, 128 * h:128 * h + 128], "eq%d" % b + XK, True, False)

        def larger(b):
            tt(blk(T.zp, b), blk(far[0], b).indirect(far[2][:]), blk(T.vg, b), A.max, "%s%d vg%d %s" % (far[1], b, b, far[3]), "zp%d" % b)

        def home(b, h):
            o, w, key = T.zt[:, 512 * h + b:512 * h + 512:4], blk(T.zp, b).indirect(T.pz[:, 8 * h:8 * h + 8]), "zt%d%d" % (b, h)
            if b > 1:
                a = 256 * (b - 2) + 128 * h
                tt(o, w, T.vc[:, a:a + 128], A.max, "pz zp%d vc%d" % (b, b), key)
            else:
                act(o, w, "pz zp%d" % b, key)

        def product(h):
            a = 128 * h
            quant(T.zq[:, a:a + 128], T.zs[:, a:a + 128], T.zt[:, 4 * a:4 * a + 512], " ".join("zt%d%d" % (b, h) for b in range(4)), "zq%d" % h)
            for b in range(4):
                mm(4 * h + b, 128, T.wq[:, 128 * b:128 * b + 128], T.wsc[:, 128 * b:128 * b + 128], T.zq[:, a:a + 128], T.zs[:, a:a + 128],
                   "wq zq%d" % h, False, True)

        if not selfish:
            part(2, own, "v", blk(T.vg, 2), "vg2"), part(3, own, "s", blk(T.vg, 3), "vg3"), part(1, own, "s", blk(T.vg, 1), "vg1")
            column(3, "s")
        part(0, own, "v", blk(T.vg, 0), "vg0"), column(2, "v")
        larger(0), part(2, far, "s", blk(T.zp, 2), "zp2"), larger(1), part(3, far, "s", blk(T.zp, 3), "zp3")
        home(0, 0), home(2, 0), home(1, 0), home(3, 0), home(2, 1), product(0), home(0, 1), home(1, 1), home(3, 1), product(1)
        s2 = str(t + 1)
        for h in range(2):
            a = 128 * h
            for b in range(4):
                scaled("svsv"[b], T.xn[:, 4 * a + b:4 * a + 512:4], ps(4 * h + b, 0, 128), "ps%d" % (4 * h + b), "xn%d%d" % (h, b))
            quant(T["xq" + s2][:, a:a + 128], T["xs" + s2][:, a:a + 128], T.xn[:, 4 * a:4 * a + 512],
                  " ".join("xn%d%d" % (h, b) for b in range(4)), ("xq", "xr")[h] + s2)

    s = str(R)
    xq, xs = T["xq" + s], T["xs" + s]
    w, wk = (T.al, "al alb") if side < 0 else (hn, "hn%d" % (R - 1))
    for h in range(2):
        a, key = 128 * h, ("xq", "xr")[h] + s
        mm(h, 128, T.vq[:], T.vs[:], xq[:, a:a + 128], xs[:, a:a + 128], "vq " + key)
        dma("y", T.oc[:, 4 * a:4 * a + 512], xq[:, a:a + 128].bitcast(dt.uint8), "sty", key, "")
        (cp if h else act)(T.yo[:, a:a + 128], ps(h, 0, 128), "ps%d" % h, "yo%d" % h)
    dma("y", T.y[:], T.yo[:], "sty", "yo0 yo1", "")
    act(T.ab[:], T.px[:].indirect(w[:]), "px " + wk, "ab")
    cp(T.wj[:], T.ab[:].indirect(T.pz[:]), "ab pz", "wj")
    for k in range(4):
        dma("s", T.osc[4 * k:4 * k + 4, :], xs[32 * k:32 * k + 4, :], "sts", "xq%s xr%s" % (s, s), "")
    dma("y", T.ol[:], T.wj[0:128:16, :], "sty", "wj", "")
    for q in POOL:
        for e in cnt[q][-POOL[q]:]:
            need("g", e)
    g.wait_ge(T.sem.loc, sent[0])
    g.wait_ge(T.sem.sty, tot["sty"])
    g.wait_ge(T.sem.sts, tot["sts"])
